import numpy as np, ml_dtypes
CORES = [24,25,26,27,28,29,30,31]
N = 8
import mx_ref
BF = ml_dtypes.bfloat16
def entries(a):
    return np.ascontiguousarray(a.T).reshape(-1)
def table(e):
    return np.ascontiguousarray(np.reshape(e, (-1, 16)).T).astype(np.int32)
def pick(q, e):
    c = np.concatenate([q[0].reshape(128, -1, 4), np.zeros((128, 1, 4), np.uint8)], axis=1); s = np.concatenate([q[1], np.ones((16, 1), np.uint8)], axis=1)
    return (np.ascontiguousarray(c[:, e].reshape(128, -1)), np.ascontiguousarray(s[:, e]))
def join(*qs):
    return (np.concatenate([q[0] for q in qs], axis=1), np.concatenate([q[1] for q in qs], axis=1))
def put(q, e, v):
    c, s = q[0].reshape(128, -1, 4).copy(), q[1].copy(); c[:, e] = v[0].reshape(128, -1, 4); s[:, e] = v[1]
    return (c.reshape(128, -1), s)
def pk(c, s):
    return (np.ascontiguousarray(c), mx_ref.live(s))
def emit(q):
    return q[0], q[1]
def decode(q):
    o = []
    for b in range(4):
        e = np.zeros((128, 128, 4), np.float32); e[np.arange(128), np.arange(128), b] = 1
        o.append(mx_ref.matmul(mx_ref.quantize(e.reshape(128, 512).astype(BF)), q))
    return np.stack(o, axis=2).reshape(128, -1)
def f(rng, *shape):
    return mx_ref.flush((rng.standard_normal(shape, dtype=np.float32) * np.exp2(rng.integers(-2, 3, shape[:-1] + (1,)))).astype(BF))
def wide(rng, *shape, cols=0):
    v = rng.standard_normal(shape, dtype=np.float32) * np.exp2(rng.integers(-12, 13, shape)).astype(np.float32)
    if cols: v *= np.repeat(np.exp2(rng.integers(-cols, cols + 1, shape[:-2] + (1, shape[-1] // 4))) * (rng.random(shape[:-2] + (1, shape[-1] // 4)) > 0.0625), 4, axis=-1).astype(np.float32)
    return mx_ref.flush(v.astype(BF))
P, F, R = 256, 32, 2
def big(v):
    v = np.array(v, np.float32)
    v[np.abs(v) < np.float32(2.0 ** -16)] = 0
    return v.astype(BF)
def share(v):
    return big(np.ascontiguousarray(v.reshape(128, N, 4 * P).transpose(1, 0, 2)))
def links(nb):
    return np.concatenate([entries(nb[r]).reshape(P, 3) for r in range(N)])
def graph(rng, ends=False):
    to, far, n = np.zeros((N * P, 3), int), [], P - (N - 1) * F
    for r in range(N):
        a, i = P * r + rng.permutation(P), 0
        while i < P:
            m = min(2 * int(rng.integers(2, 17)), P - i)
            if P - i - m < 4: m = P - i
            for k in range(2):
                c = np.roll(a[i:i + m], -k)
                to[c[0::2], k], to[c[1::2], k] = c[1::2], c[0::2]
            i += m
        if ends:
            h = rng.permutation(a[a < to[a, 0]])[:n]
            e = np.where(rng.random(n) < 0.5, h, to[h, 0])
        else: e = rng.permutation(a)[:n]
        far.append(rng.permutation(np.setdiff1d(a, e)).reshape(N - 1, F))
        for i in range(0, n, 2):
            if e[i + 1] in to[e[i], :2]:
                for j in range(0, n, 2):
                    if j != i and e[j + 1] not in to[e[i], :2] and e[i + 1] not in to[e[j], :2]:
                        e[i + 1], e[j + 1] = e[j + 1], e[i + 1]
                        break
        to[e[0::2], 2], to[e[1::2], 2] = e[1::2], e[0::2]
    for r in range(N):
        for q in range(r + 1, N):
            u, v = far[r][q - 1], far[q][r]
            to[u, 2], to[v, 2] = v, u
    return to
def inputs(rng, x, to):
    return {"x": x, "nb": np.stack([table(to[P * r:P * r + P].reshape(-1)) for r in range(N)]), "w": f(rng, N, 128, 512)}
def setup_inputs(rng):
    return inputs(rng, big(f(rng, N, 128, 4 * P)), graph(rng))
def setup_inputs_far(rng):
    to, n = graph(rng), np.arange(N * P)
    v = (1 + 0.5 * rng.random((128, N * P, 4))) * rng.choice([-1.0, 1.0], (128, N * P, 4))
    a = n[(to[:, 2] // P != n // P) & (n < to[:, 2])]
    b = to[a, 2]
    v[:, b] = np.abs(v[:, b]) * np.sign(v[:, a]) * np.where(rng.random((128, a.size, 4)) < 0.125, -1.0, 1.0)
    return inputs(rng, share(v), to)
def setup_inputs_none(rng):
    to, n, z = graph(rng, ends=True), np.arange(N * P), int(rng.integers(0, N))
    own = n // P == z
    size = np.where(own & (to[:, 2] // P == z), 0.125, 1.0)
    color = np.full(N * P, -1)
    for a in n[n < to[:, 0]]:
        both = np.array([a, to[a, 0]])
        near = color[to[both, 1:]].reshape(-1).tolist()
        color[both] = next(int(c) for c in rng.permutation(5) if c not in near)
    v = rng.choice([-1.0, 1.0], (128, N * P, 4))
    a = n[(to[:, 2] // P != n // P) & (n < to[:, 2])]
    v[:, to[a, 2]] = v[:, a]
    v[:40] = np.where((np.arange(40) // 8)[:, None, None] == color[None, :, None], 8.0, 0.0)
    v[40:48] = 64.0
    v = np.where(own[None, :, None], (1 + 0.5 * rng.random((128, N * P, 4))) * size[None, :, None], 16.0 * v)
    return inputs(rng, share(v), to)
def setup_inputs_spread(rng):
    return inputs(rng, big(wide(rng, N, 128, 4 * P, cols=6)), graph(rng))
def setup_inputs_ties(rng):
    to = graph(rng)
    t = f(rng, 128, 12).astype(np.float32).reshape(128, 3, 4)
    five = np.concatenate([t, 0 - t[:, :1], np.zeros((128, 1, 4), np.float32)], axis=1)
    e = rng.integers(0, 5, N * P)
    for r in range(N):
        j = P * r + int(rng.integers(0, P))
        e[to[j]] = 0
        e[to[to[j]].reshape(-1)] = 0
    return inputs(rng, share(five[:, e]), to)
def setup_inputs_twice(rng):
    to, large = graph(rng), np.zeros(N * P, bool)
    v = np.abs(rng.standard_normal((128, N * P, 4))) * np.exp2(rng.integers(-1, 2, (1, N * P, 1)))
    for i in range(P // 32):
        for r in rng.permutation(N):
            for j in rng.permutation(P):
                n1 = P * r + j
                n2 = to[n1, 1]
                p = np.array([to[n1, 0], n1, n2, to[n2, 0]])
                if i == 0:
                    m = to[[n1, n2], 2]
                    q = np.concatenate([p, m])
                    if large[q].any() or large[to[q]].any() or np.count_nonzero(np.isin(to[q], q)) != 10: continue
                    size = np.concatenate([rng.choice([1.0, 1.25], (128, 4, 4)), rng.choice([3.5, 4.0], (128, 2, 4))], axis=1) * 2.0 ** 26
                    v[:, q] = size * rng.choice([-1.0, 1.0], (128, 1, 4)) * np.array([1.0, 1.0, -1.0, -1.0, -1.0, 1.0])[None, :, None]
                    large[q] = True
                    large[to[m]] = True
                    break
                if large[p].any() or large[to[p]].any() or np.isin(to[p, 2], p).any() or to[p[0], 1] == p[3]: continue
                large[p] = True
                v[:, p] = (1 + 0.5 * rng.random((128, 4, 4))) * np.array([256.0, 64.0, 64.0, 256.0])[None, :, None]
                break
    return inputs(rng, share(v), to)
def check_inputs(d):
    b = []
    for k, low, high in (("x", -16, 28), ("w", -30, 30)):
        v = np.abs(d[k].astype(np.float32))
        if not (np.isfinite(v).all() and ((v == 0) | (v >= 2.0 ** low) & (v <= 2.0 ** high)).all()): b.append("a value of " + k)
    to, n = links(d["nb"]), np.arange(N * P)
    if to.min() < 0 or to.max() >= N * P: return b + ["range of nb"]
    for k in range(3):
        if (to[to[:, k], k] != n).any() or (to[:, k] == n).any(): b.append("edges k = %d are no pairs" % k)
    if (to[:, :2] // P != n[:, None] // P).any(): b.append("an edge k = 0 or 1 leaves its rank")
    if (to[:, 0] == to[:, 1]).any() or (to[:, 0] == to[:, 2]).any() or (to[:, 1] == to[:, 2]).any(): b.append("two edges of a node lead to the same node")
    c = np.zeros((N, N), int)
    np.add.at(c, (n // P, to[:, 2] // P), 1)
    if (c[~np.eye(N, dtype=bool)] != F).any(): b.append("number of edges between two ranks")
    return b
def scores(h, to):
    s = np.zeros((N * P, 3), np.float32)
    for i in range(0, N * P, 128):
        a = pick(h, np.arange(i, i + 128))
        for k in range(3): s[i:i + 128, k] = np.diagonal(mx_ref.matmul(a, pick(h, to[i:i + 128, k]))) + np.float32(0)
    return s
def reference(x, nb, w):
    to, n = links(nb), np.arange(N * P)
    h = join(*[mx_ref.quantize(np.ascontiguousarray(x[r])) for r in range(N)])
    merged, pr = np.zeros((N * P, 3), bool), np.zeros((N, R, P), np.float32)
    for t in range(R):
        s = scores(h, to)
        s[merged] = -np.inf
        c = np.argmax(s, axis=1)
        v = to[n, c]
        met = c[v] == c
        merged[n[met], c[met]] = True
        pr[:, t] = np.where(met, v, -1).reshape(N, P)
        d = decode(h).reshape(128, N * P, 4)
        m = np.float32(0.5) * d + np.float32(0.5) * d[:, np.where(met, v, n)]
        new = mx_ref.quantize(np.ascontiguousarray(m.reshape(128, -1).astype(BF)))
        h = pick(join(h, new), np.where(met, N * P + n, n))
    oc, osc, y = np.zeros((N, 128, 4 * P), np.uint8), np.zeros((N, 16, P), np.uint8), np.zeros((N, 128, P), np.float32)
    for r in range(N):
        own = pick(h, np.arange(P * r, P * r + P))
        oc[r], osc[r] = emit(own)
        y[r] = mx_ref.matmul(mx_ref.quantize(np.ascontiguousarray(w[r])), own)
    return {"oc": oc, "osc": osc, "pr": pr, "y": y}

@@ -1,0 +1,644 @@
+import math
+from concourse.bass import DstId, RemoteDMATransfer
+from concourse.mybir import dt, AluOpType, AxisListType, ActivationFunctionType
+
+OP = AluOpType
+AF = ActivationFunctionType
+NK = 2304
+BIG = 4096.0
+HOP = 0.06
+CY = 1.0e-3
+FP8, U8, F32, BF, I32, U16 = "float8_e4m3fn_x4", "uint8", "float32", "bfloat16", "int32", "uint16"
+
+SCRATCH = {"nst": ("dram", [16, 144], I32), "p32a": ("sbuf", [32, 32], F32), "p32": ("sbuf", [32, 32], F32),
+           "lm": ("sbuf", [32, 64], F32)}
+for _t, _l in (
+        (F32, "tk 16 tk32 32 j64 64 g48 48 cmp 128 k3 144 tb 16 d8 8 io32 32 col 16 col2 8 m48 48 mk 144 jl 16 gl 16 cl 16 dm 64 "
+              "rs16 64 rs8 48 gm 48 idn 128 msk 8 dw 32 iv 32 xg 192 hl 20 ld 24 xl0 48 xl1 48 mn 256 gs 512 gg 192 sc 64 pen 64 "
+              "sm 64 m0 2 m1 2 mx0 8 mx1 8 mm 16 mq 128 xd 256 jk 256 z 160 zp 160 fp 96 lnf 64 fl 144 ys 256"),
+        (BF, "xt 1024 wt 512 iob 256 rowb 256 vrow 256 ones 256 zt 2304 cs 2304 et 2048 pg 256 pt 256 ir 256 ig 256 it 256 "
+             "pos 256 posn 256 xr 512 nr 512 xlg 512 xlt 512 xng 768 xnt 768 nat 64 ct 2048 u0 512 u1 512 nt 1024"),
+        (I32, "nb2 48 nn 144 rowa 256 row16 256 nli 96 xi 36")):
+    _w = _l.split()
+    for _n, _k in zip(_w[0::2], _w[1::2]):
+        SCRATCH[_n] = ("sbuf", [128, int(_k)], _t)
+PIECE = {}
+for _b, _t, _l in (
+        ("uu", U16, "dup 32 dupc 16 ku 16 kdu 16 plu 16 l18 18 o01 32 of4 4 xo 4 ldu 32 pou 16 ofx 4 lp 32 ln 36"),
+        ("kk", F32, "nf 48 ns 16 klow 16 kt 16 kb 16 kj 16 ky 16 kf 16 kd 24 nlf 144 nl 48"),
+        ("kn", I32, "n2 16 ka 16 ki 16"),
+        ("cn", I32, "pp 4 n48 48 ci 16 ma 48 mb 48 mc 48 va 256 vb 256")):
+    _w, _c = _l.split(), 0
+    for _n, _k in zip(_w[0::2], _w[1::2]):
+        PIECE[_n] = (_b, _c, int(_k))
+        _c += int(_k)
+    SCRATCH[_b] = ("sbuf", [128, _c], _t)
+_w = "q0 256 qw 128 b0 768 b1 512 f 512 oq 256 eq 512 cq 512 uq 256 p0 256 p1 256".split()
+for _n, _k in zip(_w[0::2], _w[1::2]):
+    SCRATCH[_n + "c"] = ("sbuf", [128, int(_k)], FP8)
+    SCRATCH[_n + "s"] = ("sbuf", [128, int(_k)], U8)
+for _k in range(8):
+    SCRATCH["bk%d" % _k] = ("psum", [128, 512], F32)
+
+SEMAPHORES = ["qv", "qs", "qt", "qp", "lnb", "lx", "lw", "lst", "lnn", "st0", "loc", "a0", "a1", "e0", "e1"]
+
+
+def program(g, core, T, topo):
+    r = T.rank_of(core)
+    Q = {"v": g.vector, "s": g.scalar, "t": g.tensor, "y": g.sync, "p": g}
+    cnt = {}
+    known = {k: {} for k in Q}
+    acc = {}
+    ops = []
+    gate = [None]
+    group = {}
+
+    def meet(a, b):
+        return a[0] < b[1] and b[0] < a[1] and (a[0] - b[0]) % math.gcd(a[2], b[2]) == 0
+
+    def issue(q, fn, reads, writes, sem, n, dur, lat=None):
+        deps, me = set(), len(ops)
+        for w, regs in ((False, reads), (True, writes)):
+            for b, lo, hi, st in regs:
+                for a in acc.get(b, []):
+                    if (w or a[3]) and meet((lo, hi, st), a):
+                        deps.update(group.get(ops[a[4]][3], [a[4]]))
+        ops.append([q, fn, sorted(deps), sem, n, dur, dur if lat is None else lat, gate[0]])
+        if n != 1:
+            group.setdefault(sem, []).append(me)
+        for w, regs in ((False, reads), (True, writes)):
+            for b, lo, hi, st in regs:
+                l = acc.setdefault(b, [])
+                if w and st == 1:
+                    l[:] = [a for a in l if not (lo <= a[0] and a[1] <= hi)]
+                l.append((lo, hi, st, w, me))
+        return me
+
+    def order():
+        n = len(ops)
+        succ, left, prio = [[] for _ in ops], [len(o[2]) + (o[7] is not None) for o in ops], [0.0] * n
+        for i, o in enumerate(ops):
+            for d in o[2] + ([] if o[7] is None else [o[7]]):
+                succ[d].append(i)
+        for i in range(n - 1, -1, -1):
+            prio[i] = ops[i][6] + max([prio[j] + HOP for j in succ[i]] or [0.0])
+        ready, free, start = [0.0] * n, {q: 0.0 for q in "vstypa"}, [0.0] * n
+        cand = {q: [] for q in free}
+        for i in range(n):
+            if not left[i]:
+                cand[ops[i][0]].append(i)
+        for _ in range(n):
+            best = None
+            for q, l in cand.items():
+                if not l:
+                    continue
+                st = {i: max(0.0 if q == "a" else free[q], ready[i]) for i in l}
+                lo = min(st.values())
+                i = max((j for j in l if st[j] <= lo + 0.02), key=lambda j: prio[j])
+                better = [j for j in l if prio[j] > prio[i] and st[j] < st[i] + ops[i][5] - 0.05]
+                if better:
+                    i = max(better, key=lambda j: prio[j])
+                if best is None or st[i] < best[0]:
+                    best = (st[i], q, i)
+            t, q, i = best
+            cand[q].remove(i)
+            start[i] = t
+            free[q] = t + ops[i][5]
+            for j in succ[i]:
+                left[j] -= 1
+                ready[j] = max(ready[j], t + ops[i][6] + HOP)
+                if not left[j]:
+                    cand[ops[j][0]].append(j)
+        return sorted(range(n), key=lambda i: (start[i], i))
+
+    def emit():
+        total = {m: sum(ops[i][4] for i in l) for m, l in group.items()}
+        count, clock = [0] * len(ops), [None] * len(ops)
+        for i in order():
+            q, fn, deps, sem, n = ops[i][:5]
+            if q == "a":
+                count[i], clock[i] = n, {}
+                continue
+            kn = known[q]
+            for d in sorted(deps, key=lambda d: -count[d]):
+                if not ops[d][3] or (q == "t" and ops[d][0] == "t"):
+                    continue
+                m = ops[d][3]
+                c = total.get(m, count[d])
+                if kn.get(m, 0) < c:
+                    Q[q].wait_ge(T.sem[m], c)
+                    kn[m] = c
+                for k, v in clock[d].items():
+                    kn[k] = max(kn.get(k, 0), v)
+            ins = fn()
+            if sem:
+                ins.then_inc(T.sem[sem], n)
+                cnt[sem] = cnt.get(sem, 0) + n
+                count[i] = cnt[sem]
+            clock[i] = dict(kn)
+
+    def R(n, a=0, b=None, s=1, p=None):
+        n, base, w = PIECE.get(n, (n, 0, SCRATCH[n][1][1] if n in SCRATCH else 0))
+        a, b = base + a, base + (w if b is None else b)
+        c = slice(a, b) if s == 1 else slice(a, b, s)
+        ap = T[n][:, c] if p is None else T[n][0:p, c]
+        if SCRATCH[n][0] == "psum":
+            return ap, [(n, 0, 512, 1)]
+        return ap, [(n, a, b, s)]
+
+    def W32(v):
+        return v[0].bitcast(dt.uint32), v[1]
+
+    def W8(v):
+        return v[0].bitcast(dt.uint8), v[1]
+
+    def ind(win, off):
+        return win[0].indirect(off[0]), win[1] + off[1]
+
+    def val(s):
+        return (s[0], s[1]) if isinstance(s, tuple) else (s, [])
+
+    def us(n, c=1.0):
+        return max(64, n * c) * CY
+
+    def width(v):
+        r0 = v[1][0]
+        return -(-(r0[2] - r0[1]) // r0[3])
+
+    def half(*vs):
+        return 0.5 if all(SCRATCH[v[1][0][0]][2] in (BF, U16) for v in vs) else 1.0
+
+    def ts(o, i, s1, op0, s2=None, op1=None):
+        a, b = val(s1), val(s2)
+        rd = i[1] + a[1] + b[1]
+        if op1 is None:
+            issue("v", lambda: g.vector.tensor_scalar(o[0], i[0], a[0], None, op0), rd, o[1], "qv", 1, us(width(o), half(o, i)))
+        else:
+            issue("v", lambda: g.vector.tensor_scalar(o[0], i[0], a[0], b[0], op0, op1), rd, o[1], "qv", 1, us(width(o), half(o, i)))
+
+    def tt(o, a, b, op):
+        issue("v", lambda: g.vector.tensor_tensor(o[0], a[0], b[0], op), a[1] + b[1], o[1], "qv", 1,
+              us(width(o), 1 if a[1][0][0][:2] == "bk" else 2))
+
+    def cp(o, i):
+        issue("v", lambda: g.vector.tensor_copy(o[0], i[0]), i[1] + o[1][1:], o[1][:1], "qv", 1,
+              (0.05 + us(width(i), 3.5)) if len(o[1]) > 1 else (0.05 + us(width(o), 1.5)) if len(i[1]) > 1 else us(width(o), half(o, i)))
+
+    def fill(o, c):
+        issue("v", lambda: g.vector.memset(o[0], c), [], o[1], "qv", 1, us(width(o), half(o)))
+
+    def red(o, i):
+        issue("v", lambda: g.vector.tensor_reduce(o[0], i[0], AxisListType.X, OP.add), i[1], o[1], "qv", 1, us(width(i)))
+
+    def scan(o, a, b, op0, op1):
+        issue("v", lambda: g.vector.tensor_tensor_scan(o[0], a[0], b[0], 0.0, op0, op1), a[1] + b[1], o[1], "qv", 1, us(width(o), half(o, a)))
+
+    def tr(o, i):
+        issue("v", lambda: g.vector.transpose(o[0], i[0]), i[1], o[1], "qv", 1, us(width(o), half(o)))
+
+    def qz(c, s, i):
+        issue("v", lambda: g.vector.quantize_mx(c[0], s[0], i[0]), i[1], c[1] + s[1], "qv", 1, 0.02 + width(i) * 0.26e-3)
+
+    def act(o, i, f=AF.Copy, bias=None, scale=None, accum=None):
+        kw, rd, wr = {}, list(i[1]), list(o[1])
+        if bias is not None:
+            kw["bias"] = val(bias)[0]
+            rd += val(bias)[1]
+        if scale is not None:
+            kw["scale"] = val(scale)[0]
+            rd += val(scale)[1]
+        if accum is not None:
+            kw["accum_out"] = accum[0]
+            wr += accum[1]
+        issue("s", lambda: g.scalar.activation(o[0], i[0], f, **kw), rd, wr, "qs", 1,
+              (0.08 + us(width(o), 1.5)) if len(i[1]) > 1 else 0.03 + us(width(o)))
+
+    def mm(o, lc, ls, rc, rs, start=True, stop=True):
+        issue("t", lambda: g.tensor.matmul_mx(o[0], lc[0], ls[0], rc[0], rs[0], start, stop),
+              lc[1] + ls[1] + rc[1] + rs[1], o[1], "qt", 1, us(width(rc) + 16, 1.25))
+
+    def iota(o, pat, base, cm):
+        issue("p", lambda: g.iota(o[0], pat, base, cm, allow_small_or_imprecise_dtypes=True), [], o[1], "qp", 1, 0.13 + us(width(o), 2))
+
+    def dma(q, sem, out, i):
+        issue(q, lambda: Q[q].dma_start(out[0], i[0]), i[1], out[1], sem, 16, 0.07, 2.5)
+
+    for gr in range(8):
+        dma("y" if gr % 2 == 0 else "s", "lnb", (T.nb2[16 * gr:16 * gr + 16, :], [("nb2", 0, 48, 1)] if gr == 0 else []), (T.nb[:, :], []))
+    dma("y", "lx", R("xt"), (T.x[:, :], []))
+    for k in range(3):
+        i = 0
+        while i < 16:
+            a = (3 * i + k) % 16
+            n = min((15 - a) // 3 + 1, 16 - i)
+            dma("s", "lst", (T.nst[i:i + n, 48 * k:48 * k + 48], [("nst", 0, 144, 1)] if i + k == 0 else []),
+                (T.nb[a:a + 3 * (n - 1) + 1:3, :], []))
+            i += n
+    for gr in range(8):
+        dma("y", "lnn", (T.nn[16 * gr:16 * gr + 16, :], [("nn", 0, 144, 1)] if gr == 0 else []), (T.nst[:, :], [("nst", 0, 144, 1)]))
+    dma("y", "lw", R("wt"), (T.w[:, :], []))
+
+    iota(R("pp", 0, 1), [[0, 1]], 0, 1)
+    iota(R("n48"), [[1, 48]], 1, 0)
+    iota(R("tk"), [[1, 16]], 0, 0)
+    iota(R("rowa"), [[0, 16], [1, 16]], 0, 0)
+    iota(R("row16"), [[16, 16], [0, 16]], 0, 0)
+    iota(R("tb"), [[32, 8], [0, 2]], 0, 0)
+    iota(R("k3"), [[0, 48], [1, 3]], 0, 0)
+    iota(R("j64"), [[0, 4], [1, 16]], 0, 0)
+    iota(R("g48"), [[0, 6], [1, 8]], 0, 0)
+    iota(R("cmp"), [[1, 128]], 0, -1)
+    iota(R("tk32"), [[0, 2], [1, 16]], 0, 0)
+    iota(R("d8"), [[0, 2], [1, 4]], 0, 0)
+    iota(R("io32"), [[1, 32]], 0, 0)
+    iota(R("iob"), [[1, 256]], 0, 0)
+    iota(R("rowb"), [[0, 16], [1, 16]], 0, 0)
+    fill(R("zt", 0, 1152), 0.0)
+    fill(R("zt", 1152, NK), 0.0)
+    act(R("et"), R("zt", 0, 2048))
+    act(R("u0"), R("et", 0, 512))
+    act(R("u1"), R("et", 512, 1024))
+    fill(R("ones"), 1.0)
+
+    def c(k):
+        return R("ci", k, k + 1)
+
+    def col(k):
+        return R("col", k, k + 1)
+
+    def col2(k):
+        return R("col2", k, k + 1)
+    ts(c(0), R("pp", 0, 1), 15, OP.bitwise_and)
+    ts(c(1), R("pp", 0, 1), 4, OP.arith_shift_right)
+    ts(c(2), R("pp", 0, 1), 5, OP.arith_shift_right)
+    ts(c(8), c(0), 11, OP.mult, 10, OP.add)
+    for k in range(3):
+        ts(c(9 + k), c(0), 3, OP.mult, k, OP.add)
+    ts(c(3), c(1), 1, OP.bitwise_and)
+    ts(c(4), c(8), 15, OP.bitwise_and)
+    ts(R("ci", 5, 8), R("ci", 9, 12), 4, OP.arith_shift_right)
+    ts(c(12), c(11), 15, OP.bitwise_and)
+    cp(R("col", 0, 13), R("ci", 0, 13))
+    ts(R("ma"), R("n48"), col(0), OP.add)
+    ts(R("mb"), R("ma"), 43, OP.mult)
+    ts(R("mc"), R("mb"), 7, OP.arith_shift_right)
+    ts(R("mb"), R("mc"), 3, OP.mult)
+    tt(R("m48"), R("ma"), R("mb"), OP.is_equal)
+    ts(R("jl"), R("tk"), 16.0, OP.mult, col(4), OP.add)
+    ts(R("gl"), R("jl"), 256.0 * r, OP.add)
+    ts(col2(0), col(3), -1.0, OP.mult, 1.0, OP.add)
+    ts(col2(1), col(3), 16.0, OP.mult, col(0), OP.add)
+    ts(col2(3), col(1), 8.0, OP.add)
+    ts(col2(4), col(0), 2.0, OP.mult)
+    ts(col2(5), col(0), 2.0, OP.mult, 1.0, OP.add)
+    ts(R("va"), R("rowa"), 11, OP.mult, 10, OP.add)
+    ts(R("vb"), R("va"), 15, OP.bitwise_and)
+    tt(R("vrow"), R("vb"), R("row16"), OP.add)
+    ts(R("dup", 0, 16), R("tb"), col2(1), OP.add)
+    ts(R("dupc"), R("tk"), 16.0, OP.mult, col(12), OP.add)
+
+    tt(R("nf"), R("nb2"), R("m48"), OP.mult)
+    tt(R("ns"), R("nf", 0, 48, 3), R("nf", 1, 48, 3), OP.add)
+    tt(R("n2"), R("ns"), R("nf", 2, 48, 3), OP.add)
+    ts(R("ka"), R("n2"), 256 * r, OP.bitwise_and)
+    ts(R("ki"), R("n2"), 255, OP.bitwise_and)
+    tt(R("klow"), R("n2"), R("gl"), OP.is_gt)
+    ts(R("kt"), R("n2"), 256.0 * (r + 1), OP.is_lt, -256.0, OP.mult)
+    ts(R("kb"), R("ka"), -2.0, OP.mult, 256.0 * r + 256.0, OP.add)
+    tt(R("kj"), R("jl"), R("ki"), OP.subtract)
+    tt(R("ky"), R("kb"), R("n2"), OP.add)
+    tt(R("kb"), R("kj"), R("kt"), OP.add)
+    tt(R("kj"), R("kb"), R("klow"), OP.mult)
+    tt(R("kf"), R("ky"), R("kj"), OP.add)
+    cp(R("ku"), R("kf"))
+    cp(ind(R("zt"), R("ku")), R("ones"))
+    act(R("kd", 0, 8), R("kf", 0, 16, 2), AF.Copy, scale=col2(0))
+    act(R("kd", 8, 16), R("kf", 1, 16, 2), AF.Copy, scale=col(3))
+    scan(R("cs"), R("zt"), R("zt"), OP.add, OP.max)
+    tt(R("kd", 16, 24), R("kd", 0, 8), R("kd", 8, 16), OP.add)
+    cp(R("kdu", 0, 16, 2), R("kd", 16, 24))
+    cp(R("kdu", 1, 16, 2), R("kd", 16, 24))
+    cp(R("pg"), ind(R("cs"), R("kdu")))
+    act(R("pos"), ind(R("cs"), R("ku")))
+    act(R("posn"), ind(R("pos"), R("dupc")))
+    tr(R("pt"), R("pg"))
+    ts(R("plu"), R("pt", 0, 256, 16), -1.0, OP.add)
+    cp(ind(R("ir"), R("plu")), R("vrow"))
+    cp(R("ig"), ind(R("ir"), R("dup", 0, 16)))
+    qz(R("q0c"), R("q0s"), R("xt"))
+    tr(R("it"), R("ig"))
+    cp(R("l18", 0, 16), R("it", 0, 256, 16))
+    cp(R("l18", 16, 17), R("it", 16, 17))
+    cp(R("l18", 17, 18), R("it", 0, 1))
+
+    def pick(dc, ds, a, b, sc, ss, w0, w1, off):
+        cp(W32(R(dc, a, b)), ind(W32(R(sc, w0, w1)), off))
+        act(R(ds, a, b), ind(R(ss, w0, w1), off))
+
+    others = [d for d in range(1, 8)]
+    far = [d for d in others if topo.die(T.cores[r ^ d]) != topo.die(core)]
+    near = [d for d in others if d not in far]
+    lanes = {}
+    for k, l in enumerate((far, near)):
+        for n, d in enumerate(l):
+            e = topo.engines(core, T.cores[r ^ d])
+            lanes[d] = [e[4 * n + k], e[4 * n + 2 + k]]
+
+    def send(srcs, dsts, sem, regs):
+        def call():
+            tf = []
+            for d in others:
+                ad = topo.addr(T.cores[r ^ d])
+                tf.append(RemoteDMATransfer(dst_ids=[DstId(rid=ad[0], pnc=ad[1])], dma_engine_mask=sum(1 << e for e in lanes[d]),
+                                            remote_sem=T.sem[sem], src=srcs(d), dst=dsts(d)))
+            g.remote_dma_fused(tf, local_sem=T.sem.loc)
+            cnt["loc"] = cnt.get("loc", 0) + 14
+        me = issue("p", call, [(b, lo, hi, 1) for b, lo, hi in regs], [], None, 1, 0.7, 0.7)
+        group.setdefault(sem, []).append(len(ops))
+        ops.append(["a", None, [me], sem, 14, 0.0, 2.5, None])
+
+    def arrive(sem, b, lo, hi):
+        acc.setdefault(b, []).append((lo, hi, 1, True, group[sem][0]))
+
+    def send_w(bc, bs, sem):
+        send(lambda d: T[bc][:, 32 * d:32 * d + 32].bitcast(dt.uint8), lambda d: T[bc][:, 256 + 32 * d:288 + 32 * d].bitcast(dt.uint8),
+             sem, [(bc, 0, 256)])
+        send(lambda d: T[bs][:, 32 * d:32 * d + 32], lambda d: T[bs][:, 256 + 32 * d:288 + 32 * d], sem, [(bs, 0, 256)])
+
+    def bank(k, n):
+        return R("bk%d" % k, 0, n)
+
+    def gram(bc, bs):
+        for h in range(2):
+            mm(bank(h, 256), R(bc, 128 * h, 128 * h + 128), R(bs, 128 * h, 128 * h + 128), R(bc, 0, 256), R(bs, 0, 256))
+        cp(R("gs", 0, 256), bank(0, 256))
+        act(R("gs", 256, 512), bank(1, 256))
+
+    BK = [[4, 5, 6, 7], [0, 1, 2, 3]]
+
+    def dec(h, b, cc, cs, start):
+        mm(bank(BK[h][b], 128), R("eqc", 128 * b, 128 * b + 128), R("eqs", 128 * b, 128 * b + 128),
+           R(cc, 128 * h, 128 * h + 128), R(cs, 128 * h, 128 * h + 128), start, not start)
+
+    def local_scores(t):
+        for h in range(2):
+            cp(R("gg", 32 * h, 32 * h + 32), ind(R("gs", 256 * h, 256 * h + 256), R("xo", 2 * h, 2 * h + 2)))
+        tt(R("gg", 64, 128), R("gg", 0, 64), R("dm"), OP.mult)
+        scan(R("sc"), R("rs16"), R("gg", 64, 128), OP.mult, OP.add)
+        s0, s1 = R("sc", 15, 64, 32), R("sc", 31, 64, 32)
+        if t == 1:
+            for k in range(2):
+                tt(R("sm", 32 + k, 36, 2), R("sc", 15 + 16 * k, 64, 32), R("pen", 2 * k, 2 * k + 2), OP.add)
+            s0, s1 = R("sm", 32, 36, 2), R("sm", 33, 36, 2)
+        m = "m%d" % t
+        tt(R(m), s0, s1, OP.max)
+        send(lambda d: T[m][:, d // 4:d // 4 + 1], lambda d: T["mx%d" % t][:, d:d + 1], "e%d" % t, [(m, 0, 2)])
+        tt(R("sm", 0, 2), s0, s1, OP.is_ge)
+        act(R("sm", 2, 4), R("sm", 0, 2), AF.Copy, bias=-4e29, scale=4e29)
+        act(R("sm", 4, 6), R("sm", 0, 2), AF.Copy, scale=-4e29)
+        tt(R("sm", 8, 12, 2), s0, R("sm", 2, 4), OP.add)
+        tt(R("sm", 9, 12, 2), s1, R("sm", 4, 6), OP.add)
+        ts(R("lm", 0, 32), R("p32"), R(m, 0, 1, 1, 32), OP.mult)
+        tr(R("lm", 32, 64), R("lm", 0, 32))
+        red(R("mm", 0, 1, 1, 32), R("lm", 32, 64))
+
+    def biased(t):
+        for h in range(2):
+            for k in range(2):
+                a = 64 * h + 32 * k
+                act(R("mq", a, a + 32), R("mn", 128 * t + a, 128 * t + a + 32), AF.Identity, bias=R("sm", 8 + 2 * h + k, 9 + 2 * h + k))
+
+    def statics(t, hi_own, hl):
+        for h in range(2):
+            a = 128 * t + 64 * h
+            ts(R("mn", a, a + 64, 2), R("tk32"), hi_own[h], OP.not_equal, -8e29, OP.mult)
+            for k in range(2):
+                ts(R("mn", a + 32 * k + 1, a + 32 * k + 32, 2), R("tk"), R("hl", hl + 2 * h + k, hl + 2 * h + k + 1), OP.not_equal, -8e29, OP.mult)
+            ts(R("nat", 32 * t + 16 * h, 32 * t + 16 * h + 16), R("tk"), hi_own[h], OP.is_equal, 2.0, OP.mult)
+
+    def weights(t, lo_own, hl):
+        for h in range(2):
+            ts(R("ct", 1024 * t + h, 1024 * t + 1024, 4), R("rowb"), lo_own[h], OP.is_equal, BIG, OP.mult)
+            for k in range(2):
+                a = 1024 * t + 512 * k
+                ts(R("ct", a + 2 + h, a + 512, 4), R("rowb", 0, 128), R("hl", hl + 4 + 2 * h + k, hl + 5 + 2 * h + k), OP.is_equal, BIG, OP.mult)
+        qz(R("cqc", 256 * t, 256 * t + 256), R("cqs", 256 * t, 256 * t + 256), R("ct", 1024 * t, 1024 * t + 1024))
+
+    def choose(t, bc, bs):
+        u, uq, m = "u%d" % t, 128 * t, "m%d" % t
+        arrive("a%d" % t, bc, 288, 512)
+        arrive("a%d" % t, bs, 288, 512)
+        for h in range(2):
+            mm(bank(2 + h, 128), R(bc, 128 * h, 128 * h + 128), R(bs, 128 * h, 128 * h + 128),
+               R(bc, 256 + 128 * h, 384 + 128 * h), R(bs, 256 + 128 * h, 384 + 128 * h))
+        arrive("e%d" % t, "mx%d" % t, 0, 8)
+        tt(R("mm", 1, 8), R("mx%d" % t, 1, 8), R("msk", 1, 8), OP.mult)
+        red(R("mm", 8, 9), R("mm", 0, 4))
+        red(R("mm", 9, 10), R("mm", 4, 8))
+        for h in range(2):
+            tt(R("xd", 128 * h, 128 * h + 128), bank(2 + h, 128), R("idn"), OP.mult)
+        act(R("jk", 0, 128), R("xd", 0, 128), AF.Identity, accum=R("sm", 16, 17))
+        red(R("sm", 17, 18), R("xd", 128, 256))
+        s2 = 16
+        if t == 1:
+            tt(R("sm", 18, 20), R("sm", 16, 18), R("pen", 4, 6), OP.add)
+            s2 = 18
+        for h in range(2):
+            ts(R("ofx", 2 * h, 2 * h + 1), R("sm", s2 + h, s2 + h + 1), R("mm", 8 + h, 9 + h), OP.is_gt, col2(4), OP.add)
+        for h in range(2):
+            act(R("jk", 128 + 16 * h, 144 + 16 * h), ind(R("dw"), R("ofx", 2 * h, 2 * h + 1)), AF.Copy, accum=R("sm", 20 + h, 21 + h))
+        tt(R("sm", 22, 24), R("sm", s2, s2 + 2), R(m), OP.is_gt)
+        for h in range(2):
+            ts(R(u, h, 128, 2), R("mq", 64 * h, 64 * h + 64), R("sm", s2 + h, s2 + h + 1), OP.is_ge)
+        for h in range(2):
+            ts(R(u, 128 + h, 192, 4), R("nat", 32 * t + 16 * h, 32 * t + 16 * h + 16), R("sm", 20 + h, 21 + h), OP.mult, R("sm", 22 + h, 23 + h), OP.mult)
+        qz(R("uqc", uq, uq + 128), R("uqs", uq, uq + 128), R(u))
+        for k in range(2):
+            ca = 256 * t + 128 * k
+            mm(bank(2 + k, 128), R("cqc", ca, ca + 128), R("cqs", ca, ca + 128), R("uqc", uq, uq + 128), R("uqs", uq, uq + 128))
+        z, xl, off = 80 * t, "xl%d" % t, 16 * t
+        tt(R("z", z, z + 16), R("bk2", 0, 16), R(xl, 0, 16), OP.add)
+        tt(R("z", z + 16, z + 48), R("bk3", 16, 48), R(xl, 16, 48), OP.add)
+        tt(R("z", z + 48, z + 64), R("z", z, z + 16), R("z", z + 16, z + 32), OP.max)
+        tt(R("z", z + 64, z + 80), R("z", z + 48, z + 64), R("z", z + 32, z + 48), OP.max)
+        ts(R("lp", off, off + 16), R("z", z + 64, z + 80), -2 * BIG - 1.0, OP.add)
+
+    def own_parts(cc, cs):
+        for b in range(4):
+            dec(0, b, cc, cs, True)
+        for b in range(2):
+            dec(1, b, cc, cs, True)
+
+    def merge(t, bc, bs, cc, cs, base, after_lists, half_done):
+        pc, psn, off = "p%dc" % t, "p%ds" % t, 16 * t
+        for h in range(2):
+            pick(pc, psn, 128 * h, 128 * h + 128, bc, bs, 0, 512, R("lp", off + 8 * h, off + 8 * h + 8))
+        for b in range(2, 4):
+            dec(1, b, cc, cs, True)
+        for h in range(2):
+            for b in range(4):
+                dec(h, b, pc, psn, False)
+        after_lists()
+        for h in range(2):
+            for b in range(4):
+                oo, ii = R("nt", 512 * h + b, 512 * h + 512, 4), bank(BK[h][b], 128)
+                if b % 2 == 0:
+                    cp(oo, ii)
+                else:
+                    act(oo, ii)
+            qz(R(cc, base + 128 * h, base + 128 * h + 128), R(cs, base + 128 * h, base + 128 * h + 128), R("nt", 512 * h, 512 * h + 512))
+            half_done(h)
+
+    pick("b0c", "b0s", 0, 256, "q0c", "q0s", 0, 256, R("l18", 0, 16))
+    send_w("b0c", "b0s", "a0")
+    pick("b0c", "b0s", 256, 288, "q0c", "q0s", 0, 256, R("l18", 16, 18))
+    gram("b0c", "b0s")
+    for k in range(3):
+        ts(R("mk", 48 * k, 48 * k + 48), R("k3", 0, 48), col(5 + k), OP.is_equal)
+    tt(R("nlf"), R("nn"), R("mk"), OP.mult)
+    tt(R("nl"), R("nlf", 0, 144, 3), R("nlf", 1, 144, 3), OP.add)
+    tt(R("nli", 0, 48), R("nl"), R("nlf", 2, 144, 3), OP.add)
+    ts(R("nli", 48, 80), R("nli", 0, 32), 255, OP.bitwise_and)
+    cp(R("o01"), R("nli", 48, 80))
+    act(R("xr"), ind(R("posn"), R("o01")))
+    ts(R("gm"), R("g48"), col(1), OP.is_equal)
+    ts(R("rs8"), R("g48"), 0.0, OP.not_equal)
+    ts(R("rs16"), R("j64"), 0.0, OP.not_equal)
+    ts(R("dm"), R("j64"), col(0), OP.is_equal)
+    tt(R("iv", 0, 16), R("it", 0, 256, 16), R("gm", 0, 16), OP.mult)
+    scan(R("iv", 16, 32), R("rs8", 0, 16), R("iv", 0, 16), OP.mult, OP.add)
+    inv = R("iv", 23, 32, 8)
+    cp(R("of4", 0, 4, 2), inv)
+    ts(R("of4", 1, 4, 2), inv, 256.0, OP.add)
+    cp(R("xg", 0, 64), ind(R("xr"), R("of4")))
+    tt(R("xg", 64, 128), R("xg", 0, 64), R("dm"), OP.mult)
+    scan(R("xg", 128, 192), R("rs16"), R("xg", 64, 128), OP.mult, OP.add)
+    ts(R("xo"), R("xg", 143, 192, 16), -1.0, OP.add)
+    tt(R("p32a"), R("cmp", 0, 32, 1, 32), R("cmp", 0, 32, 1, 32), OP.mult)
+    ts(R("p32"), R("p32a"), 256.0, OP.is_equal)
+    fill(R("mm"), 0.0)
+    local_scores(0)
+    ts(R("xi", 0, 4), R("xg", 143, 192, 16), -1.0, OP.add)
+    ts(R("xi", 4, 8), R("xi", 0, 4), 4, OP.arith_shift_right)
+    ts(R("xi", 8, 12), R("xi", 0, 4), 15, OP.bitwise_and)
+    cp(R("hl", 0, 8), R("xi", 4, 12))
+    statics(0, [col(1), col2(3)], 0)
+    biased(0)
+    ts(R("idn"), R("cmp"), 0.0, OP.is_equal)
+    ts(R("msk"), R("d8"), col(2), OP.is_equal)
+    ts(R("dw"), R("io32"), col2(5), OP.is_equal)
+    weights(0, [col(0), col(0)], 0)
+    act(R("ld", 0, 8), R("it", 0, 256, 32), AF.Copy, scale=col2(0))
+    act(R("ld", 8, 16), R("it", 16, 256, 32), AF.Copy, scale=col(3))
+    tt(R("ld", 16, 24), R("ld", 0, 8), R("ld", 8, 16), OP.add)
+    for k in range(2):
+        for w in range(2):
+            ts(R("ldu", 16 * k + w, 16 * k + 16, 2), R("ld", 16, 24), 256.0 * k, OP.add)
+    act(R("xlg"), ind(R("xr"), R("ldu")))
+    for b in range(4):
+        act(R("et", b + 512 * b, 512 * b + 512, 4), R("idn"), AF.Copy, scale=0.5)
+        qz(R("eqc", 128 * b, 128 * b + 128), R("eqs", 128 * b, 128 * b + 128), R("et", 512 * b, 512 * b + 512))
+    tr(R("xlt"), R("xlg"))
+    act(R("xl0", 0, 32), R("xlt", 0, 512, 16))
+    act(R("cl"), R("tk"), AF.Identity, bias=col(0), scale=16.0)
+    act(R("xl0", 32, 48), R("cl"), AF.Copy, bias=257.0)
+    own_parts("b0c", "b0s")
+    choose(0, "b0c", "b0s")
+    picked = []
+
+    def lists0():
+        ts(R("lnf", 0, 16), R("z", 64, 80), 2 * BIG, OP.is_ge, 512.0, OP.mult)
+        tt(R("lnf", 16, 32), R("lnf", 0, 16), R("cl"), OP.add)
+        cp(R("ln", 0, 16), R("lnf", 16, 32))
+        cp(R("ln", 16, 17), R("lnf", 17, 18))
+        cp(R("ln", 17, 18), R("lnf", 16, 17))
+
+    def half0(h):
+        if h == 0:
+            pick("b1c", "b1s", 0, 128, "b0c", "b0s", 0, 640, R("ln", 0, 8))
+        else:
+            pick("b1c", "b1s", 128, 256, "b0c", "b0s", 0, 768, R("ln", 8, 16))
+            picked.append(len(ops) - 2)
+    merge(0, "b0c", "b0s", "b0c", "b0s", 512, lists0, half0)
+
+    send_w("b1c", "b1s", "a1")
+    pick("b1c", "b1s", 256, 288, "b0c", "b0s", 0, 640, R("ln", 16, 18))
+    gram("b1c", "b1s")
+    ts(R("fl", 0, 48), R("z", 0, 48), 2 * BIG, OP.is_ge)
+    tt(R("fl", 48, 96), R("fl", 0, 48), R("gm"), OP.mult)
+    scan(R("fl", 96, 144), R("rs8"), R("fl", 48, 96), OP.mult, OP.add)
+    ts(R("pen", 0, 6), R("fl", 103, 144, 8), -1e29, OP.mult)
+    local_scores(1)
+    gate[0] = picked[0]
+    ts(R("dup", 16, 32), R("tb"), col2(1), OP.add, 256.0, OP.add)
+    act(R("nr"), ind(R("iob"), R("o01")))
+    act(R("xng", 0, 512), ind(R("xr"), R("dup")))
+    act(R("xng", 512, 768), ind(R("posn"), R("dup", 0, 16)))
+    cp(R("xg", 0, 64), ind(R("nr"), R("of4")))
+    tt(R("xg", 64, 128), R("xg", 0, 64), R("dm"), OP.mult)
+    scan(R("xg", 128, 192), R("rs16"), R("xg", 64, 128), OP.mult, OP.add)
+    cp(R("xi", 12, 16), R("xg", 143, 192, 16))
+    cp(R("xi", 16, 18), inv)
+    ts(R("xi", 18, 24), R("xi", 12, 18), 4, OP.arith_shift_right)
+    ts(R("xi", 24, 30), R("xi", 12, 18), 15, OP.bitwise_and)
+    cp(R("hl", 8, 12), R("xi", 18, 22))
+    cp(R("hl", 12, 16), R("xi", 24, 28))
+    cp(R("hl", 16, 18), R("xi", 22, 24))
+    cp(R("hl", 18, 20), R("xi", 28, 30))
+    statics(1, [R("hl", 16, 17), R("hl", 17, 18)], 8)
+    biased(1)
+    tr(R("xnt"), R("xng"))
+    ts(R("pou"), R("xnt", 512, 768, 16), -1.0, OP.add)
+    pick("fc", "fs", 0, 256, "b1c", "b1s", 0, 256, R("pou"))
+    act(R("xl1", 0, 32), R("xnt", 0, 512, 16))
+    act(R("xl1", 32, 48), R("xnt", 512, 768, 16), AF.Copy, bias=256.0)
+    weights(1, [R("hl", 18, 19), R("hl", 19, 20)], 8)
+    for k in range(3):
+        for h in range(2):
+            ts(R("u1", 192 + 64 * k + h, 256 + 64 * k, 4), R("nat", 32 + 16 * h, 48 + 16 * h), R("fl", 103 + 8 * (2 * k + h), 104 + 8 * (2 * k + h)), OP.mult)
+    qz(R("qwc"), R("qws"), R("wt"))
+    gate[0] = None
+    own_parts("fc", "fs")
+    choose(1, "b1c", "b1s")
+    tt(R("zp", 0, 16), R("bk2", 0, 16), R("nli", 0, 16), OP.add)
+    tt(R("zp", 16, 48), R("bk3", 16, 48), R("nli", 16, 48), OP.add)
+    tt(R("zp", 48, 96), R("bk3", 48, 96), R("nli", 0, 48), OP.add)
+
+    def lists1():
+        ts(R("lnf", 32, 48), R("z", 144, 160), 2 * BIG, OP.is_ge, 256.0, OP.mult)
+        tt(R("lnf", 48, 64), R("lnf", 32, 48), R("cl"), OP.add)
+        cp(R("ln", 20, 36), R("lnf", 48, 64))
+        for t in range(2):
+            a = 48 - 48 * t
+            tt(R("zp", 128 + 16 * t, 144 + 16 * t), R("zp", a, a + 16), R("zp", a + 16, a + 32), OP.max)
+            tt(R("zp", 96 + 16 * t, 112 + 16 * t), R("zp", 128 + 16 * t, 144 + 16 * t), R("zp", a + 32, a + 48), OP.max)
+        ts(R("fp", 0, 32), R("zp", 96, 128), -2 * BIG, OP.add, -1.0, OP.max)
+        tt(R("fp", 32, 64), R("fp", 0, 32), R("gm", 0, 32), OP.mult)
+        scan(R("fp", 64, 96), R("rs8", 0, 32), R("fp", 32, 64), OP.mult, OP.add)
+        for t in range(2):
+            for h in range(2):
+                a = 64 + 8 * (2 * t + h) + 7
+                dma("y", "st0", (T.pr[t:t + 1, 128 * h:128 * h + 128], []), R("fp", a, a + 1))
+
+    def half1(h):
+        a, b = 128 * h, 128 * h + 128
+        pick("oqc", "oqs", a, b, "fc", "fs", 0, 384 + 128 * h, R("ln", 20 + 8 * h, 28 + 8 * h))
+        dma("y", "st0", (T.oc[:, 4 * a:4 * b], []), W8(R("oqc", a, b)))
+        mm(bank(4 + h, 128), R("qwc"), R("qws"), R("oqc", a, b), R("oqs", a, b))
+    merge(1, "b1c", "b1s", "fc", "fs", 256, lists1, half1)
+    for k in range(4):
+        dma("s" if k % 2 else "y", "st0", (T.osc[4 * k:4 * k + 4, :], []), (T.oqs[32 * k:32 * k + 4, :], [("oqs", 0, 256, 1)]))
+    cp(R("ys", 0, 128), bank(4, 128))
+    act(R("ys", 128, 256), bank(5, 128))
+    for h in range(2):
+        dma("y" if h == 0 else "s", "st0", (T.y[:, 128 * h:128 * h + 128], []), R("ys", 128 * h, 128 * h + 128))
+
+    emit()
+    cnt.update({"a0": 28, "a1": 28, "e0": 14, "e1": 14})
+    for sem in sorted(cnt):
+        g.wait_ge(T.sem[sem], cnt[sem])
+
+
+def rank_program(g, core, T, topo):
+    if T.rank_of(core) is not None:
+        program(g, core, T, topo)

@@ -6,28 +6,28 @@ OP = AluOpType
 AF = ActivationFunctionType
 NK = 2304
 BIG = 4096.0
-HOP = 0.06
-CY = 1.0e-3
+HOP = 0.14
+CY = 1.1e-3
 FP8, U8, F32, BF, I32, U16 = "float8_e4m3fn_x4", "uint8", "float32", "bfloat16", "int32", "uint16"
 
-SCRATCH = {"nst": ("dram", [16, 144], I32), "p32a": ("sbuf", [32, 32], F32), "p32": ("sbuf", [32, 32], F32),
+SCRATCH = {"nst": ("dram", [16, 92], I32), "p32a": ("sbuf", [32, 32], F32), "p32": ("sbuf", [32, 32], F32),
            "lm": ("sbuf", [32, 64], F32)}
 for _t, _l in (
-        (F32, "tk 16 tk32 32 j64 64 g48 48 cmp 128 k3 144 tb 16 d8 8 io32 32 col 16 col2 8 m48 48 mk 144 jl 16 gl 16 cl 16 dm 64 "
-              "rs16 64 rs8 48 gm 48 idn 128 msk 8 dw 32 iv 32 xg 192 hl 20 ld 24 xl0 48 xl1 48 mn 256 gs 512 gg 192 sc 64 pen 64 "
-              "sm 64 m0 2 m1 2 mx0 8 mx1 8 mm 16 mq 128 xd 256 jk 256 z 160 zp 160 fp 96 lnf 64 fl 144 ys 256"),
-        (BF, "xt 1024 wt 512 iob 256 rowb 256 vrow 256 ones 256 zt 2304 cs 2304 et 2048 pg 256 pt 256 ir 256 ig 256 it 256 "
-             "pos 256 posn 256 xr 512 nr 512 xlg 512 xlt 512 xng 768 xnt 768 nat 64 ct 2048 u0 512 u1 512 nt 1024"),
-        (I32, "nb2 48 nn 144 rowa 256 row16 256 nli 96 xi 36")):
+        (F32, "tk 16 tk32 32 j64 64 g48 48 cmp 128 k3 48 tb 16 d8 8 io32 32 cf 2 col 4 col2 8 jl 16 gl 16 dm 64 rs16 64 rs8 48 rs3 48 "
+              "gm 48 idn 128 msk 16 dw 32 iv 64 xg 64 hl 20 ld 24 xl0 48 xl1 48 mn 256 gs 528 gg 64 sc 64 pen 16 sm 64 m0 2 m1 2 "
+              "ma0 8 ma1 8 mx0 8 mx1 8 lmm 1 mq 128 xd 256 jk 256 z 192 zp 160 fp 96 lnf 64 fl 144 ys 256"),
+        (BF, "xt 1024 wt 512 iob 256 rowb 256 ones 256 zt 2304 cs 2304 et 2048 pg 256 pt 256 ir 256 ig 256 it 256 "
+             "posn 256 xr 512 nr 512 xlg 512 xlt 512 xng 768 xnt 768 nat 64 ct 2048 u0 512 u1 512 nt 1024"),
+        (I32, "nb2 48 nn 92 xi 160")):
     _w = _l.split()
     for _n, _k in zip(_w[0::2], _w[1::2]):
         SCRATCH[_n] = ("sbuf", [128, int(_k)], _t)
 PIECE = {}
 for _b, _t, _l in (
-        ("uu", U16, "dup 32 dupc 16 ku 16 kdu 16 plu 16 l18 18 o01 32 of4 4 xo 4 ldu 32 pou 16 ofx 4 lp 32 ln 36"),
-        ("kk", F32, "nf 48 ns 16 klow 16 kt 16 kb 16 kj 16 ky 16 kf 16 kd 24 nlf 144 nl 48"),
-        ("kn", I32, "n2 16 ka 16 ki 16"),
-        ("cn", I32, "pp 4 n48 48 ci 16 ma 48 mb 48 mc 48 va 256 vb 256")):
+        ("uu", U16, "dup 32 ku 16 kdu 16 plu 16 l18 18 o01 32 of4 4 xo 4 xoa 4 ldu 32 pou 16 ofx 8 lp 32 ln 36 cc 2"),
+        ("kk", F32, "klow 16 kt 16 kb 16 kl 16 k1 16 k2 16 kf 16 kd 24"),
+        ("kn", I32, "ka 16 kh 16 km 16 ki 16"),
+        ("cn", I32, "pp 4 ci 4")):
     _w, _c = _l.split(), 0
     for _n, _k in zip(_w[0::2], _w[1::2]):
         PIECE[_n] = (_b, _c, int(_k))
@@ -106,7 +106,7 @@ def program(g, core, T, topo):
             free[q] = t + ops[i][5]
             for j in succ[i]:
                 left[j] -= 1
-                ready[j] = max(ready[j], t + ops[i][6] + HOP)
+                ready[j] = max(ready[j], t + ops[i][6] + (HOP if i in ops[j][2] else 0.0))
                 if not left[j]:
                     cand[ops[j][0]].append(j)
         return sorted(range(n), key=lambda i: (start[i], i))
@@ -178,7 +178,7 @@ def program(g, core, T, topo):
 
     def tt(o, a, b, op):
         issue("v", lambda: g.vector.tensor_tensor(o[0], a[0], b[0], op), a[1] + b[1], o[1], "qv", 1,
-              us(width(o), 1 if a[1][0][0][:2] == "bk" else 2))
+              (0.05 + us(width(o), 1.5)) if len(a[1]) > 1 else us(width(o), 1 if a[1][0][0][:2] == "bk" else 2))
 
     def cp(o, i):
         issue("v", lambda: g.vector.tensor_copy(o[0], i[0]), i[1] + o[1][1:], o[1][:1], "qv", 1,
@@ -223,42 +223,47 @@ def program(g, core, T, topo):
     def dma(q, sem, out, i):
         issue(q, lambda: Q[q].dma_start(out[0], i[0]), i[1], out[1], sem, 16, 0.07, 2.5)
 
-    for gr in range(8):
-        dma("y" if gr % 2 == 0 else "s", "lnb", (T.nb2[16 * gr:16 * gr + 16, :], [("nb2", 0, 48, 1)] if gr == 0 else []), (T.nb[:, :], []))
-    dma("y", "lx", R("xt"), (T.x[:, :], []))
+    runs = []
     for k in range(3):
         i = 0
         while i < 16:
             a = (3 * i + k) % 16
             n = min((15 - a) // 3 + 1, 16 - i)
-            dma("s", "lst", (T.nst[i:i + n, 48 * k:48 * k + 48], [("nst", 0, 144, 1)] if i + k == 0 else []),
-                (T.nb[a:a + 3 * (n - 1) + 1:3, :], []))
+            runs.append((k, i, n, T.nb[a:a + 3 * (n - 1) + 1:3, (3 * i + k) // 16:(3 * i + k) // 16 + 46]))
             i += n
     for gr in range(8):
-        dma("y", "lnn", (T.nn[16 * gr:16 * gr + 16, :], [("nn", 0, 144, 1)] if gr == 0 else []), (T.nst[:, :], [("nst", 0, 144, 1)]))
+        for j, (k, i, n, src) in enumerate(u for u in runs if u[0] == 2):
+            dma("ys"[(3 * gr + j) % 2], "lnb", (T.nb2[16 * gr + i:16 * gr + i + n, 0:46], [("nb2", 0, 48, 1)] if gr + i == 0 else []), (src, []))
+    dma("y", "lx", R("xt"), (T.x[:, :], []))
+    for k, i, n, src in runs:
+        if k < 2:
+            dma("s", "lst", (T.nst[i:i + n, 46 * k:46 * k + 46], [("nst", 0, 92, 1)] if i + k == 0 else []), (src, []))
+    for gr in range(8):
+        dma("y", "lnn", (T.nn[16 * gr:16 * gr + 16, :], [("nn", 0, 92, 1)] if gr == 0 else []), (T.nst[:, :], [("nst", 0, 92, 1)]))
     dma("y", "lw", R("wt"), (T.w[:, :], []))
+    n2 = R("nb2", 0, 46, 3)
+    nl = [R("nn", 46 * k, 46 * k + 46, 3) for k in range(2)] + [n2]
 
     iota(R("pp", 0, 1), [[0, 1]], 0, 1)
-    iota(R("n48"), [[1, 48]], 1, 0)
     iota(R("tk"), [[1, 16]], 0, 0)
-    iota(R("rowa"), [[0, 16], [1, 16]], 0, 0)
-    iota(R("row16"), [[16, 16], [0, 16]], 0, 0)
+    iota(R("iob"), [[1, 256]], 0, 0)
     iota(R("tb"), [[32, 8], [0, 2]], 0, 0)
-    iota(R("k3"), [[0, 48], [1, 3]], 0, 0)
+    iota(R("k3"), [[0, 16], [1, 3]], 0, 0)
+    iota(R("cf"), [[128, 2]], 0, 1)
     iota(R("j64"), [[0, 4], [1, 16]], 0, 0)
     iota(R("g48"), [[0, 6], [1, 8]], 0, 0)
     iota(R("cmp"), [[1, 128]], 0, -1)
     iota(R("tk32"), [[0, 2], [1, 16]], 0, 0)
     iota(R("d8"), [[0, 2], [1, 4]], 0, 0)
     iota(R("io32"), [[1, 32]], 0, 0)
-    iota(R("iob"), [[1, 256]], 0, 0)
+    iota(R("ones"), [[0, 256]], 1, 0)
     iota(R("rowb"), [[0, 16], [1, 16]], 0, 0)
+    iota(R("u0"), [[0, 512]], 0, 0)
+    iota(R("u1"), [[0, 512]], 0, 0)
     fill(R("zt", 0, 1152), 0.0)
-    fill(R("zt", 1152, NK), 0.0)
-    act(R("et"), R("zt", 0, 2048))
-    act(R("u0"), R("et", 0, 512))
-    act(R("u1"), R("et", 512, 1024))
-    fill(R("ones"), 1.0)
+    act(R("zt", 1152, NK), R("zt", 0, 1152))
+    for b in range(4):
+        act(R("et", 512 * b, 512 * b + 512), R("zt", 512 * (b % 2), 512 * (b % 2) + 512))
 
     def c(k):
         return R("ci", k, k + 1)
@@ -271,45 +276,29 @@ def program(g, core, T, topo):
     ts(c(0), R("pp", 0, 1), 15, OP.bitwise_and)
     ts(c(1), R("pp", 0, 1), 4, OP.arith_shift_right)
     ts(c(2), R("pp", 0, 1), 5, OP.arith_shift_right)
-    ts(c(8), c(0), 11, OP.mult, 10, OP.add)
-    for k in range(3):
-        ts(c(9 + k), c(0), 3, OP.mult, k, OP.add)
-    ts(c(3), c(1), 1, OP.bitwise_and)
-    ts(c(4), c(8), 15, OP.bitwise_and)
-    ts(R("ci", 5, 8), R("ci", 9, 12), 4, OP.arith_shift_right)
-    ts(c(12), c(11), 15, OP.bitwise_and)
-    cp(R("col", 0, 13), R("ci", 0, 13))
-    ts(R("ma"), R("n48"), col(0), OP.add)
-    ts(R("mb"), R("ma"), 43, OP.mult)
-    ts(R("mc"), R("mb"), 7, OP.arith_shift_right)
-    ts(R("mb"), R("mc"), 3, OP.mult)
-    tt(R("m48"), R("ma"), R("mb"), OP.is_equal)
-    ts(R("jl"), R("tk"), 16.0, OP.mult, col(4), OP.add)
-    ts(R("gl"), R("jl"), 256.0 * r, OP.add)
-    ts(col2(0), col(3), -1.0, OP.mult, 1.0, OP.add)
-    ts(col2(1), col(3), 16.0, OP.mult, col(0), OP.add)
-    ts(col2(3), col(1), 8.0, OP.add)
-    ts(col2(4), col(0), 2.0, OP.mult)
-    ts(col2(5), col(0), 2.0, OP.mult, 1.0, OP.add)
-    ts(R("va"), R("rowa"), 11, OP.mult, 10, OP.add)
-    ts(R("vb"), R("va"), 15, OP.bitwise_and)
-    tt(R("vrow"), R("vb"), R("row16"), OP.add)
+    ts(c(3), R("pp", 0, 1), 4, OP.arith_shift_right, 1, OP.bitwise_and)
+    cp(R("col"), R("ci"))
+    act(R("jl"), R("tk"), AF.Identity, bias=col(0), scale=16.0)
+    act(R("gl"), R("jl"), AF.Copy, bias=256.0 * r)
+    act(col2(0), col(3), AF.Copy, bias=1.0, scale=-1.0)
+    act(col2(1), col(3), AF.Identity, bias=col(0), scale=16.0)
+    act(col2(3), col(1), AF.Copy, bias=8.0)
+    act(col2(4), col(0), AF.Copy, scale=2.0)
+    act(col2(5), col(0), AF.Copy, bias=1.0, scale=2.0)
     ts(R("dup", 0, 16), R("tb"), col2(1), OP.add)
-    ts(R("dupc"), R("tk"), 16.0, OP.mult, col(12), OP.add)
+    cp(R("cc"), R("cf"))
 
-    tt(R("nf"), R("nb2"), R("m48"), OP.mult)
-    tt(R("ns"), R("nf", 0, 48, 3), R("nf", 1, 48, 3), OP.add)
-    tt(R("n2"), R("ns"), R("nf", 2, 48, 3), OP.add)
-    ts(R("ka"), R("n2"), 256 * r, OP.bitwise_and)
-    ts(R("ki"), R("n2"), 255, OP.bitwise_and)
-    tt(R("klow"), R("n2"), R("gl"), OP.is_gt)
-    ts(R("kt"), R("n2"), 256.0 * (r + 1), OP.is_lt, -256.0, OP.mult)
+    ts(R("ka"), n2, 256 * r, OP.bitwise_and)
+    ts(R("kh"), n2, 1792, OP.bitwise_and)
+    tt(R("km"), n2, R("gl"), OP.min)
+    tt(R("klow"), n2, R("gl"), OP.is_gt)
+    ts(R("kt"), n2, 256.0 * (r + 1), OP.is_lt, -256.0, OP.mult)
     ts(R("kb"), R("ka"), -2.0, OP.mult, 256.0 * r + 256.0, OP.add)
-    tt(R("kj"), R("jl"), R("ki"), OP.subtract)
-    tt(R("ky"), R("kb"), R("n2"), OP.add)
-    tt(R("kb"), R("kj"), R("kt"), OP.add)
-    tt(R("kj"), R("kb"), R("klow"), OP.mult)
-    tt(R("kf"), R("ky"), R("kj"), OP.add)
+    ts(R("ki"), R("km"), 255, OP.bitwise_and)
+    tt(R("kl"), R("kt"), R("klow"), OP.mult)
+    tt(R("k1"), R("kb"), R("kh"), OP.add)
+    tt(R("k2"), R("ki"), R("kl"), OP.add)
+    tt(R("kf"), R("k1"), R("k2"), OP.add)
     cp(R("ku"), R("kf"))
     cp(ind(R("zt"), R("ku")), R("ones"))
     act(R("kd", 0, 8), R("kf", 0, 16, 2), AF.Copy, scale=col2(0))
@@ -319,11 +308,10 @@ def program(g, core, T, topo):
     cp(R("kdu", 0, 16, 2), R("kd", 16, 24))
     cp(R("kdu", 1, 16, 2), R("kd", 16, 24))
     cp(R("pg"), ind(R("cs"), R("kdu")))
-    act(R("pos"), ind(R("cs"), R("ku")))
-    act(R("posn"), ind(R("pos"), R("dupc")))
+    act(R("posn"), ind(R("cs"), R("ku")), AF.Copy, bias=-1.0)
     tr(R("pt"), R("pg"))
     ts(R("plu"), R("pt", 0, 256, 16), -1.0, OP.add)
-    cp(ind(R("ir"), R("plu")), R("vrow"))
+    cp(ind(R("ir"), R("plu")), R("iob"))
     cp(R("ig"), ind(R("ir"), R("dup", 0, 16)))
     qz(R("q0c"), R("q0s"), R("xt"))
     tr(R("it"), R("ig"))
@@ -372,7 +360,7 @@ def program(g, core, T, topo):
         for h in range(2):
             mm(bank(h, 256), R(bc, 128 * h, 128 * h + 128), R(bs, 128 * h, 128 * h + 128), R(bc, 0, 256), R(bs, 0, 256))
         cp(R("gs", 0, 256), bank(0, 256))
-        act(R("gs", 256, 512), bank(1, 256))
+        act(R("gs", 264, 520), bank(1, 256))
 
     BK = [[4, 5, 6, 7], [0, 1, 2, 3]]
 
@@ -380,19 +368,23 @@ def program(g, core, T, topo):
         mm(bank(BK[h][b], 128), R("eqc", 128 * b, 128 * b + 128), R("eqs", 128 * b, 128 * b + 128),
            R(cc, 128 * h, 128 * h + 128), R(cs, 128 * h, 128 * h + 128), start, not start)
 
+    def diagonal(o, i, off):
+        tt(R("xg"), ind(i, off), R("dm"), OP.mult)
+        scan(o, R("rs16"), R("xg"), OP.mult, OP.add)
+
+    sent, chosen, picked = [], [], []
+
     def local_scores(t):
         for h in range(2):
-            cp(R("gg", 32 * h, 32 * h + 32), ind(R("gs", 256 * h, 256 * h + 256), R("xo", 2 * h, 2 * h + 2)))
-        tt(R("gg", 64, 128), R("gg", 0, 64), R("dm"), OP.mult)
-        scan(R("sc"), R("rs16"), R("gg", 64, 128), OP.mult, OP.add)
+            tt(R("gg", 32 * h, 32 * h + 32), ind(R("gs", 264 * h, 264 * h + 264), R("xoa" if t else "xo", 2 * h, 2 * h + 2)), R("dm", 0, 32), OP.mult)
+        scan(R("sc"), R("rs16"), R("gg"), OP.mult, OP.add)
         s0, s1 = R("sc", 15, 64, 32), R("sc", 31, 64, 32)
-        if t == 1:
-            for k in range(2):
-                tt(R("sm", 32 + k, 36, 2), R("sc", 15 + 16 * k, 64, 32), R("pen", 2 * k, 2 * k + 2), OP.add)
-            s0, s1 = R("sm", 32, 36, 2), R("sm", 33, 36, 2)
-        m = "m%d" % t
+        m, ma = "m%d" % t, "ma%d" % t
+        for h in range(2):
+            ts(R(ma, 4 * h, 4 * h + 4), R("msk", 4 * h, 4 * h + 4), R("sc", 15 + 32 * h, 16 + 32 * h), OP.max, R("sc", 31 + 32 * h, 32 + 32 * h), OP.max)
+        sent.append(len(ops))
+        send(lambda d: T[ma][:, d:d + 1], lambda d: T["mx%d" % t][:, d:d + 1], "e%d" % t, [(ma, 0, 8)])
         tt(R(m), s0, s1, OP.max)
-        send(lambda d: T[m][:, d // 4:d // 4 + 1], lambda d: T["mx%d" % t][:, d:d + 1], "e%d" % t, [(m, 0, 2)])
         tt(R("sm", 0, 2), s0, s1, OP.is_ge)
         act(R("sm", 2, 4), R("sm", 0, 2), AF.Copy, bias=-4e29, scale=4e29)
         act(R("sm", 4, 6), R("sm", 0, 2), AF.Copy, scale=-4e29)
@@ -400,21 +392,24 @@ def program(g, core, T, topo):
         tt(R("sm", 9, 12, 2), s1, R("sm", 4, 6), OP.add)
         ts(R("lm", 0, 32), R("p32"), R(m, 0, 1, 1, 32), OP.mult)
         tr(R("lm", 32, 64), R("lm", 0, 32))
-        red(R("mm", 0, 1, 1, 32), R("lm", 32, 64))
-
-    def biased(t):
-        for h in range(2):
+        red(R("lmm", 0, 1, 1, 32), R("lm", 32, 64))
+        if t == 1:
             for k in range(2):
-                a = 64 * h + 32 * k
-                act(R("mq", a, a + 32), R("mn", 128 * t + a, 128 * t + a + 32), AF.Identity, bias=R("sm", 8 + 2 * h + k, 9 + 2 * h + k))
+                tt(R("sm", 8 + k, 12, 2), R("sm", 8 + k, 12, 2), R("pen", 4, 6), OP.add)
+            tt(R(m), R(m), R("pen", 4, 6), OP.add)
 
     def statics(t, hi_own, hl):
         for h in range(2):
             a = 128 * t + 64 * h
-            ts(R("mn", a, a + 64, 2), R("tk32"), hi_own[h], OP.not_equal, -8e29, OP.mult)
+            act(R("mn", a, a + 64, 2), R("tk32"), AF.Square, bias=hi_own[h], scale=-1.0)
             for k in range(2):
-                ts(R("mn", a + 32 * k + 1, a + 32 * k + 32, 2), R("tk"), R("hl", hl + 2 * h + k, hl + 2 * h + k + 1), OP.not_equal, -8e29, OP.mult)
-            ts(R("nat", 32 * t + 16 * h, 32 * t + 16 * h + 16), R("tk"), hi_own[h], OP.is_equal, 2.0, OP.mult)
+                act(R("mn", a + 32 * k + 1, a + 32 * k + 32, 2), R("tk"), AF.Square, bias=R("hl", hl + 2 * h + k, hl + 2 * h + k + 1), scale=-1.0)
+            act(R("nat", 32 * t + 16 * h, 32 * t + 16 * h + 16), R("mn", a, a + 32, 2), AF.Relu, bias=2.0, scale=-2.0)
+        for h in range(2):
+            for k in range(2):
+                a = 64 * h + 32 * k
+                act(R("mq", a, a + 32), R("mn", 128 * t + a, 128 * t + a + 32), AF.Identity,
+                    bias=R("sm", 8 + 2 * h + k, 9 + 2 * h + k), scale=-8e29)
 
     def weights(t, lo_own, hl):
         for h in range(2):
@@ -425,43 +420,36 @@ def program(g, core, T, topo):
         qz(R("cqc", 256 * t, 256 * t + 256), R("cqs", 256 * t, 256 * t + 256), R("ct", 1024 * t, 1024 * t + 1024))
 
     def choose(t, bc, bs):
-        u, uq, m = "u%d" % t, 128 * t, "m%d" % t
+        u, uq, m, mx = "u%d" % t, 128 * t, "m%d" % t, "mx%d" % t
         arrive("a%d" % t, bc, 288, 512)
         arrive("a%d" % t, bs, 288, 512)
         for h in range(2):
             mm(bank(2 + h, 128), R(bc, 128 * h, 128 * h + 128), R(bs, 128 * h, 128 * h + 128),
                R(bc, 256 + 128 * h, 384 + 128 * h), R(bs, 256 + 128 * h, 384 + 128 * h))
-        arrive("e%d" % t, "mx%d" % t, 0, 8)
-        tt(R("mm", 1, 8), R("mx%d" % t, 1, 8), R("msk", 1, 8), OP.mult)
-        red(R("mm", 8, 9), R("mm", 0, 4))
-        red(R("mm", 9, 10), R("mm", 4, 8))
+        arrive("e%d" % t, mx, 0, 8)
         for h in range(2):
             tt(R("xd", 128 * h, 128 * h + 128), bank(2 + h, 128), R("idn"), OP.mult)
         act(R("jk", 0, 128), R("xd", 0, 128), AF.Identity, accum=R("sm", 16, 17))
         red(R("sm", 17, 18), R("xd", 128, 256))
-        s2 = 16
-        if t == 1:
-            tt(R("sm", 18, 20), R("sm", 16, 18), R("pen", 4, 6), OP.add)
-            s2 = 18
+        for a, b, i in ((0, 1, R("lmm")), (1, 4, R(mx, 1, 4)), (4, 8, R(mx, 4, 8))):
+            ts(R("ofx", a, b), i, R("sm", 16 + a // 4, 17 + a // 4), OP.is_lt, col2(4), OP.add)
         for h in range(2):
-            ts(R("ofx", 2 * h, 2 * h + 1), R("sm", s2 + h, s2 + h + 1), R("mm", 8 + h, 9 + h), OP.is_gt, col2(4), OP.add)
+            act(R("jk", 128 + 64 * h, 192 + 64 * h), ind(R("dw"), R("ofx", 4 * h, 4 * h + 4)), AF.Copy, accum=R("sm", 20 + h, 21 + h))
+        tt(R("sm", 22, 24), R("sm", 16, 18), R(m), OP.is_gt)
         for h in range(2):
-            act(R("jk", 128 + 16 * h, 144 + 16 * h), ind(R("dw"), R("ofx", 2 * h, 2 * h + 1)), AF.Copy, accum=R("sm", 20 + h, 21 + h))
-        tt(R("sm", 22, 24), R("sm", s2, s2 + 2), R(m), OP.is_gt)
-        for h in range(2):
-            ts(R(u, h, 128, 2), R("mq", 64 * h, 64 * h + 64), R("sm", s2 + h, s2 + h + 1), OP.is_ge)
+            ts(R(u, h, 128, 2), R("mq", 64 * h, 64 * h + 64), R("sm", 16 + h, 17 + h), OP.is_ge)
         for h in range(2):
             ts(R(u, 128 + h, 192, 4), R("nat", 32 * t + 16 * h, 32 * t + 16 * h + 16), R("sm", 20 + h, 21 + h), OP.mult, R("sm", 22 + h, 23 + h), OP.mult)
         qz(R("uqc", uq, uq + 128), R("uqs", uq, uq + 128), R(u))
         for k in range(2):
             ca = 256 * t + 128 * k
             mm(bank(2 + k, 128), R("cqc", ca, ca + 128), R("cqs", ca, ca + 128), R("uqc", uq, uq + 128), R("uqs", uq, uq + 128))
-        z, xl, off = 80 * t, "xl%d" % t, 16 * t
-        tt(R("z", z, z + 16), R("bk2", 0, 16), R(xl, 0, 16), OP.add)
-        tt(R("z", z + 16, z + 48), R("bk3", 16, 48), R(xl, 16, 48), OP.add)
-        tt(R("z", z + 48, z + 64), R("z", z, z + 16), R("z", z + 16, z + 32), OP.max)
-        tt(R("z", z + 64, z + 80), R("z", z + 48, z + 64), R("z", z + 32, z + 48), OP.max)
-        ts(R("lp", off, off + 16), R("z", z + 64, z + 80), -2 * BIG - 1.0, OP.add)
+        z, xl, off = 96 * t, "xl%d" % t, 16 * t
+        for k in range(3):
+            tt(R("z", z + k, z + 48, 3), R("bk%d" % (3 if k else 2), 16 * k, 16 * k + 16), R(xl, 16 * k, 16 * k + 16), OP.add)
+        scan(R("z", z + 48, z + 96), R("rs3"), R("z", z, z + 48), OP.mult, OP.max)
+        ts(R("lp", off, off + 16), R("z", z + 50, z + 96, 3), -2 * BIG, OP.add)
+        chosen.append(len(ops) - 1)
 
     def own_parts(cc, cs):
         for b in range(4):
@@ -476,9 +464,12 @@ def program(g, core, T, topo):
         for b in range(2, 4):
             dec(1, b, cc, cs, True)
         for h in range(2):
-            for b in range(4):
+            for b in (1, 3, 0, 2):
+                gate[0] = len(ops) - 1 if h + b != 1 else None
                 dec(h, b, pc, psn, False)
+        gate[0] = chosen[t]
         after_lists()
+        gate[0] = None
         for h in range(2):
             for b in range(4):
                 oo, ii = R("nt", 512 * h + b, 512 * h + 512, 4), bank(BK[h][b], 128)
@@ -493,39 +484,34 @@ def program(g, core, T, topo):
     send_w("b0c", "b0s", "a0")
     pick("b0c", "b0s", 256, 288, "q0c", "q0s", 0, 256, R("l18", 16, 18))
     gram("b0c", "b0s")
-    for k in range(3):
-        ts(R("mk", 48 * k, 48 * k + 48), R("k3", 0, 48), col(5 + k), OP.is_equal)
-    tt(R("nlf"), R("nn"), R("mk"), OP.mult)
-    tt(R("nl"), R("nlf", 0, 144, 3), R("nlf", 1, 144, 3), OP.add)
-    tt(R("nli", 0, 48), R("nl"), R("nlf", 2, 144, 3), OP.add)
-    ts(R("nli", 48, 80), R("nli", 0, 32), 255, OP.bitwise_and)
-    cp(R("o01"), R("nli", 48, 80))
-    act(R("xr"), ind(R("posn"), R("o01")))
+    for k in range(2):
+        ts(R("o01", 16 * k, 16 * k + 16), nl[k], -256.0 * r, OP.add)
+        act(R("xr", 256 * k, 256 * k + 256), ind(R("posn"), R("o01", 16 * k, 16 * k + 16)))
     ts(R("gm"), R("g48"), col(1), OP.is_equal)
     ts(R("rs8"), R("g48"), 0.0, OP.not_equal)
     ts(R("rs16"), R("j64"), 0.0, OP.not_equal)
+    ts(R("rs3"), R("k3"), 0.0, OP.not_equal)
     ts(R("dm"), R("j64"), col(0), OP.is_equal)
-    tt(R("iv", 0, 16), R("it", 0, 256, 16), R("gm", 0, 16), OP.mult)
-    scan(R("iv", 16, 32), R("rs8", 0, 16), R("iv", 0, 16), OP.mult, OP.add)
-    inv = R("iv", 23, 32, 8)
+    tt(R("iv", 0, 32), ind(R("ir"), R("cc")), R("dm", 0, 32), OP.mult)
+    scan(R("iv", 32, 64), R("rs16", 0, 32), R("iv", 0, 32), OP.mult, OP.add)
+    inv = R("iv", 47, 64, 16)
     cp(R("of4", 0, 4, 2), inv)
     ts(R("of4", 1, 4, 2), inv, 256.0, OP.add)
-    cp(R("xg", 0, 64), ind(R("xr"), R("of4")))
-    tt(R("xg", 64, 128), R("xg", 0, 64), R("dm"), OP.mult)
-    scan(R("xg", 128, 192), R("rs16"), R("xg", 64, 128), OP.mult, OP.add)
-    ts(R("xo"), R("xg", 143, 192, 16), -1.0, OP.add)
+    diagonal(R("xi", 0, 64), R("xr"), R("of4"))
+    cp(R("xo"), R("xi", 15, 64, 16))
     tt(R("p32a"), R("cmp", 0, 32, 1, 32), R("cmp", 0, 32, 1, 32), OP.mult)
     ts(R("p32"), R("p32a"), 256.0, OP.is_equal)
-    fill(R("mm"), 0.0)
+    fill(R("lmm"), 1e29)
+    for h in range(2):
+        fill(R("gs", 256 + 264 * h, 264 + 264 * h), -1e29)
+    ts(R("msk", 8, 16), R("d8"), col(2), OP.not_equal, 2e29, OP.mult)
+    ts(R("msk", 0, 8), R("msk", 8, 16), -1e29, OP.add)
     local_scores(0)
-    ts(R("xi", 0, 4), R("xg", 143, 192, 16), -1.0, OP.add)
-    ts(R("xi", 4, 8), R("xi", 0, 4), 4, OP.arith_shift_right)
-    ts(R("xi", 8, 12), R("xi", 0, 4), 15, OP.bitwise_and)
-    cp(R("hl", 0, 8), R("xi", 4, 12))
+    ts(R("xi", 128, 132), R("xi", 15, 64, 16), 4, OP.arith_shift_right)
+    ts(R("xi", 132, 136), R("xi", 15, 64, 16), 15, OP.bitwise_and)
+    cp(R("hl", 0, 8), R("xi", 128, 136))
     statics(0, [col(1), col2(3)], 0)
-    biased(0)
     ts(R("idn"), R("cmp"), 0.0, OP.is_equal)
-    ts(R("msk"), R("d8"), col(2), OP.is_equal)
     ts(R("dw"), R("io32"), col2(5), OP.is_equal)
     weights(0, [col(0), col(0)], 0)
     act(R("ld", 0, 8), R("it", 0, 256, 32), AF.Copy, scale=col2(0))
@@ -534,21 +520,20 @@ def program(g, core, T, topo):
     for k in range(2):
         for w in range(2):
             ts(R("ldu", 16 * k + w, 16 * k + 16, 2), R("ld", 16, 24), 256.0 * k, OP.add)
-    act(R("xlg"), ind(R("xr"), R("ldu")))
+    for k in range(2):
+        act(R("xlg", 256 * k, 256 * k + 256), ind(R("xr"), R("ldu", 16 * k, 16 * k + 16)))
     for b in range(4):
         act(R("et", b + 512 * b, 512 * b + 512, 4), R("idn"), AF.Copy, scale=0.5)
         qz(R("eqc", 128 * b, 128 * b + 128), R("eqs", 128 * b, 128 * b + 128), R("et", 512 * b, 512 * b + 512))
     tr(R("xlt"), R("xlg"))
     act(R("xl0", 0, 32), R("xlt", 0, 512, 16))
-    act(R("cl"), R("tk"), AF.Identity, bias=col(0), scale=16.0)
-    act(R("xl0", 32, 48), R("cl"), AF.Copy, bias=257.0)
+    act(R("xl0", 32, 48), R("jl"), AF.Copy, bias=256.0)
     own_parts("b0c", "b0s")
     choose(0, "b0c", "b0s")
-    picked = []
 
     def lists0():
-        ts(R("lnf", 0, 16), R("z", 64, 80), 2 * BIG, OP.is_ge, 512.0, OP.mult)
-        tt(R("lnf", 16, 32), R("lnf", 0, 16), R("cl"), OP.add)
+        ts(R("lnf", 0, 16), R("z", 50, 96, 3), 2 * BIG, OP.is_ge, 512.0, OP.mult)
+        tt(R("lnf", 16, 32), R("lnf", 0, 16), R("jl"), OP.add)
         cp(R("ln", 0, 16), R("lnf", 16, 32))
         cp(R("ln", 16, 17), R("lnf", 17, 18))
         cp(R("ln", 17, 18), R("lnf", 16, 17))
@@ -564,32 +549,38 @@ def program(g, core, T, topo):
     send_w("b1c", "b1s", "a1")
     pick("b1c", "b1s", 256, 288, "b0c", "b0s", 0, 640, R("ln", 16, 18))
     gram("b1c", "b1s")
-    ts(R("fl", 0, 48), R("z", 0, 48), 2 * BIG, OP.is_ge)
+    gate[0] = chosen[0]
+    for k in range(3):
+        ts(R("fl", 16 * k, 16 * k + 16), R("z", k, 48, 3), 2 * BIG, OP.is_ge)
     tt(R("fl", 48, 96), R("fl", 0, 48), R("gm"), OP.mult)
     scan(R("fl", 96, 144), R("rs8"), R("fl", 48, 96), OP.mult, OP.add)
-    ts(R("pen", 0, 6), R("fl", 103, 144, 8), -1e29, OP.mult)
+    for k in range(3):
+        act(R("pen", k, 4, 2) if k < 2 else R("pen", 4, 6), R("fl", 103 + 16 * k, 112 + 16 * k, 8), AF.Copy, scale=256.0 if k < 2 else 1e29)
+    tt(R("pen", 8, 12), R("pen", 0, 4), R("xi", 15, 64, 16), OP.max)
+    cp(R("xoa"), R("pen", 8, 12))
+    gate[0] = None
     local_scores(1)
-    gate[0] = picked[0]
-    ts(R("dup", 16, 32), R("tb"), col2(1), OP.add, 256.0, OP.add)
-    act(R("nr"), ind(R("iob"), R("o01")))
-    act(R("xng", 0, 512), ind(R("xr"), R("dup")))
+    gate[0] = chosen[0]
     act(R("xng", 512, 768), ind(R("posn"), R("dup", 0, 16)))
-    cp(R("xg", 0, 64), ind(R("nr"), R("of4")))
-    tt(R("xg", 64, 128), R("xg", 0, 64), R("dm"), OP.mult)
-    scan(R("xg", 128, 192), R("rs16"), R("xg", 64, 128), OP.mult, OP.add)
-    cp(R("xi", 12, 16), R("xg", 143, 192, 16))
-    cp(R("xi", 16, 18), inv)
-    ts(R("xi", 18, 24), R("xi", 12, 18), 4, OP.arith_shift_right)
-    ts(R("xi", 24, 30), R("xi", 12, 18), 15, OP.bitwise_and)
-    cp(R("hl", 8, 12), R("xi", 18, 22))
-    cp(R("hl", 12, 16), R("xi", 24, 28))
-    cp(R("hl", 16, 18), R("xi", 22, 24))
-    cp(R("hl", 18, 20), R("xi", 28, 30))
-    statics(1, [R("hl", 16, 17), R("hl", 17, 18)], 8)
-    biased(1)
-    tr(R("xnt"), R("xng"))
-    ts(R("pou"), R("xnt", 512, 768, 16), -1.0, OP.add)
+    tr(R("xnt", 512, 768), R("xng", 512, 768))
+    cp(R("pou"), R("xnt", 512, 768, 16))
     pick("fc", "fs", 0, 256, "b1c", "b1s", 0, 256, R("pou"))
+    own_parts("fc", "fs")
+    gate[0] = sent[0]
+    ts(R("dup", 16, 32), R("tb"), col2(1), OP.add, 256.0, OP.add)
+    for k in range(2):
+        act(R("nr", 256 * k, 256 * k + 256), ind(R("iob"), R("o01", 16 * k, 16 * k + 16)))
+        act(R("xng", 256 * k, 256 * k + 256), ind(R("xr"), R("dup", 16 * k, 16 * k + 16)))
+    diagonal(R("xi", 64, 128), R("nr"), R("of4"))
+    cp(R("xi", 136, 138), inv)
+    ts(R("xi", 144, 148), R("xi", 79, 128, 16), 4, OP.arith_shift_right)
+    ts(R("xi", 148, 152), R("xi", 79, 128, 16), 15, OP.bitwise_and)
+    ts(R("xi", 152, 154), R("xi", 136, 138), 4, OP.arith_shift_right)
+    ts(R("xi", 154, 156), R("xi", 136, 138), 15, OP.bitwise_and)
+    cp(R("hl", 8, 20), R("xi", 144, 156))
+    gate[0] = picked[0]
+    statics(1, [R("hl", 16, 17), R("hl", 17, 18)], 8)
+    tr(R("xnt", 0, 512), R("xng", 0, 512))
     act(R("xl1", 0, 32), R("xnt", 0, 512, 16))
     act(R("xl1", 32, 48), R("xnt", 512, 768, 16), AF.Copy, bias=256.0)
     weights(1, [R("hl", 18, 19), R("hl", 19, 20)], 8)
@@ -598,15 +589,14 @@ def program(g, core, T, topo):
             ts(R("u1", 192 + 64 * k + h, 256 + 64 * k, 4), R("nat", 32 + 16 * h, 48 + 16 * h), R("fl", 103 + 8 * (2 * k + h), 104 + 8 * (2 * k + h)), OP.mult)
     qz(R("qwc"), R("qws"), R("wt"))
     gate[0] = None
-    own_parts("fc", "fs")
     choose(1, "b1c", "b1s")
-    tt(R("zp", 0, 16), R("bk2", 0, 16), R("nli", 0, 16), OP.add)
-    tt(R("zp", 16, 48), R("bk3", 16, 48), R("nli", 16, 48), OP.add)
-    tt(R("zp", 48, 96), R("bk3", 48, 96), R("nli", 0, 48), OP.add)
+    gate[0] = chosen[1]
+    for k in range(6):
+        tt(R("zp", 16 * k, 16 * k + 16), R("bk%d" % (3 if k else 2), 16 * k, 16 * k + 16), nl[k % 3], OP.add)
 
     def lists1():
-        ts(R("lnf", 32, 48), R("z", 144, 160), 2 * BIG, OP.is_ge, 256.0, OP.mult)
-        tt(R("lnf", 48, 64), R("lnf", 32, 48), R("cl"), OP.add)
+        ts(R("lnf", 32, 48), R("z", 146, 192, 3), 2 * BIG, OP.is_ge, 256.0, OP.mult)
+        tt(R("lnf", 48, 64), R("lnf", 32, 48), R("jl"), OP.add)
         cp(R("ln", 20, 36), R("lnf", 48, 64))
         for t in range(2):
             a = 48 - 48 * t
@@ -625,6 +615,7 @@ def program(g, core, T, topo):
         pick("oqc", "oqs", a, b, "fc", "fs", 0, 384 + 128 * h, R("ln", 20 + 8 * h, 28 + 8 * h))
         dma("y", "st0", (T.oc[:, 4 * a:4 * b], []), W8(R("oqc", a, b)))
         mm(bank(4 + h, 128), R("qwc"), R("qws"), R("oqc", a, b), R("oqs", a, b))
+    gate[0] = None
     merge(1, "b1c", "b1s", "fc", "fs", 256, lists1, half1)
     for k in range(4):
         dma("s" if k % 2 else "y", "st0", (T.osc[4 * k:4 * k + 4, :], []), (T.oqs[32 * k:32 * k + 4, :], [("oqs", 0, 256, 1)]))

@@ -1,4 +1,5 @@
 import math
+import numpy as np
 from concourse.bass import DstId, RemoteDMATransfer
 from concourse.mybir import dt, AluOpType, AxisListType, ActivationFunctionType
 
@@ -6,17 +7,21 @@ OP = AluOpType
 AF = ActivationFunctionType
 NK = 2304
 BIG = 4096.0
+RND = 1.5 * 2.0 ** 27
 HOP = 0.14
 CY = 1.1e-3
+TRIES = 1500
+ORDERS = {}
 FP8, U8, F32, BF, I32, U16 = "float8_e4m3fn_x4", "uint8", "float32", "bfloat16", "int32", "uint16"
 
 SCRATCH = {"nst": ("dram", [16, 92], I32), "p32a": ("sbuf", [32, 32], F32), "p32": ("sbuf", [32, 32], F32),
            "lm": ("sbuf", [32, 64], F32)}
 for _t, _l in (
-        (F32, "tk 16 tk32 32 j64 64 g48 48 cmp 128 k3 48 tb 16 d8 8 io32 32 cf 2 col 4 col2 8 jl 16 gl 16 dm 64 rs16 64 rs8 48 rs3 48 "
-              "gm 48 idn 128 msk 16 dw 32 iv 64 xg 64 hl 20 ld 24 xl0 48 xl1 48 mn 256 gs 528 gg 64 sc 64 pen 16 sm 64 m0 2 m1 2 "
-              "ma0 8 ma1 8 mx0 8 mx1 8 lmm 1 mq 128 xd 256 jk 256 z 192 zp 160 fp 96 lnf 64 fl 144 ys 256"),
-        (BF, "xt 1024 wt 512 iob 256 rowb 256 ones 256 zt 2304 cs 2304 et 2048 pg 256 pt 256 ir 256 ig 256 it 256 "
+        (F32, "tk 16 tk32 32 j64 64 g48 48 cmp 128 k3 48 tb 16 d8 8 io32 32 col 4 col2 8 jl 16 gl 16 dm 64 rs16 64 rs8 48 rs3 48 "
+              "gm 48 idn 128 msk 16 dw 32 iv 32 xg 64 hl 20 ld 24 xl0 48 xl1 48 mn 256 gs 528 gg 64 sc 64 pen 16 sm 64 m0 2 m1 2 "
+              "ma0 8 ma1 8 mx0 8 mx1 8 lmm 1 mq 128 kcm 32 pcg 64 ph 4 nv 4 tkc 16 nlst 16 xd 256 jk 256 z 192 zp 160 fp 96 "
+              "lnf 64 fl 144 ys 256"),
+        (BF, "xt 1024 wt 512 iob 256 rowb 256 rowc 128 ones 256 zt 2304 cs 2304 et 2048 hf 512 pa 512 pm 512 "
              "posn 256 xr 512 nr 512 xlg 512 xlt 512 xng 768 xnt 768 nat 64 ct 2048 u0 512 u1 512 nt 1024"),
         (I32, "nb2 48 nn 92 xi 160")):
     _w = _l.split()
@@ -24,8 +29,8 @@ for _t, _l in (
         SCRATCH[_n] = ("sbuf", [128, int(_k)], _t)
 PIECE = {}
 for _b, _t, _l in (
-        ("uu", U16, "dup 32 ku 16 kdu 16 plu 16 l18 18 o01 32 of4 4 xo 4 xoa 4 ldu 32 pou 16 ofx 8 lp 32 ln 36 cc 2"),
-        ("kk", F32, "klow 16 kt 16 kb 16 kl 16 k1 16 k2 16 kf 16 kd 24"),
+        ("uu", U16, "dup 32 ku 16 l18 18 o01 32 of4 4 xo 4 xoa 4 ldu 32 pou 16 ofx 8 lp 32 ln 36 kcu 2"),
+        ("kk", F32, "klow 16 kt 16 kb 16 kl 16 k1 16 k2 16 kf 16"),
         ("kn", I32, "ka 16 kh 16 km 16 ki 16"),
         ("cn", I32, "pp 4 ci 4")):
     _w, _c = _l.split(), 0
@@ -33,14 +38,89 @@ for _b, _t, _l in (
         PIECE[_n] = (_b, _c, int(_k))
         _c += int(_k)
     SCRATCH[_b] = ("sbuf", [128, _c], _t)
-_w = "q0 256 qw 128 b0 768 b1 512 f 512 oq 256 eq 512 cq 512 uq 256 p0 256 p1 256".split()
+_w = "pa 128 pm 128 q0 256 qw 128 b0 768 b1 512 f 512 oq 256 eq 512 cq 512 uq 256 p0 256 p1 256".split()
 for _n, _k in zip(_w[0::2], _w[1::2]):
     SCRATCH[_n + "c"] = ("sbuf", [128, int(_k)], FP8)
     SCRATCH[_n + "s"] = ("sbuf", [128, int(_k)], U8)
 for _k in range(8):
     SCRATCH["bk%d" % _k] = ("psum", [128, 512], F32)
 
-SEMAPHORES = ["qv", "qs", "qt", "qp", "lnb", "lx", "lw", "lst", "lnn", "st0", "loc", "a0", "a1", "e0", "e1"]
+SEMAPHORES = ["qv", "qs", "qt", "qp", "lnb", "lx", "lx2", "lw", "lst", "lnn", "st0", "loc", "a0", "a1", "e0", "e1"]
+
+
+def list_schedule(ops, succ, prio, slack):
+    n = len(ops)
+    left = [len(o[2]) for o in ops]
+    ready, start = [0.0] * n, [0.0] * n
+    free = {q: 0.0 for q in "vstypa"}
+    cand = {q: [] for q in free}
+    for i in range(n):
+        if not left[i]:
+            cand[ops[i][0]].append(i)
+    for _ in range(n):
+        best = None
+        for q, l in cand.items():
+            if not l:
+                continue
+            f = 0.0 if q == "a" else free[q]
+            st = {i: f if f > ready[i] else ready[i] for i in l}
+            lo = min(st.values()) + 0.02
+            i = max((j for j in l if st[j] <= lo), key=lambda j: prio[j])
+            e, p = st[i] + ops[i][5] - slack, prio[i]
+            better = [j for j in l if prio[j] > p and st[j] < e]
+            if better:
+                i = max(better, key=lambda j: prio[j])
+            if best is None or st[i] < best[0]:
+                best = (st[i], q, i)
+        t, q, i = best
+        cand[q].remove(i)
+        start[i] = t
+        free[q] = t + ops[i][5]
+        for j in succ[i]:
+            left[j] -= 1
+            ready[j] = max(ready[j], t + ops[i][6] + HOP)
+            if not left[j]:
+                cand[ops[j][0]].append(j)
+    return start
+
+
+def span(ops, seq, hop, comp, far):
+    fin, free, end = [0.0] * len(ops), {q: 0.0 for q in "vstypa"}, 0.0
+    for i in seq:
+        q, deps, dur, lat = ops[i][0], ops[i][2], ops[i][5], ops[i][6]
+        t = 0.0 if q == "a" else free[q]
+        for d in deps:
+            if fin[d] + hop > t:
+                t = fin[d] + hop
+        free[q] = t + (dur * comp if q in "vst" and lat == dur else dur)
+        fin[i] = t + (lat * far if lat > 1.0 else lat * comp)
+        end = max(end, fin[i])
+    return end
+
+
+def search(ops):
+    n = len(ops)
+    succ, prio = [[] for _ in ops], [0.0] * n
+    for i, o in enumerate(ops):
+        for d in o[2]:
+            succ[d].append(i)
+    for i in range(n - 1, -1, -1):
+        prio[i] = ops[i][6] + max([prio[j] + HOP for j in succ[i]] or [0.0])
+    rng = np.random.default_rng(5)
+    best = None
+    for k in range(TRIES):
+        p = list(prio)
+        for _ in range(int(rng.integers(1, 13)) if k else 0):
+            p[int(rng.integers(n))] += float(rng.normal()) * (0.1, 0.5, 2.0)[int(rng.integers(3))]
+        start = list_schedule(ops, succ, p, 0.05 * (k % 2))
+        e = max(start[i] + ops[i][6] for i in range(n))
+        if best is not None and e > best[2]:
+            continue
+        seq = sorted(range(n), key=lambda i: (start[i], i))
+        e2 = 2 * e + span(ops, seq, 0.08, 0.9, 0.85) + span(ops, seq, 0.22, 1.2, 1.2)
+        if best is None or e2 <= best[0]:
+            best, prio = (e2, start, e + 0.1), p
+    return best[1]
 
 
 def program(g, core, T, topo):
@@ -50,7 +130,6 @@ def program(g, core, T, topo):
     known = {k: {} for k in Q}
     acc = {}
     ops = []
-    gate = [None]
     group = {}
 
     def meet(a, b):
@@ -63,7 +142,7 @@ def program(g, core, T, topo):
                 for a in acc.get(b, []):
                     if (w or a[3]) and meet((lo, hi, st), a):
                         deps.update(group.get(ops[a[4]][3], [a[4]]))
-        ops.append([q, fn, sorted(deps), sem, n, dur, dur if lat is None else lat, gate[0]])
+        ops.append([q, fn, sorted(deps), sem, n, dur, dur if lat is None else lat])
         if n != 1:
             group.setdefault(sem, []).append(me)
         for w, regs in ((False, reads), (True, writes)):
@@ -75,40 +154,10 @@ def program(g, core, T, topo):
         return me
 
     def order():
-        n = len(ops)
-        succ, left, prio = [[] for _ in ops], [len(o[2]) + (o[7] is not None) for o in ops], [0.0] * n
-        for i, o in enumerate(ops):
-            for d in o[2] + ([] if o[7] is None else [o[7]]):
-                succ[d].append(i)
-        for i in range(n - 1, -1, -1):
-            prio[i] = ops[i][6] + max([prio[j] + HOP for j in succ[i]] or [0.0])
-        ready, free, start = [0.0] * n, {q: 0.0 for q in "vstypa"}, [0.0] * n
-        cand = {q: [] for q in free}
-        for i in range(n):
-            if not left[i]:
-                cand[ops[i][0]].append(i)
-        for _ in range(n):
-            best = None
-            for q, l in cand.items():
-                if not l:
-                    continue
-                st = {i: max(0.0 if q == "a" else free[q], ready[i]) for i in l}
-                lo = min(st.values())
-                i = max((j for j in l if st[j] <= lo + 0.02), key=lambda j: prio[j])
-                better = [j for j in l if prio[j] > prio[i] and st[j] < st[i] + ops[i][5] - 0.05]
-                if better:
-                    i = max(better, key=lambda j: prio[j])
-                if best is None or st[i] < best[0]:
-                    best = (st[i], q, i)
-            t, q, i = best
-            cand[q].remove(i)
-            start[i] = t
-            free[q] = t + ops[i][5]
-            for j in succ[i]:
-                left[j] -= 1
-                ready[j] = max(ready[j], t + ops[i][6] + (HOP if i in ops[j][2] else 0.0))
-                if not left[j]:
-                    cand[ops[j][0]].append(j)
+        key = tuple((o[0], tuple(o[2]), o[5], o[6]) for o in ops)
+        if key not in ORDERS:
+            ORDERS[key] = search(ops)
+        start, n = ORDERS[key], len(ops)
         return sorted(range(n), key=lambda i: (start[i], i))
 
     def emit():
@@ -220,6 +269,9 @@ def program(g, core, T, topo):
     def iota(o, pat, base, cm):
         issue("p", lambda: g.iota(o[0], pat, base, cm, allow_small_or_imprecise_dtypes=True), [], o[1], "qp", 1, 0.13 + us(width(o), 2))
 
+    def one(o, i, b):
+        issue("p", lambda: g.affine_select(o[0], i[0], [[-1, 512]], OP.is_equal, 0.0, b, 4), i[1], o[1], "qp", 1, 0.17 + us(width(o), 2))
+
     def dma(q, sem, out, i):
         issue(q, lambda: Q[q].dma_start(out[0], i[0]), i[1], out[1], sem, 16, 0.07, 2.5)
 
@@ -235,6 +287,7 @@ def program(g, core, T, topo):
         for j, (k, i, n, src) in enumerate(u for u in runs if u[0] == 2):
             dma("ys"[(3 * gr + j) % 2], "lnb", (T.nb2[16 * gr + i:16 * gr + i + n, 0:46], [("nb2", 0, 48, 1)] if gr + i == 0 else []), (src, []))
     dma("y", "lx", R("xt"), (T.x[:, :], []))
+    dma("y", "lx2", R("pm", 64, 512), (T.x[:, 0:448], []))
     for k, i, n, src in runs:
         if k < 2:
             dma("s", "lst", (T.nst[i:i + n, 46 * k:46 * k + 46], [("nst", 0, 92, 1)] if i + k == 0 else []), (src, []))
@@ -249,7 +302,7 @@ def program(g, core, T, topo):
     iota(R("iob"), [[1, 256]], 0, 0)
     iota(R("tb"), [[32, 8], [0, 2]], 0, 0)
     iota(R("k3"), [[0, 16], [1, 3]], 0, 0)
-    iota(R("cf"), [[128, 2]], 0, 1)
+    iota(R("rowc"), [[0, 8], [1, 16]], 1, 0)
     iota(R("j64"), [[0, 4], [1, 16]], 0, 0)
     iota(R("g48"), [[0, 6], [1, 8]], 0, 0)
     iota(R("cmp"), [[1, 128]], 0, -1)
@@ -258,12 +311,11 @@ def program(g, core, T, topo):
     iota(R("io32"), [[1, 32]], 0, 0)
     iota(R("ones"), [[0, 256]], 1, 0)
     iota(R("rowb"), [[0, 16], [1, 16]], 0, 0)
-    iota(R("u0"), [[0, 512]], 0, 0)
-    iota(R("u1"), [[0, 512]], 0, 0)
     fill(R("zt", 0, 1152), 0.0)
-    act(R("zt", 1152, NK), R("zt", 0, 1152))
-    for b in range(4):
-        act(R("et", 512 * b, 512 * b + 512), R("zt", 512 * (b % 2), 512 * (b % 2) + 512))
+    fill(R("zt", 1152, NK), 0.0)
+    fill(R("hf"), 0.5)
+    act(R("u0"), R("hf"), AF.Copy, scale=0.0)
+    act(R("u1"), R("hf"), AF.Copy, scale=0.0)
 
     def c(k):
         return R("ci", k, k + 1)
@@ -286,7 +338,14 @@ def program(g, core, T, topo):
     act(col2(4), col(0), AF.Copy, scale=2.0)
     act(col2(5), col(0), AF.Copy, bias=1.0, scale=2.0)
     ts(R("dup", 0, 16), R("tb"), col2(1), OP.add)
-    cp(R("cc"), R("cf"))
+    ts(R("tkc"), R("tk"), 16.0, OP.mult, RND, OP.add)
+    for h in range(2):
+        act(R("nv", 2 * h, 2 * h + 1), col(1), AF.Copy, bias=128.0 * h, scale=16.0)
+        act(R("nv", 2 * h + 1, 2 * h + 2), col(0), AF.Copy)
+    ts(R("gm"), R("g48"), col(1), OP.is_equal)
+    ts(R("rs8"), R("g48"), 0.0, OP.not_equal)
+    ts(R("rs16"), R("j64"), 0.0, OP.not_equal)
+    ts(R("dm"), R("j64"), col(0), OP.is_equal)
 
     ts(R("ka"), n2, 256 * r, OP.bitwise_and)
     ts(R("kh"), n2, 1792, OP.bitwise_and)
@@ -301,23 +360,27 @@ def program(g, core, T, topo):
     tt(R("kf"), R("k1"), R("k2"), OP.add)
     cp(R("ku"), R("kf"))
     cp(ind(R("zt"), R("ku")), R("ones"))
-    act(R("kd", 0, 8), R("kf", 0, 16, 2), AF.Copy, scale=col2(0))
-    act(R("kd", 8, 16), R("kf", 1, 16, 2), AF.Copy, scale=col(3))
+    tt(R("kcm", 0, 16), R("kf"), R("gm", 0, 16), OP.mult)
+    scan(R("kcm", 16, 32), R("rs8", 0, 16), R("kcm", 0, 16), OP.mult, OP.add)
+    cp(R("kcu"), R("kcm", 23, 32, 8))
     scan(R("cs"), R("zt"), R("zt"), OP.add, OP.max)
-    tt(R("kd", 16, 24), R("kd", 0, 8), R("kd", 8, 16), OP.add)
-    cp(R("kdu", 0, 16, 2), R("kd", 16, 24))
-    cp(R("kdu", 1, 16, 2), R("kd", 16, 24))
-    cp(R("pg"), ind(R("cs"), R("kdu")))
+    tt(R("pcg", 0, 32), ind(R("cs"), R("kcu")), R("dm", 0, 32), OP.mult)
+    scan(R("pcg", 32, 64), R("rs16", 0, 32), R("pcg", 0, 32), OP.mult, OP.add)
     act(R("posn"), ind(R("cs"), R("ku")), AF.Copy, bias=-1.0)
-    tr(R("pt"), R("pg"))
-    ts(R("plu"), R("pt", 0, 256, 16), -1.0, OP.add)
-    cp(ind(R("ir"), R("plu")), R("iob"))
-    cp(R("ig"), ind(R("ir"), R("dup", 0, 16)))
+    ts(R("ph", 0, 2), R("pcg", 47, 64, 16), -8.5, OP.add, RND, OP.add)
+    ts(R("ph", 2, 4), R("ph", 0, 2), -RND, OP.add)
+    for e in range(4):
+        ts(R("pm", e, 64, 4), R("tkc"), R("ph", e // 2, e // 2 + 1), OP.is_equal, R("nv", e, e + 1), OP.mult)
+    qz(R("pmc"), R("pms"), R("pm"))
+    for e in range(4):
+        ts(R("pa", e, 512, 4), R("rowc"), R("ph", 2 + e // 2, 3 + e // 2), OP.add, R("pcg", 47 + 16 * (e // 2), 48 + 16 * (e // 2)), OP.is_equal)
+    qz(R("pac"), R("pas"), R("pa"))
+    mm(R("bk6", 0, 128), R("pac"), R("pas"), R("pmc"), R("pms"))
+    cp(R("l18", 0, 16), R("bk6", 0, 16))
+    cp(R("nlst"), R("bk6", 0, 16))
+    cp(R("l18", 16, 17), R("nlst", 1, 2))
+    cp(R("l18", 17, 18), R("nlst", 0, 1))
     qz(R("q0c"), R("q0s"), R("xt"))
-    tr(R("it"), R("ig"))
-    cp(R("l18", 0, 16), R("it", 0, 256, 16))
-    cp(R("l18", 16, 17), R("it", 16, 17))
-    cp(R("l18", 17, 18), R("it", 0, 1))
 
     def pick(dc, ds, a, b, sc, ss, w0, w1, off):
         cp(W32(R(dc, a, b)), ind(W32(R(sc, w0, w1)), off))
@@ -343,7 +406,7 @@ def program(g, core, T, topo):
             cnt["loc"] = cnt.get("loc", 0) + 14
         me = issue("p", call, [(b, lo, hi, 1) for b, lo, hi in regs], [], None, 1, 0.7, 0.7)
         group.setdefault(sem, []).append(len(ops))
-        ops.append(["a", None, [me], sem, 14, 0.0, 2.5, None])
+        ops.append(["a", None, [me], sem, 14, 0.0, 2.5])
 
     def arrive(sem, b, lo, hi):
         acc.setdefault(b, []).append((lo, hi, 1, True, group[sem][0]))
@@ -357,10 +420,12 @@ def program(g, core, T, topo):
         return R("bk%d" % k, 0, n)
 
     def gram(bc, bs):
-        for h in range(2):
-            mm(bank(h, 256), R(bc, 128 * h, 128 * h + 128), R(bs, 128 * h, 128 * h + 128), R(bc, 0, 256), R(bs, 0, 256))
-        cp(R("gs", 0, 256), bank(0, 256))
-        act(R("gs", 264, 520), bank(1, 256))
+        mm(bank(0, 256), R(bc, 0, 128), R(bs, 0, 128), R(bc, 0, 256), R(bs, 0, 256))
+        for k, j in enumerate((1, 3)):
+            mm(bank(j, 128), R(bc, 128, 256), R(bs, 128, 256), R(bc, 128 * k, 128 * k + 128), R(bs, 128 * k, 128 * k + 128))
+        act(R("gs", 0, 256), bank(0, 256))
+        cp(R("gs", 264, 392), bank(1, 128))
+        cp(R("gs", 392, 520), bank(3, 128))
 
     BK = [[4, 5, 6, 7], [0, 1, 2, 3]]
 
@@ -372,8 +437,6 @@ def program(g, core, T, topo):
         tt(R("xg"), ind(i, off), R("dm"), OP.mult)
         scan(o, R("rs16"), R("xg"), OP.mult, OP.add)
 
-    sent, chosen, picked = [], [], []
-
     def local_scores(t):
         for h in range(2):
             tt(R("gg", 32 * h, 32 * h + 32), ind(R("gs", 264 * h, 264 * h + 264), R("xoa" if t else "xo", 2 * h, 2 * h + 2)), R("dm", 0, 32), OP.mult)
@@ -382,7 +445,6 @@ def program(g, core, T, topo):
         m, ma = "m%d" % t, "ma%d" % t
         for h in range(2):
             ts(R(ma, 4 * h, 4 * h + 4), R("msk", 4 * h, 4 * h + 4), R("sc", 15 + 32 * h, 16 + 32 * h), OP.max, R("sc", 31 + 32 * h, 32 + 32 * h), OP.max)
-        sent.append(len(ops))
         send(lambda d: T[ma][:, d:d + 1], lambda d: T["mx%d" % t][:, d:d + 1], "e%d" % t, [(ma, 0, 8)])
         tt(R(m), s0, s1, OP.max)
         tt(R("sm", 0, 2), s0, s1, OP.is_ge)
@@ -449,7 +511,6 @@ def program(g, core, T, topo):
             tt(R("z", z + k, z + 48, 3), R("bk%d" % (3 if k else 2), 16 * k, 16 * k + 16), R(xl, 16 * k, 16 * k + 16), OP.add)
         scan(R("z", z + 48, z + 96), R("rs3"), R("z", z, z + 48), OP.mult, OP.max)
         ts(R("lp", off, off + 16), R("z", z + 50, z + 96, 3), -2 * BIG, OP.add)
-        chosen.append(len(ops) - 1)
 
     def own_parts(cc, cs):
         for b in range(4):
@@ -465,11 +526,8 @@ def program(g, core, T, topo):
             dec(1, b, cc, cs, True)
         for h in range(2):
             for b in (1, 3, 0, 2):
-                gate[0] = len(ops) - 1 if h + b != 1 else None
                 dec(h, b, pc, psn, False)
-        gate[0] = chosen[t]
         after_lists()
-        gate[0] = None
         for h in range(2):
             for b in range(4):
                 oo, ii = R("nt", 512 * h + b, 512 * h + 512, 4), bank(BK[h][b], 128)
@@ -487,14 +545,10 @@ def program(g, core, T, topo):
     for k in range(2):
         ts(R("o01", 16 * k, 16 * k + 16), nl[k], -256.0 * r, OP.add)
         act(R("xr", 256 * k, 256 * k + 256), ind(R("posn"), R("o01", 16 * k, 16 * k + 16)))
-    ts(R("gm"), R("g48"), col(1), OP.is_equal)
-    ts(R("rs8"), R("g48"), 0.0, OP.not_equal)
-    ts(R("rs16"), R("j64"), 0.0, OP.not_equal)
     ts(R("rs3"), R("k3"), 0.0, OP.not_equal)
-    ts(R("dm"), R("j64"), col(0), OP.is_equal)
-    tt(R("iv", 0, 32), ind(R("ir"), R("cc")), R("dm", 0, 32), OP.mult)
-    scan(R("iv", 32, 64), R("rs16", 0, 32), R("iv", 0, 32), OP.mult, OP.add)
-    inv = R("iv", 47, 64, 16)
+    tt(R("iv", 0, 16), R("nlst"), R("gm", 0, 16), OP.mult)
+    scan(R("iv", 16, 32), R("rs8", 0, 16), R("iv", 0, 16), OP.mult, OP.add)
+    inv = R("iv", 23, 32, 8)
     cp(R("of4", 0, 4, 2), inv)
     ts(R("of4", 1, 4, 2), inv, 256.0, OP.add)
     diagonal(R("xi", 0, 64), R("xr"), R("of4"))
@@ -514,8 +568,8 @@ def program(g, core, T, topo):
     ts(R("idn"), R("cmp"), 0.0, OP.is_equal)
     ts(R("dw"), R("io32"), col2(5), OP.is_equal)
     weights(0, [col(0), col(0)], 0)
-    act(R("ld", 0, 8), R("it", 0, 256, 32), AF.Copy, scale=col2(0))
-    act(R("ld", 8, 16), R("it", 16, 256, 32), AF.Copy, scale=col(3))
+    act(R("ld", 0, 8), R("nlst", 0, 16, 2), AF.Copy, scale=col2(0))
+    act(R("ld", 8, 16), R("nlst", 1, 16, 2), AF.Copy, scale=col(3))
     tt(R("ld", 16, 24), R("ld", 0, 8), R("ld", 8, 16), OP.add)
     for k in range(2):
         for w in range(2):
@@ -523,7 +577,7 @@ def program(g, core, T, topo):
     for k in range(2):
         act(R("xlg", 256 * k, 256 * k + 256), ind(R("xr"), R("ldu", 16 * k, 16 * k + 16)))
     for b in range(4):
-        act(R("et", b + 512 * b, 512 * b + 512, 4), R("idn"), AF.Copy, scale=0.5)
+        one(R("et", 512 * b, 512 * b + 512), R("hf"), b)
         qz(R("eqc", 128 * b, 128 * b + 128), R("eqs", 128 * b, 128 * b + 128), R("et", 512 * b, 512 * b + 512))
     tr(R("xlt"), R("xlg"))
     act(R("xl0", 0, 32), R("xlt", 0, 512, 16))
@@ -543,13 +597,11 @@ def program(g, core, T, topo):
             pick("b1c", "b1s", 0, 128, "b0c", "b0s", 0, 640, R("ln", 0, 8))
         else:
             pick("b1c", "b1s", 128, 256, "b0c", "b0s", 0, 768, R("ln", 8, 16))
-            picked.append(len(ops) - 2)
     merge(0, "b0c", "b0s", "b0c", "b0s", 512, lists0, half0)
 
     send_w("b1c", "b1s", "a1")
     pick("b1c", "b1s", 256, 288, "b0c", "b0s", 0, 640, R("ln", 16, 18))
     gram("b1c", "b1s")
-    gate[0] = chosen[0]
     for k in range(3):
         ts(R("fl", 16 * k, 16 * k + 16), R("z", k, 48, 3), 2 * BIG, OP.is_ge)
     tt(R("fl", 48, 96), R("fl", 0, 48), R("gm"), OP.mult)
@@ -558,15 +610,12 @@ def program(g, core, T, topo):
         act(R("pen", k, 4, 2) if k < 2 else R("pen", 4, 6), R("fl", 103 + 16 * k, 112 + 16 * k, 8), AF.Copy, scale=256.0 if k < 2 else 1e29)
     tt(R("pen", 8, 12), R("pen", 0, 4), R("xi", 15, 64, 16), OP.max)
     cp(R("xoa"), R("pen", 8, 12))
-    gate[0] = None
     local_scores(1)
-    gate[0] = chosen[0]
     act(R("xng", 512, 768), ind(R("posn"), R("dup", 0, 16)))
     tr(R("xnt", 512, 768), R("xng", 512, 768))
     cp(R("pou"), R("xnt", 512, 768, 16))
     pick("fc", "fs", 0, 256, "b1c", "b1s", 0, 256, R("pou"))
     own_parts("fc", "fs")
-    gate[0] = sent[0]
     ts(R("dup", 16, 32), R("tb"), col2(1), OP.add, 256.0, OP.add)
     for k in range(2):
         act(R("nr", 256 * k, 256 * k + 256), ind(R("iob"), R("o01", 16 * k, 16 * k + 16)))
@@ -578,7 +627,6 @@ def program(g, core, T, topo):
     ts(R("xi", 152, 154), R("xi", 136, 138), 4, OP.arith_shift_right)
     ts(R("xi", 154, 156), R("xi", 136, 138), 15, OP.bitwise_and)
     cp(R("hl", 8, 20), R("xi", 144, 156))
-    gate[0] = picked[0]
     statics(1, [R("hl", 16, 17), R("hl", 17, 18)], 8)
     tr(R("xnt", 0, 512), R("xng", 0, 512))
     act(R("xl1", 0, 32), R("xnt", 0, 512, 16))
@@ -588,9 +636,7 @@ def program(g, core, T, topo):
         for h in range(2):
             ts(R("u1", 192 + 64 * k + h, 256 + 64 * k, 4), R("nat", 32 + 16 * h, 48 + 16 * h), R("fl", 103 + 8 * (2 * k + h), 104 + 8 * (2 * k + h)), OP.mult)
     qz(R("qwc"), R("qws"), R("wt"))
-    gate[0] = None
     choose(1, "b1c", "b1s")
-    gate[0] = chosen[1]
     for k in range(6):
         tt(R("zp", 16 * k, 16 * k + 16), R("bk%d" % (3 if k else 2), 16 * k, 16 * k + 16), nl[k % 3], OP.add)
 
@@ -615,7 +661,6 @@ def program(g, core, T, topo):
         pick("oqc", "oqs", a, b, "fc", "fs", 0, 384 + 128 * h, R("ln", 20 + 8 * h, 28 + 8 * h))
         dma("y", "st0", (T.oc[:, 4 * a:4 * b], []), W8(R("oqc", a, b)))
         mm(bank(4 + h, 128), R("qwc"), R("qws"), R("oqc", a, b), R("oqs", a, b))
-    gate[0] = None
     merge(1, "b1c", "b1s", "fc", "fs", 256, lists1, half1)
     for k in range(4):
         dma("s" if k % 2 else "y", "st0", (T.osc[4 * k:4 * k + 4, :], []), (T.oqs[32 * k:32 * k + 4, :], [("oqs", 0, 256, 1)]))

@@ -7,10 +7,11 @@ OP = AluOpType
 AF = ActivationFunctionType
 NK = 2304
 BIG = 4096.0
-RND = 1.5 * 2.0 ** 27
+RND = 1.5 * 2.0 ** 28
 HOP = 0.14
 CY = 1.1e-3
-TRIES = 1500
+CASES = ((0.14, 1.0, 1.0), (0.22, 1.2, 1.25), (0.1, 1.0, 0.75))
+TRIES = 8000
 ORDERS = {}
 FP8, U8, F32, BF, I32, U16 = "float8_e4m3fn_x4", "uint8", "float32", "bfloat16", "int32", "uint16"
 
@@ -18,27 +19,27 @@ SCRATCH = {"nst": ("dram", [16, 92], I32), "p32a": ("sbuf", [32, 32], F32), "p32
            "lm": ("sbuf", [32, 64], F32)}
 for _t, _l in (
         (F32, "tk 16 tk32 32 j64 64 g48 48 cmp 128 k3 48 tb 16 d8 8 io32 32 col 4 col2 8 jl 16 gl 16 dm 64 rs16 64 rs8 48 rs3 48 "
-              "gm 48 idn 128 msk 16 dw 32 iv 32 xg 64 hl 20 ld 24 xl0 48 xl1 48 mn 256 gs 528 gg 64 sc 64 pen 16 sm 64 m0 2 m1 2 "
-              "ma0 8 ma1 8 mx0 8 mx1 8 lmm 1 mq 128 kcm 32 pcg 64 ph 4 nv 4 tkc 16 nlst 16 xd 256 jk 256 z 192 zp 160 fp 96 "
-              "lnf 64 fl 144 ys 256"),
-        (BF, "xt 1024 wt 512 iob 256 rowb 256 rowc 128 ones 256 zt 2304 cs 2304 et 2048 hf 512 pa 512 pm 512 "
-             "posn 256 xr 512 nr 512 xlg 512 xlt 512 xng 768 xnt 768 nat 64 ct 2048 u0 512 u1 512 nt 1024"),
+              "gm 48 idn 128 msk 16 dw 32 iv 32 xg 64 hl 20 ld 24 xl0 32 xl1 32 mn 256 gs 528 gg 64 sc 64 pen 16 sm 64 m0 2 m1 2 "
+              "ma0 8 ma1 8 mx0 8 mx1 8 lmm 1 mq 128 kcm 32 ph 4 nv 4 tkc 16 nlst 16 xd 256 jk 256 z 192 zp 176 fp 96 "
+              "lnf 96 fl 144 ys 256 tab 2304 zb 96"),
+        (BF, "xt 1024 wt 512 iob 256 rowb 256 rowc 128 kr 264 et 2048 hf 512 pa 1024 pm 1024 "
+             "posn 256 xr 512 nr 512 xlg 512 xlt 512 xng 768 xnt 768 nat 64 ct 2048 u0 512 u1 512 ve 1024 nt 1024"),
         (I32, "nb2 48 nn 92 xi 160")):
     _w = _l.split()
     for _n, _k in zip(_w[0::2], _w[1::2]):
         SCRATCH[_n] = ("sbuf", [128, int(_k)], _t)
 PIECE = {}
 for _b, _t, _l in (
-        ("uu", U16, "dup 32 ku 16 l18 18 o01 32 of4 4 xo 4 xoa 4 ldu 32 pou 16 ofx 8 lp 32 ln 36 kcu 2"),
-        ("kk", F32, "klow 16 kt 16 kb 16 kl 16 k1 16 k2 16 kf 16"),
-        ("kn", I32, "ka 16 kh 16 km 16 ki 16"),
+        ("uu", U16, "dup 32 ku 16 l18 18 o01 32 of4 4 xo 4 xoa 4 ldu 32 pou 16 ofx 8 lp 32 ln 36 pl 16"),
+        ("kk", F32, "klow 16 kt 16 kl 16 kx 16 k2 16 kf 16 jw 16 ss 2 lo 2"),
+        ("kn", I32, "ka 16 kb 16 km 16 ki 16"),
         ("cn", I32, "pp 4 ci 4")):
     _w, _c = _l.split(), 0
     for _n, _k in zip(_w[0::2], _w[1::2]):
         PIECE[_n] = (_b, _c, int(_k))
         _c += int(_k)
     SCRATCH[_b] = ("sbuf", [128, _c], _t)
-_w = "pa 128 pm 128 q0 256 qw 128 b0 768 b1 512 f 512 oq 256 eq 512 cq 512 uq 256 p0 256 p1 256".split()
+_w = "pa 256 pm 256 q0 256 qw 128 b0 768 b1 512 f 512 oq 256 eq 512 cq 512 uq 512 p0 256 p1 256".split()
 for _n, _k in zip(_w[0::2], _w[1::2]):
     SCRATCH[_n + "c"] = ("sbuf", [128, int(_k)], FP8)
     SCRATCH[_n + "s"] = ("sbuf", [128, int(_k)], U8)
@@ -98,8 +99,26 @@ def span(ops, seq, hop, comp, far):
     return end
 
 
+def chain(ops, seq, hop, comp, far):
+    fin, free, why = [0.0] * len(ops), {q: (0.0, -1) for q in "vstypa"}, [-1] * len(ops)
+    for i in seq:
+        q, deps, dur, lat = ops[i][0], ops[i][2], ops[i][5], ops[i][6]
+        t, w = (0.0, -1) if q == "a" else free[q]
+        for d in deps:
+            if fin[d] + hop > t:
+                t, w = fin[d] + hop, d
+        free[q] = (t + (dur * comp if q in "vst" and lat == dur else dur), i)
+        fin[i], why[i] = t + (lat * far if lat > 1.0 else lat * comp), w
+    i, l = max(range(len(ops)), key=lambda i: fin[i]), []
+    while i >= 0:
+        l.append(i)
+        i = why[i]
+    return l
+
+
 def search(ops):
     n = len(ops)
+    ops = [o[:6] + [o[6] * (0.8 if o[6] > 1.0 else 1.0)] for o in ops]
     succ, prio = [[] for _ in ops], [0.0] * n
     for i, o in enumerate(ops):
         for d in o[2]:
@@ -107,19 +126,23 @@ def search(ops):
     for i in range(n - 1, -1, -1):
         prio[i] = ops[i][6] + max([prio[j] + HOP for j in succ[i]] or [0.0])
     rng = np.random.default_rng(5)
-    best = None
+    best, hot = None, list(range(n))
     for k in range(TRIES):
         p = list(prio)
-        for _ in range(int(rng.integers(1, 13)) if k else 0):
-            p[int(rng.integers(n))] += float(rng.normal()) * (0.1, 0.5, 2.0)[int(rng.integers(3))]
+        for _ in range(int(rng.integers(1, 9)) if k else 0):
+            i = hot[int(rng.integers(len(hot)))] if rng.random() < 0.85 else int(rng.integers(n))
+            p[i] += float(rng.normal()) * (0.1, 0.5, 2.0)[int(rng.integers(3))]
         start = list_schedule(ops, succ, p, 0.05 * (k % 2))
-        e = max(start[i] + ops[i][6] for i in range(n))
-        if best is not None and e > best[2]:
-            continue
         seq = sorted(range(n), key=lambda i: (start[i], i))
-        e2 = 2 * e + span(ops, seq, 0.08, 0.9, 0.85) + span(ops, seq, 0.22, 1.2, 1.2)
-        if best is None or e2 <= best[0]:
-            best, prio = (e2, start, e + 0.1), p
+        e, top = 0.0, best[0] if best else 1e9
+        for case in CASES:
+            e += span(ops, seq, *case)
+            if e > top:
+                break
+        if e <= top:
+            if e < top:
+                hot = [i for case in CASES for i in chain(ops, seq, *case) if ops[i][0] in "vstp"]
+            best, prio = (e, start), p
     return best[1]
 
 
@@ -220,16 +243,17 @@ def program(g, core, T, topo):
     def ts(o, i, s1, op0, s2=None, op1=None):
         a, b = val(s1), val(s2)
         rd = i[1] + a[1] + b[1]
+        d = (0.05 + us(width(o), 1.5)) if len(i[1]) > 1 else us(width(o), half(o, i))
         if op1 is None:
-            issue("v", lambda: g.vector.tensor_scalar(o[0], i[0], a[0], None, op0), rd, o[1], "qv", 1, us(width(o), half(o, i)))
+            issue("v", lambda: g.vector.tensor_scalar(o[0], i[0], a[0], None, op0), rd, o[1], "qv", 1, d)
         else:
-            issue("v", lambda: g.vector.tensor_scalar(o[0], i[0], a[0], b[0], op0, op1), rd, o[1], "qv", 1, us(width(o), half(o, i)))
+            issue("v", lambda: g.vector.tensor_scalar(o[0], i[0], a[0], b[0], op0, op1), rd, o[1], "qv", 1, d)
 
     def tt(o, a, b, op):
         issue("v", lambda: g.vector.tensor_tensor(o[0], a[0], b[0], op), a[1] + b[1], o[1], "qv", 1,
               (0.05 + us(width(o), 1.5)) if len(a[1]) > 1 else us(width(o), 1 if a[1][0][0][:2] == "bk" else 2))
 
-    def cp(o, i):
+    def cp(o, i, n=None):
         issue("v", lambda: g.vector.tensor_copy(o[0], i[0]), i[1] + o[1][1:], o[1][:1], "qv", 1,
               (0.05 + us(width(i), 3.5)) if len(o[1]) > 1 else (0.05 + us(width(o), 1.5)) if len(i[1]) > 1 else us(width(o), half(o, i)))
 
@@ -287,7 +311,8 @@ def program(g, core, T, topo):
         for j, (k, i, n, src) in enumerate(u for u in runs if u[0] == 2):
             dma("ys"[(3 * gr + j) % 2], "lnb", (T.nb2[16 * gr + i:16 * gr + i + n, 0:46], [("nb2", 0, 48, 1)] if gr + i == 0 else []), (src, []))
     dma("y", "lx", R("xt"), (T.x[:, :], []))
-    dma("y", "lx2", R("pm", 64, 512), (T.x[:, 0:448], []))
+    for h in range(2):
+        dma("y", "lx2", R("pm", 512 * h + 64, 512 * h + 512), (T.x[:, 0:448], []))
     for k, i, n, src in runs:
         if k < 2:
             dma("s", "lst", (T.nst[i:i + n, 46 * k:46 * k + 46], [("nst", 0, 92, 1)] if i + k == 0 else []), (src, []))
@@ -298,24 +323,30 @@ def program(g, core, T, topo):
     nl = [R("nn", 46 * k, 46 * k + 46, 3) for k in range(2)] + [n2]
 
     iota(R("pp", 0, 1), [[0, 1]], 0, 1)
-    iota(R("tk"), [[1, 16]], 0, 0)
     iota(R("iob"), [[1, 256]], 0, 0)
+    iota(R("tk"), [[1, 16]], 0, 0)
     iota(R("tb"), [[32, 8], [0, 2]], 0, 0)
     iota(R("k3"), [[0, 16], [1, 3]], 0, 0)
-    iota(R("rowc"), [[0, 8], [1, 16]], 1, 0)
+    iota(R("rowc"), [[0, 8], [2, 16]], -255, 0)
     iota(R("j64"), [[0, 4], [1, 16]], 0, 0)
     iota(R("g48"), [[0, 6], [1, 8]], 0, 0)
     iota(R("cmp"), [[1, 128]], 0, -1)
     iota(R("tk32"), [[0, 2], [1, 16]], 0, 0)
     iota(R("d8"), [[0, 2], [1, 4]], 0, 0)
     iota(R("io32"), [[1, 32]], 0, 0)
-    iota(R("ones"), [[0, 256]], 1, 0)
     iota(R("rowb"), [[0, 16], [1, 16]], 0, 0)
-    fill(R("zt", 0, 1152), 0.0)
-    fill(R("zt", 1152, NK), 0.0)
     fill(R("hf"), 0.5)
+    fill(R("kr", 256, 264), -255.0)
+    fill(R("pm", 512, 576), 0.0)
     act(R("u0"), R("hf"), AF.Copy, scale=0.0)
     act(R("u1"), R("hf"), AF.Copy, scale=0.0)
+    for t in range(2):
+        act(R("ve", 512 * t, 512 * t + 512), R("hf"), AF.Copy, scale=0.0)
+    for b in range(NK // 256):
+        if b % 3 == 1:
+            act(R("tab", 256 * b, 256 * b + 256), R("iob"), AF.Copy, bias=256.0 * (b - 1 - r))
+        else:
+            ts(R("tab", 256 * b, 256 * b + 256), R("iob"), 256.0 * (b - 1 - r), OP.add)
 
     def c(k):
         return R("ci", k, k + 1)
@@ -332,13 +363,15 @@ def program(g, core, T, topo):
     cp(R("col"), R("ci"))
     act(R("jl"), R("tk"), AF.Identity, bias=col(0), scale=16.0)
     act(R("gl"), R("jl"), AF.Copy, bias=256.0 * r)
+    act(R("jw"), R("jl"), AF.Copy, bias=256.0)
+    act(R("z", 2, 48, 3), R("jl"))
     act(col2(0), col(3), AF.Copy, bias=1.0, scale=-1.0)
     act(col2(1), col(3), AF.Identity, bias=col(0), scale=16.0)
     act(col2(3), col(1), AF.Copy, bias=8.0)
     act(col2(4), col(0), AF.Copy, scale=2.0)
     act(col2(5), col(0), AF.Copy, bias=1.0, scale=2.0)
     ts(R("dup", 0, 16), R("tb"), col2(1), OP.add)
-    ts(R("tkc"), R("tk"), 16.0, OP.mult, RND, OP.add)
+    ts(R("tkc"), R("tk"), 32.0, OP.mult, RND, OP.add)
     for h in range(2):
         act(R("nv", 2 * h, 2 * h + 1), col(1), AF.Copy, bias=128.0 * h, scale=16.0)
         act(R("nv", 2 * h + 1, 2 * h + 2), col(0), AF.Copy)
@@ -346,40 +379,49 @@ def program(g, core, T, topo):
     ts(R("rs8"), R("g48"), 0.0, OP.not_equal)
     ts(R("rs16"), R("j64"), 0.0, OP.not_equal)
     ts(R("dm"), R("j64"), col(0), OP.is_equal)
+    for e in range(4):
+        ts(R("pa", 512 + e, 1024, 4), R("rowb", 0, 128), col(0), OP.is_equal)
+    qz(R("pac", 128, 256), R("pas", 128, 256), R("pa", 512, 1024))
 
     ts(R("ka"), n2, 256 * r, OP.bitwise_and)
-    ts(R("kh"), n2, 1792, OP.bitwise_and)
+    ts(R("kb"), n2, 1792 - 256 * r, OP.bitwise_and)
     tt(R("km"), n2, R("gl"), OP.min)
     tt(R("klow"), n2, R("gl"), OP.is_gt)
     ts(R("kt"), n2, 256.0 * (r + 1), OP.is_lt, -256.0, OP.mult)
-    ts(R("kb"), R("ka"), -2.0, OP.mult, 256.0 * r + 256.0, OP.add)
     ts(R("ki"), R("km"), 255, OP.bitwise_and)
+    tt(R("kx"), R("kb"), R("ka"), OP.subtract)
     tt(R("kl"), R("kt"), R("klow"), OP.mult)
-    tt(R("k1"), R("kb"), R("kh"), OP.add)
     tt(R("k2"), R("ki"), R("kl"), OP.add)
-    tt(R("kf"), R("k1"), R("k2"), OP.add)
-    cp(R("ku"), R("kf"))
-    cp(ind(R("zt"), R("ku")), R("ones"))
+    tt(R("kf"), R("k2"), R("kx"), OP.add)
+    ts(R("ku"), R("kf"), 256.0 * (r + 1), OP.add)
     tt(R("kcm", 0, 16), R("kf"), R("gm", 0, 16), OP.mult)
     scan(R("kcm", 16, 32), R("rs8", 0, 16), R("kcm", 0, 16), OP.mult, OP.add)
-    cp(R("kcu"), R("kcm", 23, 32, 8))
-    scan(R("cs"), R("zt"), R("zt"), OP.add, OP.max)
-    tt(R("pcg", 0, 32), ind(R("cs"), R("kcu")), R("dm", 0, 32), OP.mult)
-    scan(R("pcg", 32, 64), R("rs16", 0, 32), R("pcg", 0, 32), OP.mult, OP.add)
-    act(R("posn"), ind(R("cs"), R("ku")), AF.Copy, bias=-1.0)
-    ts(R("ph", 0, 2), R("pcg", 47, 64, 16), -8.5, OP.add, RND, OP.add)
-    ts(R("ph", 2, 4), R("ph", 0, 2), -RND, OP.add)
+    act(R("jk"), ind(R("tab"), R("ku")), AF.Sign, bias=R("kcm", 23, 24), scale=-1.0, accum=R("ss", 0, 1))
+    ts(R("kr", 0, 256), ind(R("tab"), R("ku")), R("kcm", 31, 32), OP.is_lt, 2.0, OP.mult)
+    red(R("ss", 1, 2), R("kr", 0, 257))
+    for h in range(2):
+        ts(R("ph", h, h + 1), R("ss", h, h + 1), 240.0, OP.add, RND, OP.add)
+        ts(R("ph", 2 + h, 3 + h), R("ph", h, h + 1), -RND, OP.add)
     for e in range(4):
         ts(R("pm", e, 64, 4), R("tkc"), R("ph", e // 2, e // 2 + 1), OP.is_equal, R("nv", e, e + 1), OP.mult)
-    qz(R("pmc"), R("pms"), R("pm"))
+    qz(R("pmc", 0, 128), R("pms", 0, 128), R("pm", 0, 512))
     for e in range(4):
-        ts(R("pa", e, 512, 4), R("rowc"), R("ph", 2 + e // 2, 3 + e // 2), OP.add, R("pcg", 47 + 16 * (e // 2), 48 + 16 * (e // 2)), OP.is_equal)
-    qz(R("pac"), R("pas"), R("pa"))
-    mm(R("bk6", 0, 128), R("pac"), R("pas"), R("pmc"), R("pms"))
+        ts(R("pa", e, 512, 4), R("rowc"), R("ph", 2 + e // 2, 3 + e // 2), OP.add, R("ss", e // 2, e // 2 + 1), OP.is_equal)
+    qz(R("pac", 0, 128), R("pas", 0, 128), R("pa", 0, 512))
+    mm(R("bk6", 0, 128), R("pac", 0, 128), R("pas", 0, 128), R("pmc", 0, 128), R("pms", 0, 128))
     cp(R("l18", 0, 16), R("bk6", 0, 16))
     cp(R("nlst"), R("bk6", 0, 16))
     cp(R("l18", 16, 17), R("nlst", 1, 2))
     cp(R("l18", 17, 18), R("nlst", 0, 1))
+    for h in range(2):
+        ts(R("lo", h, h + 1), R("ss", h, h + 1), 255.0, OP.add, R("ph", 2 + h, 3 + h), OP.subtract)
+        a = 512 + 34 * h
+        act(R("pm", a, 544 + 32 * h, 4), R("gm", 0, 8), AF.Copy, scale=R("ph", 2 + h, 3 + h))
+        act(R("pm", a + 1, 544 + 32 * h, 4), R("gm", 0, 8), AF.Copy, scale=R("lo", h, h + 1))
+    qz(R("pmc", 128, 256), R("pms", 128, 256), R("pm", 512, 1024))
+    mm(R("bk5", 0, 128), R("pac", 128, 256), R("pas", 128, 256), R("pmc", 128, 256), R("pms", 128, 256))
+    ts(R("pl"), R("bk5", 0, 16), 0.5, OP.mult)
+    act(R("posn"), ind(R("iob"), R("pl")))
     qz(R("q0c"), R("q0s"), R("xt"))
 
     def pick(dc, ds, a, b, sc, ss, w0, w1, off):
@@ -412,26 +454,28 @@ def program(g, core, T, topo):
         acc.setdefault(b, []).append((lo, hi, 1, True, group[sem][0]))
 
     def send_w(bc, bs, sem):
-        send(lambda d: T[bc][:, 32 * d:32 * d + 32].bitcast(dt.uint8), lambda d: T[bc][:, 256 + 32 * d:288 + 32 * d].bitcast(dt.uint8),
-             sem, [(bc, 0, 256)])
-        send(lambda d: T[bs][:, 32 * d:32 * d + 32], lambda d: T[bs][:, 256 + 32 * d:288 + 32 * d], sem, [(bs, 0, 256)])
+        send(lambda d: T[bc][:, 256 + 32 * d:288 + 32 * d].bitcast(dt.uint8), lambda d: T[bc][:, 32 * d:32 * d + 32].bitcast(dt.uint8),
+             sem, [(bc, 256, 512)])
+        send(lambda d: T[bs][:, 256 + 32 * d:288 + 32 * d], lambda d: T[bs][:, 32 * d:32 * d + 32], sem, [(bs, 256, 512)])
 
     def bank(k, n):
         return R("bk%d" % k, 0, n)
 
-    def gram(bc, bs):
-        mm(bank(0, 256), R(bc, 0, 128), R(bs, 0, 128), R(bc, 0, 256), R(bs, 0, 256))
+    def gram(bc, bs, mc, ms, m0):
+        mm(bank(0, 256), R(bc, 256, 384), R(bs, 256, 384), R(mc, m0, m0 + 256), R(ms, m0, m0 + 256))
         for k, j in enumerate((1, 3)):
-            mm(bank(j, 128), R(bc, 128, 256), R(bs, 128, 256), R(bc, 128 * k, 128 * k + 128), R(bs, 128 * k, 128 * k + 128))
+            a = m0 + 128 * k
+            mm(bank(j, 128), R(bc, 384, 512), R(bs, 384, 512), R(mc, a, a + 128), R(ms, a, a + 128))
         act(R("gs", 0, 256), bank(0, 256))
         cp(R("gs", 264, 392), bank(1, 128))
         cp(R("gs", 392, 520), bank(3, 128))
 
-    BK = [[4, 5, 6, 7], [0, 1, 2, 3]]
+    BK = [[0, 4, 5, 6], [0, 1, 2, 3]]
 
-    def dec(h, b, cc, cs, start):
-        mm(bank(BK[h][b], 128), R("eqc", 128 * b, 128 * b + 128), R("eqs", 128 * b, 128 * b + 128),
-           R(cc, 128 * h, 128 * h + 128), R(cs, 128 * h, 128 * h + 128), start, not start)
+    def dec(h, b, cc, cs, a, start):
+        w = 256 if b == 0 else 128
+        mm(bank(BK[h][b], w), R("eqc", 128 * b, 128 * b + 128), R("eqs", 128 * b, 128 * b + 128),
+           R(cc, a + 128 * h, a + 128 * h + w), R(cs, a + 128 * h, a + 128 * h + w), start, not start)
 
     def diagonal(o, i, off):
         tt(R("xg"), ind(i, off), R("dm"), OP.mult)
@@ -466,7 +510,7 @@ def program(g, core, T, topo):
             act(R("mn", a, a + 64, 2), R("tk32"), AF.Square, bias=hi_own[h], scale=-1.0)
             for k in range(2):
                 act(R("mn", a + 32 * k + 1, a + 32 * k + 32, 2), R("tk"), AF.Square, bias=R("hl", hl + 2 * h + k, hl + 2 * h + k + 1), scale=-1.0)
-            act(R("nat", 32 * t + 16 * h, 32 * t + 16 * h + 16), R("mn", a, a + 32, 2), AF.Relu, bias=2.0, scale=-2.0)
+            act(R("nat", 32 * t + 16 * h, 32 * t + 16 * h + 16), R("mn", a, a + 32, 2), AF.Relu, bias=0.0625, scale=-0.0625)
         for h in range(2):
             for k in range(2):
                 a = 64 * h + 32 * k
@@ -481,78 +525,88 @@ def program(g, core, T, topo):
                 ts(R("ct", a + 2 + h, a + 512, 4), R("rowb", 0, 128), R("hl", hl + 4 + 2 * h + k, hl + 5 + 2 * h + k), OP.is_equal, BIG, OP.mult)
         qz(R("cqc", 256 * t, 256 * t + 256), R("cqs", 256 * t, 256 * t + 256), R("ct", 1024 * t, 1024 * t + 1024))
 
+    def flags_times(t, k, b, uq):
+        ca = 256 * t + 128 * k
+        mm(bank(b, 128), R("cqc", ca, ca + 128), R("cqs", ca, ca + 128), R("uqc", uq, uq + 128), R("uqs", uq, uq + 128))
+
     def choose(t, bc, bs):
-        u, uq, m, mx = "u%d" % t, 128 * t, "m%d" % t, "mx%d" % t
-        arrive("a%d" % t, bc, 288, 512)
-        arrive("a%d" % t, bs, 288, 512)
+        u, uq, z, xl = "u%d" % t, 128 * t, 96 * t, "xl%d" % t
+        arrive("a%d" % t, bc, 32, 256)
+        arrive("a%d" % t, bs, 32, 256)
         for h in range(2):
-            mm(bank(2 + h, 128), R(bc, 128 * h, 128 * h + 128), R(bs, 128 * h, 128 * h + 128),
-               R(bc, 256 + 128 * h, 384 + 128 * h), R(bs, 256 + 128 * h, 384 + 128 * h))
-        arrive("e%d" % t, mx, 0, 8)
+            mm(bank(2 + h, 128), R(bc, 256 + 128 * h, 384 + 128 * h), R(bs, 256 + 128 * h, 384 + 128 * h),
+               R(bc, 128 * h, 128 * h + 128), R(bs, 128 * h, 128 * h + 128))
         for h in range(2):
             tt(R("xd", 128 * h, 128 * h + 128), bank(2 + h, 128), R("idn"), OP.mult)
         act(R("jk", 0, 128), R("xd", 0, 128), AF.Identity, accum=R("sm", 16, 17))
         red(R("sm", 17, 18), R("xd", 128, 256))
+        for h in range(2):
+            ts(R(u, h, 128, 2), R("mq", 64 * h, 64 * h + 64), R("sm", 16 + h, 17 + h), OP.is_ge)
+        qz(R("uqc", uq, uq + 128), R("uqs", uq, uq + 128), R(u))
+        for k in range(2):
+            flags_times(t, k, 2 + k, uq)
+        for k in range(2):
+            tt(R("z", z + k, z + 48, 3), R("bk%d" % (2 + k), 16 * k, 16 * k + 16), R(xl, 16 * k, 16 * k + 16), OP.add)
+        scan(R("z", z + 48, z + 96), R("rs3"), R("z", z, z + 48), OP.mult, OP.max)
+        cp(R("lp", 16 * t, 16 * t + 16), R("z", z + 50, z + 96, 3))
+
+    def decide(t):
+        mx, v = "mx%d" % t, 512 * t
+        arrive("e%d" % t, mx, 0, 8)
         for a, b, i in ((0, 1, R("lmm")), (1, 4, R(mx, 1, 4)), (4, 8, R(mx, 4, 8))):
             ts(R("ofx", a, b), i, R("sm", 16 + a // 4, 17 + a // 4), OP.is_lt, col2(4), OP.add)
         for h in range(2):
             act(R("jk", 128 + 64 * h, 192 + 64 * h), ind(R("dw"), R("ofx", 4 * h, 4 * h + 4)), AF.Copy, accum=R("sm", 20 + h, 21 + h))
-        tt(R("sm", 22, 24), R("sm", 16, 18), R(m), OP.is_gt)
+        tt(R("sm", 22, 24), R("sm", 16, 18), R("m%d" % t), OP.is_gt)
         for h in range(2):
-            ts(R(u, h, 128, 2), R("mq", 64 * h, 64 * h + 64), R("sm", 16 + h, 17 + h), OP.is_ge)
-        for h in range(2):
-            ts(R(u, 128 + h, 192, 4), R("nat", 32 * t + 16 * h, 32 * t + 16 * h + 16), R("sm", 20 + h, 21 + h), OP.mult, R("sm", 22 + h, 23 + h), OP.mult)
-        qz(R("uqc", uq, uq + 128), R("uqs", uq, uq + 128), R(u))
-        for k in range(2):
-            ca = 256 * t + 128 * k
-            mm(bank(2 + k, 128), R("cqc", ca, ca + 128), R("cqs", ca, ca + 128), R("uqc", uq, uq + 128), R("uqs", uq, uq + 128))
-        z, xl, off = 96 * t, "xl%d" % t, 16 * t
-        for k in range(3):
-            tt(R("z", z + k, z + 48, 3), R("bk%d" % (3 if k else 2), 16 * k, 16 * k + 16), R(xl, 16 * k, 16 * k + 16), OP.add)
-        scan(R("z", z + 48, z + 96), R("rs3"), R("z", z, z + 48), OP.mult, OP.max)
-        ts(R("lp", off, off + 16), R("z", z + 50, z + 96, 3), -2 * BIG, OP.add)
+            ts(R("ve", v + h, v + 64, 4), R("nat", 32 * t + 16 * h, 32 * t + 16 * h + 16), R("sm", 20 + h, 21 + h), OP.mult, R("sm", 22 + h, 23 + h), OP.mult)
+        vq = 256 + 128 * t
+        qz(R("uqc", vq, vq + 128), R("uqs", vq, vq + 128), R("ve", v, v + 512))
+        flags_times(t, 0, 7, vq)
+        a = 48 * t
+        ts(R("lnf", a, a + 16), R("z", 96 * t + 50, 96 * t + 96, 3), 256.0, OP.is_ge, 256.0, OP.mult)
+        tt(R("lnf", a + 16, a + 32), R("lnf", a, a + 16), R("jl" if t else "jw"), OP.add)
+        tt(R("lnf", a + 32, a + 48), bank(7, 16), R("lnf", a + 16, a + 32), OP.add)
+        cp(R("ln", 20 * t, 20 * t + 16), R("lnf", a + 32, a + 48))
 
-    def own_parts(cc, cs):
-        for b in range(4):
-            dec(0, b, cc, cs, True)
-        for b in range(2):
-            dec(1, b, cc, cs, True)
+    def own_parts(cc, cs, a):
+        for h, b in ((0, 0), (0, 1), (0, 2), (0, 3), (1, 1)):
+            dec(h, b, cc, cs, a, True)
 
-    def merge(t, bc, bs, cc, cs, base, after_lists, half_done):
+    def merge(t, bc, bs, cc, cs, own, base):
         pc, psn, off = "p%dc" % t, "p%ds" % t, 16 * t
         for h in range(2):
             pick(pc, psn, 128 * h, 128 * h + 128, bc, bs, 0, 512, R("lp", off + 8 * h, off + 8 * h + 8))
         for b in range(2, 4):
-            dec(1, b, cc, cs, True)
-        for h in range(2):
-            for b in (1, 3, 0, 2):
-                dec(h, b, pc, psn, False)
-        after_lists()
+            dec(1, b, cc, cs, own, True)
+        for h, b in ((0, 1), (0, 2), (0, 3), (0, 0), (1, 1), (1, 2), (1, 3)):
+            dec(h, b, pc, psn, 0, False)
         for h in range(2):
             for b in range(4):
-                oo, ii = R("nt", 512 * h + b, 512 * h + 512, 4), bank(BK[h][b], 128)
-                if b % 2 == 0:
-                    cp(oo, ii)
+                oo = R("nt", 512 * h + b, 512 * h + 512, 4)
+                if b == 0:
+                    cp(oo, R("bk0", 128 * h, 128 * h + 128))
+                elif b == 2:
+                    cp(oo, bank(BK[h][b], 128))
                 else:
-                    act(oo, ii)
+                    act(oo, bank(BK[h][b], 128))
             qz(R(cc, base + 128 * h, base + 128 * h + 128), R(cs, base + 128 * h, base + 128 * h + 128), R("nt", 512 * h, 512 * h + 512))
-            half_done(h)
 
-    pick("b0c", "b0s", 0, 256, "q0c", "q0s", 0, 256, R("l18", 0, 16))
+    pick("b0c", "b0s", 256, 512, "q0c", "q0s", 0, 256, R("l18", 0, 16))
     send_w("b0c", "b0s", "a0")
-    pick("b0c", "b0s", 256, 288, "q0c", "q0s", 0, 256, R("l18", 16, 18))
-    gram("b0c", "b0s")
+    pick("b0c", "b0s", 0, 32, "q0c", "q0s", 0, 256, R("l18", 16, 18))
+    gram("b0c", "b0s", "q0c", "q0s", 0)
     for k in range(2):
         ts(R("o01", 16 * k, 16 * k + 16), nl[k], -256.0 * r, OP.add)
-        act(R("xr", 256 * k, 256 * k + 256), ind(R("posn"), R("o01", 16 * k, 16 * k + 16)))
+        act(R("nr", 256 * k, 256 * k + 256), ind(R("iob"), R("o01", 16 * k, 16 * k + 16)))
     ts(R("rs3"), R("k3"), 0.0, OP.not_equal)
     tt(R("iv", 0, 16), R("nlst"), R("gm", 0, 16), OP.mult)
     scan(R("iv", 16, 32), R("rs8", 0, 16), R("iv", 0, 16), OP.mult, OP.add)
     inv = R("iv", 23, 32, 8)
     cp(R("of4", 0, 4, 2), inv)
     ts(R("of4", 1, 4, 2), inv, 256.0, OP.add)
-    diagonal(R("xi", 0, 64), R("xr"), R("of4"))
-    cp(R("xo"), R("xi", 15, 64, 16))
+    diagonal(R("xi", 64, 128), R("nr"), R("of4"))
+    cp(R("xo"), R("xi", 79, 128, 16))
     tt(R("p32a"), R("cmp", 0, 32, 1, 32), R("cmp", 0, 32, 1, 32), OP.mult)
     ts(R("p32"), R("p32a"), 256.0, OP.is_equal)
     fill(R("lmm"), 1e29)
@@ -561,6 +615,9 @@ def program(g, core, T, topo):
     ts(R("msk", 8, 16), R("d8"), col(2), OP.not_equal, 2e29, OP.mult)
     ts(R("msk", 0, 8), R("msk", 8, 16), -1e29, OP.add)
     local_scores(0)
+    for k in range(2):
+        act(R("xr", 256 * k, 256 * k + 256), ind(R("posn"), R("o01", 16 * k, 16 * k + 16)))
+    diagonal(R("xi", 0, 64), R("xr"), R("of4"))
     ts(R("xi", 128, 132), R("xi", 15, 64, 16), 4, OP.arith_shift_right)
     ts(R("xi", 132, 136), R("xi", 15, 64, 16), 15, OP.bitwise_and)
     cp(R("hl", 0, 8), R("xi", 128, 136))
@@ -580,30 +637,22 @@ def program(g, core, T, topo):
         one(R("et", 512 * b, 512 * b + 512), R("hf"), b)
         qz(R("eqc", 128 * b, 128 * b + 128), R("eqs", 128 * b, 128 * b + 128), R("et", 512 * b, 512 * b + 512))
     tr(R("xlt"), R("xlg"))
-    act(R("xl0", 0, 32), R("xlt", 0, 512, 16))
-    act(R("xl0", 32, 48), R("jl"), AF.Copy, bias=256.0)
-    own_parts("b0c", "b0s")
+    act(R("xl0"), R("xlt", 0, 512, 16), AF.Copy, bias=256.0 - 2 * BIG)
+    own_parts("b0c", "b0s", 256)
     choose(0, "b0c", "b0s")
-
-    def lists0():
-        ts(R("lnf", 0, 16), R("z", 50, 96, 3), 2 * BIG, OP.is_ge, 512.0, OP.mult)
-        tt(R("lnf", 16, 32), R("lnf", 0, 16), R("jl"), OP.add)
-        cp(R("ln", 0, 16), R("lnf", 16, 32))
-        cp(R("ln", 16, 17), R("lnf", 17, 18))
-        cp(R("ln", 17, 18), R("lnf", 16, 17))
-
-    def half0(h):
-        if h == 0:
-            pick("b1c", "b1s", 0, 128, "b0c", "b0s", 0, 640, R("ln", 0, 8))
-        else:
-            pick("b1c", "b1s", 128, 256, "b0c", "b0s", 0, 768, R("ln", 8, 16))
-    merge(0, "b0c", "b0s", "b0c", "b0s", 512, lists0, half0)
+    merge(0, "b0c", "b0s", "b0c", "b0s", 256, 512)
+    decide(0)
+    cp(R("ln", 16, 17), R("lnf", 33, 34))
+    cp(R("ln", 17, 18), R("lnf", 32, 33))
+    for h in range(2):
+        pick("b1c", "b1s", 256 + 128 * h, 384 + 128 * h, "b0c", "b0s", 0, 640 + 128 * h, R("ln", 8 * h, 8 * h + 8))
 
     send_w("b1c", "b1s", "a1")
-    pick("b1c", "b1s", 256, 288, "b0c", "b0s", 0, 640, R("ln", 16, 18))
-    gram("b1c", "b1s")
-    for k in range(3):
-        ts(R("fl", 16 * k, 16 * k + 16), R("z", k, 48, 3), 2 * BIG, OP.is_ge)
+    pick("b1c", "b1s", 0, 32, "b0c", "b0s", 0, 640, R("ln", 16, 18))
+    gram("b1c", "b1s", "b1c", "b1s", 256)
+    for k in range(2):
+        ts(R("fl", 16 * k, 16 * k + 16), R("z", k, 48, 3), 256.0, OP.is_ge)
+    ts(R("fl", 32, 48), bank(7, 16), 128.0, OP.is_ge)
     tt(R("fl", 48, 96), R("fl", 0, 48), R("gm"), OP.mult)
     scan(R("fl", 96, 144), R("rs8"), R("fl", 48, 96), OP.mult, OP.add)
     for k in range(3):
@@ -614,13 +663,11 @@ def program(g, core, T, topo):
     act(R("xng", 512, 768), ind(R("posn"), R("dup", 0, 16)))
     tr(R("xnt", 512, 768), R("xng", 512, 768))
     cp(R("pou"), R("xnt", 512, 768, 16))
-    pick("fc", "fs", 0, 256, "b1c", "b1s", 0, 256, R("pou"))
-    own_parts("fc", "fs")
+    pick("fc", "fs", 0, 256, "b1c", "b1s", 256, 512, R("pou"))
+    own_parts("fc", "fs", 0)
     ts(R("dup", 16, 32), R("tb"), col2(1), OP.add, 256.0, OP.add)
     for k in range(2):
-        act(R("nr", 256 * k, 256 * k + 256), ind(R("iob"), R("o01", 16 * k, 16 * k + 16)))
         act(R("xng", 256 * k, 256 * k + 256), ind(R("xr"), R("dup", 16 * k, 16 * k + 16)))
-    diagonal(R("xi", 64, 128), R("nr"), R("of4"))
     cp(R("xi", 136, 138), inv)
     ts(R("xi", 144, 148), R("xi", 79, 128, 16), 4, OP.arith_shift_right)
     ts(R("xi", 148, 152), R("xi", 79, 128, 16), 15, OP.bitwise_and)
@@ -629,39 +676,38 @@ def program(g, core, T, topo):
     cp(R("hl", 8, 20), R("xi", 144, 156))
     statics(1, [R("hl", 16, 17), R("hl", 17, 18)], 8)
     tr(R("xnt", 0, 512), R("xng", 0, 512))
-    act(R("xl1", 0, 32), R("xnt", 0, 512, 16))
-    act(R("xl1", 32, 48), R("xnt", 512, 768, 16), AF.Copy, bias=256.0)
+    act(R("xl1"), R("xnt", 0, 512, 16), AF.Copy, bias=256.0 - 2 * BIG)
+    act(R("z", 98, 144, 3), R("xnt", 512, 768, 16))
     weights(1, [R("hl", 18, 19), R("hl", 19, 20)], 8)
     for k in range(3):
         for h in range(2):
-            ts(R("u1", 192 + 64 * k + h, 256 + 64 * k, 4), R("nat", 32 + 16 * h, 48 + 16 * h), R("fl", 103 + 8 * (2 * k + h), 104 + 8 * (2 * k + h)), OP.mult)
+            ts(R("u1", 192 + 64 * k + h, 256 + 64 * k, 4), R("nat", 32 + 16 * h, 48 + 16 * h), R("fl", 103 + 8 * (2 * k + h), 104 + 8 * (2 * k + h)), OP.mult, 32.0, OP.mult)
     qz(R("qwc"), R("qws"), R("wt"))
     choose(1, "b1c", "b1s")
-    for k in range(6):
-        tt(R("zp", 16 * k, 16 * k + 16), R("bk%d" % (3 if k else 2), 16 * k, 16 * k + 16), nl[k % 3], OP.add)
-
-    def lists1():
-        ts(R("lnf", 32, 48), R("z", 146, 192, 3), 2 * BIG, OP.is_ge, 256.0, OP.mult)
-        tt(R("lnf", 48, 64), R("lnf", 32, 48), R("jl"), OP.add)
-        cp(R("ln", 20, 36), R("lnf", 48, 64))
-        for t in range(2):
-            a = 48 - 48 * t
-            tt(R("zp", 128 + 16 * t, 144 + 16 * t), R("zp", a, a + 16), R("zp", a + 16, a + 32), OP.max)
-            tt(R("zp", 96 + 16 * t, 112 + 16 * t), R("zp", 128 + 16 * t, 144 + 16 * t), R("zp", a + 32, a + 48), OP.max)
-        ts(R("fp", 0, 32), R("zp", 96, 128), -2 * BIG, OP.add, -1.0, OP.max)
-        tt(R("fp", 32, 64), R("fp", 0, 32), R("gm", 0, 32), OP.mult)
-        scan(R("fp", 64, 96), R("rs8", 0, 32), R("fp", 32, 64), OP.mult, OP.add)
-        for t in range(2):
-            for h in range(2):
-                a = 64 + 8 * (2 * t + h) + 7
-                dma("y", "st0", (T.pr[t:t + 1, 128 * h:128 * h + 128], []), R("fp", a, a + 1))
-
-    def half1(h):
+    cp(R("zb", 0, 16), bank(2, 16))
+    cp(R("zb", 16, 96), R("bk3", 16, 96))
+    for k in (0, 1, 3, 4, 5):
+        tt(R("zp", 16 * k, 16 * k + 16), R("zb", 16 * k, 16 * k + 16), nl[k % 3], OP.add)
+    merge(1, "b1c", "b1s", "fc", "fs", 0, 256)
+    decide(1)
+    ts(R("zp", 160, 176), bank(7, 16), 32.0, OP.mult)
+    tt(R("zp", 32, 48), R("zp", 160, 176), n2, OP.add)
+    for t in range(2):
+        a = 48 - 48 * t
+        tt(R("zp", 128 + 16 * t, 144 + 16 * t), R("zp", a, a + 16), R("zp", a + 16, a + 32), OP.max)
+        tt(R("zp", 96 + 16 * t, 112 + 16 * t), R("zp", 128 + 16 * t, 144 + 16 * t), R("zp", a + 32, a + 48), OP.max)
+    ts(R("fp", 0, 32), R("zp", 96, 128), -2 * BIG, OP.add, -1.0, OP.max)
+    tt(R("fp", 32, 64), R("fp", 0, 32), R("gm", 0, 32), OP.mult)
+    scan(R("fp", 64, 96), R("rs8", 0, 32), R("fp", 32, 64), OP.mult, OP.add)
+    for t in range(2):
+        for h in range(2):
+            a = 64 + 8 * (2 * t + h) + 7
+            dma("y", "st0", (T.pr[t:t + 1, 128 * h:128 * h + 128], []), R("fp", a, a + 1))
+    for h in range(2):
         a, b = 128 * h, 128 * h + 128
         pick("oqc", "oqs", a, b, "fc", "fs", 0, 384 + 128 * h, R("ln", 20 + 8 * h, 28 + 8 * h))
         dma("y", "st0", (T.oc[:, 4 * a:4 * b], []), W8(R("oqc", a, b)))
         mm(bank(4 + h, 128), R("qwc"), R("qws"), R("oqc", a, b), R("oqs", a, b))
-    merge(1, "b1c", "b1s", "fc", "fs", 256, lists1, half1)
     for k in range(4):
         dma("s" if k % 2 else "y", "st0", (T.osc[4 * k:4 * k + 4, :], []), (T.oqs[32 * k:32 * k + 4, :], [("oqs", 0, 256, 1)]))
     cp(R("ys", 0, 128), bank(4, 128))

@@ -1,153 +1,65 @@
 import math
-import numpy as np
 from concourse.bass import DstId, RemoteDMATransfer
 from concourse.mybir import dt, AluOpType, AxisListType, ActivationFunctionType
 
 OP = AluOpType
 AF = ActivationFunctionType
-NK = 2304
 BIG = 4096.0
 RND = 1.5 * 2.0 ** 28
-HOP = 0.14
 CY = 1.1e-3
-CASES = ((0.14, 1.0, 1.0), (0.22, 1.2, 1.25), (0.1, 1.0, 0.75))
-TRIES = 8000
-ORDERS = {}
 FP8, U8, F32, BF, I32, U16 = "float8_e4m3fn_x4", "uint8", "float32", "bfloat16", "int32", "uint16"
+ORDER = """
+32 42 5 2 6 1 0 3 56 35 4 7 14 12 43 11 31 10 46 13 18 40 16 63 60 15 33 17 37 47 166 50 65 49 34 51 48 64 38 68 87 52 9 72 69 62 58 41 53 66
+59 61 74 205 97 90 36 96 73 99 75 98 76 167 71 54 24 20 8 100 26 84 25 55 45 21 22 23 101 19 28 237 29 57 30 103 27 102 77 105 104 44 106 107
+227 70 67 109 81 108 94 127 92 110 111 114 118 129 79 113 91 112 116 165 115 39 119 93 121 120 78 89 117 209 122 156 155 131 128 123 140 157
+158 124 125 159 141 142 160 126 161 143 80 229 88 162 133 149 95 134 132 145 168 130 361 150 163 144 135 152 151 164 153 203 136 148 154 191
+146 169 214 137 82 170 228 139 171 147 173 172 187 138 181 206 178 174 185 179 176 213 177 86 186 195 384 182 183 189 188 231 175 190 184 235
+211 192 210 222 207 216 180 215 218 208 196 221 239 217 197 212 199 238 202 220 241 232 193 240 201 219 200 233 243 242 223 342 245 198 244
+346 224 204 85 83 246 230 225 194 247 276 248 226 277 280 234 278 249 250 279 257 281 251 258 282 252 236 283 256 255 284 254 285 253 264 363
+286 263 307 349 262 287 345 357 308 309 272 288 273 261 266 259 310 269 260 271 370 358 265 376 267 268 274 270 275 292 356 311 291 294 293
+313 362 289 297 312 354 343 301 355 367 359 377 316 360 302 317 295 318 303 365 314 304 298 305 315 306 336 319 320 296 368 321 364 290 331
+322 323 335 333 300 324 326 328 332 327 329 369 299 366 381 347 371 379 380 325 372 344 348 334 330 373 351 353 374 382 352 386 350 383 385
+378 388 340 387 337 390 389 338 392 391 393 430 395 434 375 394 431 432 401 341 397 433 396 339 400 435 412 398 436 411 399 437 410 409 438
+404 408 407 417 443 418 405 402 439 416 445 444 440 427 413 406 403 420 415 447 421 414 441 446 425 423 419 426 422 448 428 442 424 449 429
+457 456 461 460 459 450 464 467 463 462 451 466 468 458 452 469 453 470 454 465 455 471
+"""
 
-SCRATCH = {"nst": ("dram", [16, 92], I32), "p32a": ("sbuf", [32, 32], F32), "p32": ("sbuf", [32, 32], F32),
-           "lm": ("sbuf", [32, 64], F32)}
+SCRATCH = {"nst": ("dram", [16, 138], I32)}
 for _t, _l in (
-        (F32, "tk 16 tk32 32 j64 64 g48 48 cmp 128 k3 48 tb 16 d8 8 io32 32 col 4 col2 8 jl 16 gl 16 dm 64 rs16 64 rs8 48 rs3 48 "
-              "gm 48 idn 128 msk 16 dw 32 iv 32 xg 64 hl 20 ld 24 xl0 32 xl1 32 mn 256 gs 528 gg 64 sc 64 pen 16 sm 64 m0 2 m1 2 "
-              "ma0 8 ma1 8 mx0 8 mx1 8 lmm 1 mq 128 kcm 32 ph 4 nv 4 tkc 16 nlst 16 xd 256 jk 256 z 192 zp 176 fp 96 "
-              "lnf 96 fl 144 ys 256 tab 2304 zb 96"),
-        (BF, "xt 1024 wt 512 iob 256 rowb 256 rowc 128 kr 264 et 2048 hf 512 pa 1024 pm 1024 "
-             "posn 256 xr 512 nr 512 xlg 512 xlt 512 xng 768 xnt 768 nat 64 ct 2048 u0 512 u1 512 ve 1024 nt 1024"),
-        (I32, "nb2 48 nn 92 xi 160")):
+        (F32, "t48 48 k3 48 g24 48 j64 64 g48 48 d8 8 ones 128 idn 128 sqa 128 sqb 256 gms 8 col 8 col2 4 gl48 48 own48 48 "
+              "jl 16 jw 16 dm 64 rs16 64 rs8 48 rs3 48 rs24 48 gm 48 gmt 48 mk48 48 msk 16 dw 32 iv 32 xg 64 xg2 64 hl 20 hls 8 "
+              "xl0 32 xl1 32 xlt 64 mn 256 gs 528 gg 64 sc 64 pen 20 sm 32 m0 2 m1 2 ma0 8 ma1 8 mx0 8 mx1 8 mq 128 "
+              "tkc 18 xd 260 jk 256 jq 128 z 192 zp 176 zb 80 fp 96 lnf 96 fl 144 ys 256 tab 2304"),
+        (BF, "xt 1024 wt 512 iob 256 one 516 rowb 256 rowd 128 rowc 128 kr 256 krs 256 phb 2 et 516 pa 1024 P1 584 P2 896 U0 640 U1 640 "
+             "posn 256 nr 512 nat 64 ct 2048 nt 1024"),
+        (I32, "nbw 48 nn 138 hi 48 xi 180")):
     _w = _l.split()
     for _n, _k in zip(_w[0::2], _w[1::2]):
         SCRATCH[_n] = ("sbuf", [128, int(_k)], _t)
 PIECE = {}
 for _b, _t, _l in (
-        ("uu", U16, "dup 32 ku 16 l18 18 o01 32 of4 4 xo 4 xoa 4 ldu 32 pou 16 ofx 8 lp 32 ln 36 pl 16"),
-        ("kk", F32, "klow 16 kt 16 kl 16 kx 16 k2 16 kf 16 jw 16 ss 2 lo 2"),
-        ("kn", I32, "ka 16 kb 16 km 16 ki 16"),
-        ("cn", I32, "pp 4 ci 4")):
+        ("uu", U16, "ku 16 l18 18 o01 32 of4 4 xo 4 xoa 4 ofx 8 lp 32 ln 36 pl 16"),
+        ("cn", I32, "pp 2 ci 6"),
+        ("fa", F32, "n2m 48 xa 48 kw 48 xm 48 kf 48 ks 48 km 48 kc 48 ss 2 lo 2 ph 4 nv 4 wr 2 tkw 16")):
     _w, _c = _l.split(), 0
     for _n, _k in zip(_w[0::2], _w[1::2]):
         PIECE[_n] = (_b, _c, int(_k))
         _c += int(_k)
     SCRATCH[_b] = ("sbuf", [128, _c], _t)
-_w = "pa 256 pm 256 q0 256 qw 128 b0 768 b1 512 f 512 oq 256 eq 512 cq 512 uq 512 p0 256 p1 256".split()
+_w = "pa 256 pm 256 pl2 256 q0 256 qw 128 b0 768 b1 512 f 512 oq 256 eq 512 cq 512 uq 512 p0 256 p1 256".split()
 for _n, _k in zip(_w[0::2], _w[1::2]):
     SCRATCH[_n + "c"] = ("sbuf", [128, int(_k)], FP8)
     SCRATCH[_n + "s"] = ("sbuf", [128, int(_k)], U8)
 for _k in range(8):
     SCRATCH["bk%d" % _k] = ("psum", [128, 512], F32)
 
-SEMAPHORES = ["qv", "qs", "qt", "qp", "lnb", "lx", "lx2", "lw", "lst", "lnn", "st0", "loc", "a0", "a1", "e0", "e1"]
-
-
-def list_schedule(ops, succ, prio, slack):
-    n = len(ops)
-    left = [len(o[2]) for o in ops]
-    ready, start = [0.0] * n, [0.0] * n
-    free = {q: 0.0 for q in "vstypa"}
-    cand = {q: [] for q in free}
-    for i in range(n):
-        if not left[i]:
-            cand[ops[i][0]].append(i)
-    for _ in range(n):
-        best = None
-        for q, l in cand.items():
-            if not l:
-                continue
-            f = 0.0 if q == "a" else free[q]
-            st = {i: f if f > ready[i] else ready[i] for i in l}
-            lo = min(st.values()) + 0.02
-            i = max((j for j in l if st[j] <= lo), key=lambda j: prio[j])
-            e, p = st[i] + ops[i][5] - slack, prio[i]
-            better = [j for j in l if prio[j] > p and st[j] < e]
-            if better:
-                i = max(better, key=lambda j: prio[j])
-            if best is None or st[i] < best[0]:
-                best = (st[i], q, i)
-        t, q, i = best
-        cand[q].remove(i)
-        start[i] = t
-        free[q] = t + ops[i][5]
-        for j in succ[i]:
-            left[j] -= 1
-            ready[j] = max(ready[j], t + ops[i][6] + HOP)
-            if not left[j]:
-                cand[ops[j][0]].append(j)
-    return start
-
-
-def span(ops, seq, hop, comp, far):
-    fin, free, end = [0.0] * len(ops), {q: 0.0 for q in "vstypa"}, 0.0
-    for i in seq:
-        q, deps, dur, lat = ops[i][0], ops[i][2], ops[i][5], ops[i][6]
-        t = 0.0 if q == "a" else free[q]
-        for d in deps:
-            if fin[d] + hop > t:
-                t = fin[d] + hop
-        free[q] = t + (dur * comp if q in "vst" and lat == dur else dur)
-        fin[i] = t + (lat * far if lat > 1.0 else lat * comp)
-        end = max(end, fin[i])
-    return end
-
-
-def chain(ops, seq, hop, comp, far):
-    fin, free, why = [0.0] * len(ops), {q: (0.0, -1) for q in "vstypa"}, [-1] * len(ops)
-    for i in seq:
-        q, deps, dur, lat = ops[i][0], ops[i][2], ops[i][5], ops[i][6]
-        t, w = (0.0, -1) if q == "a" else free[q]
-        for d in deps:
-            if fin[d] + hop > t:
-                t, w = fin[d] + hop, d
-        free[q] = (t + (dur * comp if q in "vst" and lat == dur else dur), i)
-        fin[i], why[i] = t + (lat * far if lat > 1.0 else lat * comp), w
-    i, l = max(range(len(ops)), key=lambda i: fin[i]), []
-    while i >= 0:
-        l.append(i)
-        i = why[i]
-    return l
-
-
-def search(ops):
-    n = len(ops)
-    ops = [o[:6] + [o[6] * (0.8 if o[6] > 1.0 else 1.0)] for o in ops]
-    succ, prio = [[] for _ in ops], [0.0] * n
-    for i, o in enumerate(ops):
-        for d in o[2]:
-            succ[d].append(i)
-    for i in range(n - 1, -1, -1):
-        prio[i] = ops[i][6] + max([prio[j] + HOP for j in succ[i]] or [0.0])
-    rng = np.random.default_rng(5)
-    best, hot = None, list(range(n))
-    for k in range(TRIES):
-        p = list(prio)
-        for _ in range(int(rng.integers(1, 9)) if k else 0):
-            i = hot[int(rng.integers(len(hot)))] if rng.random() < 0.85 else int(rng.integers(n))
-            p[i] += float(rng.normal()) * (0.1, 0.5, 2.0)[int(rng.integers(3))]
-        start = list_schedule(ops, succ, p, 0.05 * (k % 2))
-        seq = sorted(range(n), key=lambda i: (start[i], i))
-        e, top = 0.0, best[0] if best else 1e9
-        for case in CASES:
-            e += span(ops, seq, *case)
-            if e > top:
-                break
-        if e <= top:
-            if e < top:
-                hot = [i for case in CASES for i in chain(ops, seq, *case) if ops[i][0] in "vstp"]
-            best, prio = (e, start), p
-    return best[1]
+SEMAPHORES = ["qv", "qs", "qt", "qp", "lnb", "lx", "lx2", "lx3", "lw", "lst", "lnn", "st0", "lm0", "lm1", "loc", "a0", "a1", "e0", "e1"]
 
 
 def program(g, core, T, topo):
     r = T.rank_of(core)
+    blk = [(r + q) % 8 for q in range(8)]
+    lb = blk[r]
     Q = {"v": g.vector, "s": g.scalar, "t": g.tensor, "y": g.sync, "p": g}
     cnt = {}
     known = {k: {} for k in Q}
@@ -176,17 +88,10 @@ def program(g, core, T, topo):
                 l.append((lo, hi, st, w, me))
         return me
 
-    def order():
-        key = tuple((o[0], tuple(o[2]), o[5], o[6]) for o in ops)
-        if key not in ORDERS:
-            ORDERS[key] = search(ops)
-        start, n = ORDERS[key], len(ops)
-        return sorted(range(n), key=lambda i: (start[i], i))
-
     def emit():
         total = {m: sum(ops[i][4] for i in l) for m, l in group.items()}
         count, clock = [0] * len(ops), [None] * len(ops)
-        for i in order():
+        for i in ([int(k) for k in ORDER.split()] or range(len(ops))):
             q, fn, deps, sem, n = ops[i][:5]
             if q == "a":
                 count[i], clock[i] = n, {}
@@ -209,11 +114,10 @@ def program(g, core, T, topo):
                 count[i] = cnt[sem]
             clock[i] = dict(kn)
 
-    def R(n, a=0, b=None, s=1, p=None):
+    def R(n, a=0, b=None, s=1):
         n, base, w = PIECE.get(n, (n, 0, SCRATCH[n][1][1] if n in SCRATCH else 0))
         a, b = base + a, base + (w if b is None else b)
-        c = slice(a, b) if s == 1 else slice(a, b, s)
-        ap = T[n][:, c] if p is None else T[n][0:p, c]
+        ap = T[n][:, slice(a, b) if s == 1 else slice(a, b, s)]
         if SCRATCH[n][0] == "psum":
             return ap, [(n, 0, 512, 1)]
         return ap, [(n, a, b, s)]
@@ -254,8 +158,9 @@ def program(g, core, T, topo):
               (0.05 + us(width(o), 1.5)) if len(a[1]) > 1 else us(width(o), 1 if a[1][0][0][:2] == "bk" else 2))
 
     def cp(o, i, n=None):
-        issue("v", lambda: g.vector.tensor_copy(o[0], i[0]), i[1] + o[1][1:], o[1][:1], "qv", 1,
-              (0.05 + us(width(i), 3.5)) if len(o[1]) > 1 else (0.05 + us(width(o), 1.5)) if len(i[1]) > 1 else us(width(o), half(o, i)))
+        n = n or width(o)
+        issue("v", lambda: g.vector.tensor_copy(o[0], i[0]), i[1], o[1], "qv", 1,
+              (0.05 + us(n, 1.5)) if len(i[1]) > 1 else us(n, half(o, i)))
 
     def fill(o, c):
         issue("v", lambda: g.vector.memset(o[0], c), [], o[1], "qv", 1, us(width(o), half(o)))
@@ -263,17 +168,14 @@ def program(g, core, T, topo):
     def red(o, i):
         issue("v", lambda: g.vector.tensor_reduce(o[0], i[0], AxisListType.X, OP.add), i[1], o[1], "qv", 1, us(width(i)))
 
-    def scan(o, a, b, op0, op1):
-        issue("v", lambda: g.vector.tensor_tensor_scan(o[0], a[0], b[0], 0.0, op0, op1), a[1] + b[1], o[1], "qv", 1, us(width(o), half(o, a)))
-
-    def tr(o, i):
-        issue("v", lambda: g.vector.transpose(o[0], i[0]), i[1], o[1], "qv", 1, us(width(o), half(o)))
+    def scan(o, a, b, op0, op1, init=0.0):
+        issue("v", lambda: g.vector.tensor_tensor_scan(o[0], a[0], b[0], init, op0, op1), a[1] + b[1], o[1], "qv", 1, us(width(o), half(o, a)))
 
     def qz(c, s, i):
         issue("v", lambda: g.vector.quantize_mx(c[0], s[0], i[0]), i[1], c[1] + s[1], "qv", 1, 0.02 + width(i) * 0.26e-3)
 
-    def act(o, i, f=AF.Copy, bias=None, scale=None, accum=None):
-        kw, rd, wr = {}, list(i[1]), list(o[1])
+    def act(o, i, f=AF.Copy, bias=None, scale=None, accum=None, lock=(), n=None):
+        kw, rd, wr = {}, list(i[1]), list(o[1]) + list(lock)
         if bias is not None:
             kw["bias"] = val(bias)[0]
             rd += val(bias)[1]
@@ -283,8 +185,9 @@ def program(g, core, T, topo):
         if accum is not None:
             kw["accum_out"] = accum[0]
             wr += accum[1]
+        n = n or width(o)
         issue("s", lambda: g.scalar.activation(o[0], i[0], f, **kw), rd, wr, "qs", 1,
-              (0.08 + us(width(o), 1.5)) if len(i[1]) > 1 else 0.03 + us(width(o)))
+              (0.08 + us(n, 1.5)) if len(i[1]) > 1 else 0.03 + us(n))
 
     def mm(o, lc, ls, rc, rs, start=True, stop=True):
         issue("t", lambda: g.tensor.matmul_mx(o[0], lc[0], ls[0], rc[0], rs[0], start, stop),
@@ -293,60 +196,54 @@ def program(g, core, T, topo):
     def iota(o, pat, base, cm):
         issue("p", lambda: g.iota(o[0], pat, base, cm, allow_small_or_imprecise_dtypes=True), [], o[1], "qp", 1, 0.13 + us(width(o), 2))
 
-    def one(o, i, b):
-        issue("p", lambda: g.affine_select(o[0], i[0], [[-1, 512]], OP.is_equal, 0.0, b, 4), i[1], o[1], "qp", 1, 0.17 + us(width(o), 2))
+    def resets(o, a, b):
+        issue("p", lambda: g.affine_select(o[0], T.ones[:, 0:a * b], [[0, a], [1, b]], OP.not_equal, 0.0, 0, 0), R("ones", 0, a * b)[1], o[1], "qp", 1,
+              0.17 + us(a * b, 2))
+
+    def pickout(o, i, base, cm):
+        issue("p", lambda: g.affine_select(o[0], i[0], [[-1, width(o)]], OP.is_equal, 0.0, base, cm), i[1], o[1], "qp", 1, 0.17 + us(width(o), 2))
+
+    def sfill(o, c):
+        act(o, R("one", 0, width(o)), AF.Copy, scale=c)
 
     def dma(q, sem, out, i):
         issue(q, lambda: Q[q].dma_start(out[0], i[0]), i[1], out[1], sem, 16, 0.07, 2.5)
 
-    runs = []
+    for gr in range(8):
+        dma("ys"[gr % 2], "lnb", (T.nbw[16 * gr:16 * gr + 16, :], [("nbw", 0, 48, 1)] if gr == 0 else []), (T.nb[:, :], []))
+    dma("s", "lx", R("xt"), (T.x[:, :], []))
+    dma("s", "lx2", R("P1", 72, 520), (T.x[:, 0:448], []))
+    first = True
     for k in range(3):
         i = 0
         while i < 16:
-            a = (3 * i + k) % 16
+            a, o = (3 * i + k) % 16, (3 * i + k) // 16
             n = min((15 - a) // 3 + 1, 16 - i)
-            runs.append((k, i, n, T.nb[a:a + 3 * (n - 1) + 1:3, (3 * i + k) // 16:(3 * i + k) // 16 + 46]))
-            i += n
+            dma("y", "lst", (T.nst[i:i + n, 46 * k:46 * k + 46], [("nst", 0, 138, 1)] if first else []),
+                (T.nb[a:a + 3 * (n - 1) + 1:3, o:o + 46], []))
+            i, first = i + n, False
     for gr in range(8):
-        for j, (k, i, n, src) in enumerate(u for u in runs if u[0] == 2):
-            dma("ys"[(3 * gr + j) % 2], "lnb", (T.nb2[16 * gr + i:16 * gr + i + n, 0:46], [("nb2", 0, 48, 1)] if gr + i == 0 else []), (src, []))
-    dma("y", "lx", R("xt"), (T.x[:, :], []))
-    for h in range(2):
-        dma("y", "lx2", R("pm", 512 * h + 64, 512 * h + 512), (T.x[:, 0:448], []))
-    for k, i, n, src in runs:
-        if k < 2:
-            dma("s", "lst", (T.nst[i:i + n, 46 * k:46 * k + 46], [("nst", 0, 92, 1)] if i + k == 0 else []), (src, []))
-    for gr in range(8):
-        dma("y", "lnn", (T.nn[16 * gr:16 * gr + 16, :], [("nn", 0, 92, 1)] if gr == 0 else []), (T.nst[:, :], [("nst", 0, 92, 1)]))
+        dma("y", "lnn", (T.nn[16 * gr:16 * gr + 16, :], [("nn", 0, 138, 1)] if gr == 0 else []), (T.nst[:, :], [("nst", 0, 138, 1)]))
+    for b, lo, hi in (("P2", 256, 640), ("U0", 128, 576), ("U1", 320, 576)):
+        dma("y", "lx3", R(b, lo, hi), (T.x[:, 0:hi - lo], []))
     dma("y", "lw", R("wt"), (T.w[:, :], []))
-    n2 = R("nb2", 0, 46, 3)
-    nl = [R("nn", 46 * k, 46 * k + 46, 3) for k in range(2)] + [n2]
+    nl = [R("nn", 46 * k, 46 * k + 46, 3) for k in range(3)]
 
     iota(R("pp", 0, 1), [[0, 1]], 0, 1)
-    iota(R("iob"), [[1, 256]], 0, 0)
-    iota(R("tk"), [[1, 16]], 0, 0)
-    iota(R("tb"), [[32, 8], [0, 2]], 0, 0)
+    iota(R("pp", 1, 2), [[0, 1]], 10, 11)
     iota(R("k3"), [[0, 16], [1, 3]], 0, 0)
-    iota(R("rowc"), [[0, 8], [2, 16]], -255, 0)
-    iota(R("j64"), [[0, 4], [1, 16]], 0, 0)
+    iota(R("t48"), [[16, 16], [0, 3]], 256 * r, 0)
+    iota(R("g24"), [[0, 2], [1, 8], [0, 3]], 0, 0)
+    iota(R("rowd"), [[0, 8], [2, 16]], 0, 0)
     iota(R("g48"), [[0, 6], [1, 8]], 0, 0)
-    iota(R("cmp"), [[1, 128]], 0, -1)
-    iota(R("tk32"), [[0, 2], [1, 16]], 0, 0)
-    iota(R("d8"), [[0, 2], [1, 4]], 0, 0)
-    iota(R("io32"), [[1, 32]], 0, 0)
     iota(R("rowb"), [[0, 16], [1, 16]], 0, 0)
-    fill(R("hf"), 0.5)
-    fill(R("kr", 256, 264), -255.0)
-    fill(R("pm", 512, 576), 0.0)
-    act(R("u0"), R("hf"), AF.Copy, scale=0.0)
-    act(R("u1"), R("hf"), AF.Copy, scale=0.0)
-    for t in range(2):
-        act(R("ve", 512 * t, 512 * t + 512), R("hf"), AF.Copy, scale=0.0)
-    for b in range(NK // 256):
-        if b % 3 == 1:
-            act(R("tab", 256 * b, 256 * b + 256), R("iob"), AF.Copy, bias=256.0 * (b - 1 - r))
-        else:
-            ts(R("tab", 256 * b, 256 * b + 256), R("iob"), 256.0 * (b - 1 - r), OP.add)
+    iota(R("j64"), [[0, 4], [1, 16]], 0, 0)
+    iota(R("d8"), [[0, 2], [1, 4]], 0, 0)
+    iota(R("tab", 1792, 2304), [[1, 512]], 1792, 0)
+    fill(R("one", 0, 256), 1.0)
+    scan(R("iob"), R("one", 0, 256), R("one", 0, 256), OP.add, OP.mult, -1.0)
+    fill(R("one", 256, 516), 1.0)
+    act(R("ones"), R("one", 0, 128))
 
     def c(k):
         return R("ci", k, k + 1)
@@ -356,77 +253,104 @@ def program(g, core, T, topo):
 
     def col2(k):
         return R("col2", k, k + 1)
+    ts(c(3), R("pp", 1, 2), 15, OP.bitwise_and)
+    ts(c(4), c(3), 3, OP.mult, 2, OP.add)
+    ts(c(5), c(4), 4, OP.arith_shift_right)
     ts(c(0), R("pp", 0, 1), 15, OP.bitwise_and)
     ts(c(1), R("pp", 0, 1), 4, OP.arith_shift_right)
     ts(c(2), R("pp", 0, 1), 5, OP.arith_shift_right)
-    ts(c(3), R("pp", 0, 1), 4, OP.arith_shift_right, 1, OP.bitwise_and)
-    cp(R("col"), R("ci"))
-    act(R("jl"), R("tk"), AF.Identity, bias=col(0), scale=16.0)
-    act(R("gl"), R("jl"), AF.Copy, bias=256.0 * r)
-    act(R("jw"), R("jl"), AF.Copy, bias=256.0)
-    act(R("z", 2, 48, 3), R("jl"))
-    act(col2(0), col(3), AF.Copy, bias=1.0, scale=-1.0)
-    act(col2(1), col(3), AF.Identity, bias=col(0), scale=16.0)
-    act(col2(3), col(1), AF.Copy, bias=8.0)
-    act(col2(4), col(0), AF.Copy, scale=2.0)
-    act(col2(5), col(0), AF.Copy, bias=1.0, scale=2.0)
-    ts(R("dup", 0, 16), R("tb"), col2(1), OP.add)
-    ts(R("tkc"), R("tk"), 32.0, OP.mult, RND, OP.add)
+    cp(R("col", 0, 6), R("ci"))
+    ts(R("mk48"), R("k3"), col(5), OP.is_equal)
+    ts(R("gmt"), R("g24"), col(1), OP.is_equal)
+    ts(R("rs3"), R("k3"), 0.0, OP.not_equal)
+    fill(R("rs24"), 1.0)
+    fill(R("rs24", 0, 48, 24), 0.0)
+    act(R("gl48"), R("t48"), AF.Identity, bias=col(3))
+    act(R("own48"), R("gl48"), AF.Copy, bias=256.0 * (1 - r))
+    for b in range(7):
+        if b % 2:
+            act(R("tab", 256 * b, 256 * b + 256), R("iob"), AF.Copy, bias=256.0 * b)
+        else:
+            ts(R("tab", 256 * b, 256 * b + 256), R("iob"), 256.0 * b, OP.add)
+    act(R("rowc"), R("rowd"), AF.Copy, bias=-255.0)
+    act(R("tkc", 0, 16), R("iob", 0, 16), AF.Copy, bias=RND - 64.0 * r, scale=32.0)
+    ts(R("tkw"), R("iob", 0, 16), 2.0 * r, OP.is_lt, 512.0, OP.mult)
+    tt(R("tkc", 0, 16), R("tkc", 0, 16), R("tkw"), OP.add)
+    for k in range(2):
+        act(R("tkc", 16 + k, 17 + k), R("iob", 2 * r + 1 - k, 2 * r + 2 - k), AF.Copy, bias=RND, scale=32.0)
     for h in range(2):
         act(R("nv", 2 * h, 2 * h + 1), col(1), AF.Copy, bias=128.0 * h, scale=16.0)
-        act(R("nv", 2 * h + 1, 2 * h + 2), col(0), AF.Copy)
+        act(R("nv", 2 * h + 1, 2 * h + 2), col(3), AF.Copy)
     ts(R("gm"), R("g48"), col(1), OP.is_equal)
-    ts(R("rs8"), R("g48"), 0.0, OP.not_equal)
-    ts(R("rs16"), R("j64"), 0.0, OP.not_equal)
+    resets(R("rs8"), 6, 8)
+    resets(R("rs16"), 4, 16)
     ts(R("dm"), R("j64"), col(0), OP.is_equal)
+    act(R("jl"), R("iob", 0, 16), AF.Identity, bias=col(0), scale=16.0)
+    act(R("jw"), R("jl"), AF.Copy, bias=256.0)
+    act(R("z", 2, 48, 3), R("jl"))
+    act(col2(0), col(1), AF.Copy, bias=8.0)
+    act(col2(1), col(0), AF.Copy, scale=2.0)
+    act(col2(2), col(0), AF.Copy, bias=1.0, scale=2.0)
+    sfill(R("P1", 520, 584), 0.0)
+    for h in range(2):
+        act(R("P1", 522 + 30 * h, 552 + 32 * h, 4), R("gm", 0, 8), AF.Copy, scale=64.0 * r)
+    act(R("sqa"), R("rowb", 0, 128), AF.Square, bias=col(3), scale=-1.0)
     for e in range(4):
-        ts(R("pa", 512 + e, 1024, 4), R("rowb", 0, 128), col(0), OP.is_equal)
+        act(R("pa", 512 + e, 1024, 4), R("sqa"), AF.Relu, bias=1.0, scale=-1.0)
     qz(R("pac", 128, 256), R("pas", 128, 256), R("pa", 512, 1024))
 
-    ts(R("ka"), n2, 256 * r, OP.bitwise_and)
-    ts(R("kb"), n2, 1792 - 256 * r, OP.bitwise_and)
-    tt(R("km"), n2, R("gl"), OP.min)
-    tt(R("klow"), n2, R("gl"), OP.is_gt)
-    ts(R("kt"), n2, 256.0 * (r + 1), OP.is_lt, -256.0, OP.mult)
-    ts(R("ki"), R("km"), 255, OP.bitwise_and)
-    tt(R("kx"), R("kb"), R("ka"), OP.subtract)
-    tt(R("kl"), R("kt"), R("klow"), OP.mult)
-    tt(R("k2"), R("ki"), R("kl"), OP.add)
-    tt(R("kf"), R("k2"), R("kx"), OP.add)
-    ts(R("ku"), R("kf"), 256.0 * (r + 1), OP.add)
-    tt(R("kcm", 0, 16), R("kf"), R("gm", 0, 16), OP.mult)
-    scan(R("kcm", 16, 32), R("rs8", 0, 16), R("kcm", 0, 16), OP.mult, OP.add)
-    act(R("jk"), ind(R("tab"), R("ku")), AF.Sign, bias=R("kcm", 23, 24), scale=-1.0, accum=R("ss", 0, 1))
-    ts(R("kr", 0, 256), ind(R("tab"), R("ku")), R("kcm", 31, 32), OP.is_lt, 2.0, OP.mult)
-    red(R("ss", 1, 2), R("kr", 0, 257))
+    tt(R("n2m"), R("nbw"), R("mk48"), OP.mult)
+    ts(R("hi"), R("nbw"), 1792, OP.bitwise_and)
+    tt(R("kw"), R("n2m"), R("gl48"), OP.is_gt)
+    tt(R("xa"), R("hi"), R("own48"), OP.add)
+    tt(R("xm"), R("kw"), R("xa"), OP.mult)
+    tt(R("kf"), R("n2m"), R("xm"), OP.max)
+    tt(R("km"), R("kf"), R("gmt"), OP.mult)
+    scan(R("ks"), R("rs3"), R("kf"), OP.mult, OP.add)
+    scan(R("kc"), R("rs24"), R("km"), OP.mult, OP.add)
+    cp(R("ku"), R("ks", 2, 48, 3))
+    act(R("jk"), ind(R("tab"), R("ku")), AF.Sign, bias=R("kc", 23, 24), scale=-1.0, accum=R("ss", 0, 1))
+    ts(R("kr"), ind(R("tab"), R("ku")), R("kc", 47, 48), OP.is_lt, 2.0, OP.mult)
+    scan(R("krs"), R("kr"), R("kr"), OP.add, OP.max)
+    p2 = [R("ss", 0, 1), R("krs", 255, 256)]
+    rw = [R("rowc"), R("rowd")]
+    hi2 = [R("ph", 2, 3), R("phb", 0, 1)]
     for h in range(2):
-        ts(R("ph", h, h + 1), R("ss", h, h + 1), 240.0, OP.add, RND, OP.add)
-        ts(R("ph", 2 + h, 3 + h), R("ph", h, h + 1), -RND, OP.add)
+        ts(R("ph", h, h + 1), p2[h], -15.0 if h else 240.0, OP.add, RND, OP.add)
+        ts(hi2[h], R("ph", h, h + 1), -RND, OP.add)
     for e in range(4):
-        ts(R("pm", e, 64, 4), R("tkc"), R("ph", e // 2, e // 2 + 1), OP.is_equal, R("nv", e, e + 1), OP.mult)
-    qz(R("pmc", 0, 128), R("pms", 0, 128), R("pm", 0, 512))
+        ts(R("P1", e, 72, 4), R("tkc"), R("ph", e // 2, e // 2 + 1), OP.is_equal, R("nv", e, e + 1), OP.mult)
+    qz(R("pmc", 0, 128), R("pms", 0, 128), R("P1", 0, 512))
     for e in range(4):
-        ts(R("pa", e, 512, 4), R("rowc"), R("ph", 2 + e // 2, 3 + e // 2), OP.add, R("ss", e // 2, e // 2 + 1), OP.is_equal)
+        ts(R("pa", e, 512, 4), rw[e // 2], hi2[e // 2], OP.add, p2[e // 2], OP.is_equal)
     qz(R("pac", 0, 128), R("pas", 0, 128), R("pa", 0, 512))
     mm(R("bk6", 0, 128), R("pac", 0, 128), R("pas", 0, 128), R("pmc", 0, 128), R("pms", 0, 128))
-    cp(R("l18", 0, 16), R("bk6", 0, 16))
-    cp(R("nlst"), R("bk6", 0, 16))
-    cp(R("l18", 16, 17), R("nlst", 1, 2))
-    cp(R("l18", 17, 18), R("nlst", 0, 1))
+    cp(R("l18"), R("bk6", 0, 18))
+    ts(R("lo", 0, 1), p2[0], 255.0, OP.add, hi2[0], OP.subtract)
+    ts(R("lo", 1, 2), p2[1], hi2[1], OP.subtract)
     for h in range(2):
-        ts(R("lo", h, h + 1), R("ss", h, h + 1), 255.0, OP.add, R("ph", 2 + h, 3 + h), OP.subtract)
-        a = 512 + 34 * h
-        act(R("pm", a, 544 + 32 * h, 4), R("gm", 0, 8), AF.Copy, scale=R("ph", 2 + h, 3 + h))
-        act(R("pm", a + 1, 544 + 32 * h, 4), R("gm", 0, 8), AF.Copy, scale=R("lo", h, h + 1))
-    qz(R("pmc", 128, 256), R("pms", 128, 256), R("pm", 512, 1024))
+        ts(R("wr", h, h + 1), p2[h], 257.0 + 255 * h - 64 * r, OP.is_ge, -512.0, OP.mult)
+    for h in range(2):
+        a = 520 + 34 * h
+        if h == 0:
+            act(R("P1", a, 552, 4), R("gm", 0, 8), AF.Copy, scale=hi2[0])
+        else:
+            ts(R("P1", a, 584, 4), R("gm", 0, 8), hi2[1], OP.mult)
+        act(R("P1", a + 1, 552 + 32 * h, 4), R("gm", 0, 8), AF.Copy, scale=R("lo", h, h + 1))
+        act(R("P1", 523 + 30 * h, 552 + 32 * h, 4), R("gm", 0, 8), AF.Copy, scale=R("wr", h, h + 1))
+    qz(R("pmc", 128, 256), R("pms", 128, 256), R("P1", 72, 584))
     mm(R("bk5", 0, 128), R("pac", 128, 256), R("pas", 128, 256), R("pmc", 128, 256), R("pms", 128, 256))
-    ts(R("pl"), R("bk5", 0, 16), 0.5, OP.mult)
+    ts(R("pl"), R("bk5", 112, 128), 0.5, OP.mult)
+    act(R("z", 98, 144, 3), R("bk5", 112, 128), AF.Copy, scale=0.5, lock=R("bk5")[1])
     act(R("posn"), ind(R("iob"), R("pl")))
     qz(R("q0c"), R("q0s"), R("xt"))
 
-    def pick(dc, ds, a, b, sc, ss, w0, w1, off):
-        cp(W32(R(dc, a, b)), ind(W32(R(sc, w0, w1)), off))
-        act(R(ds, a, b), ind(R(ss, w0, w1), off))
+    def pick(dc, ds, a, b, sc, ss, w0, w1, off, own=False):
+        oc, os = R(dc, a, b), R(ds, a, b)
+        if own:
+            oc, os = (oc[0], [(dc, 0, 256, 1)]), (os[0], [(ds, 0, 256, 1)])
+        cp(W32(oc), ind(W32(R(sc, w0, w1)), off), b - a)
+        act(os, ind(R(ss, w0, w1), off), n=b - a)
 
     others = [d for d in range(1, 8)]
     far = [d for d in others if topo.die(T.cores[r ^ d]) != topo.die(core)]
@@ -443,7 +367,7 @@ def program(g, core, T, topo):
             for d in others:
                 ad = topo.addr(T.cores[r ^ d])
                 tf.append(RemoteDMATransfer(dst_ids=[DstId(rid=ad[0], pnc=ad[1])], dma_engine_mask=sum(1 << e for e in lanes[d]),
-                                            remote_sem=T.sem[sem], src=srcs(d), dst=dsts(d)))
+                                            remote_sem=T.sem[sem], src=srcs(blk[r ^ d]), dst=dsts(blk[r ^ d])))
             g.remote_dma_fused(tf, local_sem=T.sem.loc)
             cnt["loc"] = cnt.get("loc", 0) + 14
         me = issue("p", call, [(b, lo, hi, 1) for b, lo, hi in regs], [], None, 1, 0.7, 0.7)
@@ -454,12 +378,12 @@ def program(g, core, T, topo):
         acc.setdefault(b, []).append((lo, hi, 1, True, group[sem][0]))
 
     def send_w(bc, bs, sem):
-        send(lambda d: T[bc][:, 256 + 32 * d:288 + 32 * d].bitcast(dt.uint8), lambda d: T[bc][:, 32 * d:32 * d + 32].bitcast(dt.uint8),
+        send(lambda q: T[bc][:, 256 + 32 * q:288 + 32 * q].bitcast(dt.uint8), lambda q: T[bc][:, 32 * q:32 * q + 32].bitcast(dt.uint8),
              sem, [(bc, 256, 512)])
-        send(lambda d: T[bs][:, 256 + 32 * d:288 + 32 * d], lambda d: T[bs][:, 32 * d:32 * d + 32], sem, [(bs, 256, 512)])
+        send(lambda q: T[bs][:, 256 + 32 * q:288 + 32 * q], lambda q: T[bs][:, 32 * q:32 * q + 32], sem, [(bs, 256, 512)])
 
-    def bank(k, n):
-        return R("bk%d" % k, 0, n)
+    def bank(k, n, a=0):
+        return R("bk%d" % k, a, a + n)
 
     def gram(bc, bs, mc, ms, m0):
         mm(bank(0, 256), R(bc, 256, 384), R(bs, 256, 384), R(mc, m0, m0 + 256), R(ms, m0, m0 + 256))
@@ -477,39 +401,35 @@ def program(g, core, T, topo):
         mm(bank(BK[h][b], w), R("eqc", 128 * b, 128 * b + 128), R("eqs", 128 * b, 128 * b + 128),
            R(cc, a + 128 * h, a + 128 * h + w), R(cs, a + 128 * h, a + 128 * h + w), start, not start)
 
-    def diagonal(o, i, off):
-        tt(R("xg"), ind(i, off), R("dm"), OP.mult)
-        scan(o, R("rs16"), R("xg"), OP.mult, OP.add)
+    def diagonal(o, x, i, off):
+        tt(x, ind(i, off), R("dm"), OP.mult)
+        scan(o, R("rs16"), x, OP.mult, OP.add)
 
     def local_scores(t):
         for h in range(2):
             tt(R("gg", 32 * h, 32 * h + 32), ind(R("gs", 264 * h, 264 * h + 264), R("xoa" if t else "xo", 2 * h, 2 * h + 2)), R("dm", 0, 32), OP.mult)
         scan(R("sc"), R("rs16"), R("gg"), OP.mult, OP.add)
         s0, s1 = R("sc", 15, 64, 32), R("sc", 31, 64, 32)
-        m, ma = "m%d" % t, "ma%d" % t
+        m, ma, mx = "m%d" % t, "ma%d" % t, "mx%d" % t
         for h in range(2):
             ts(R(ma, 4 * h, 4 * h + 4), R("msk", 4 * h, 4 * h + 4), R("sc", 15 + 32 * h, 16 + 32 * h), OP.max, R("sc", 31 + 32 * h, 32 + 32 * h), OP.max)
-        send(lambda d: T[ma][:, d:d + 1], lambda d: T["mx%d" % t][:, d:d + 1], "e%d" % t, [(ma, 0, 8)])
+        send(lambda q: T[ma][:, q:q + 1], lambda q: T[mx][:, q:q + 1], "e%d" % t, [(ma, 0, 8)])
+        b = 32 * (lb % 4)
+        rest = [(0, b), (b + 32, 128)] if 0 < b < 96 else [(32 - b // 3, 64), (64, 128 - b // 3)]
+        for i, (lo, hi, to) in enumerate([(b, b + 16, b + 16), (b + 16, b + 32, b)] + [(lo, hi, lo) for lo, hi in rest]):
+            dma("y", "lm%d" % t, (T[mx][to:to + hi - lo, lb:lb + 1], [(mx, 0, 8, 1)] if i == 0 else []), (T[ma][lo:hi, lb:lb + 1], [(ma, 0, 8, 1)]))
         tt(R(m), s0, s1, OP.max)
         tt(R("sm", 0, 2), s0, s1, OP.is_ge)
-        act(R("sm", 2, 4), R("sm", 0, 2), AF.Copy, bias=-4e29, scale=4e29)
-        act(R("sm", 4, 6), R("sm", 0, 2), AF.Copy, scale=-4e29)
-        tt(R("sm", 8, 12, 2), s0, R("sm", 2, 4), OP.add)
-        tt(R("sm", 9, 12, 2), s1, R("sm", 4, 6), OP.add)
-        ts(R("lm", 0, 32), R("p32"), R(m, 0, 1, 1, 32), OP.mult)
-        tr(R("lm", 32, 64), R("lm", 0, 32))
-        red(R("lmm", 0, 1, 1, 32), R("lm", 32, 64))
-        if t == 1:
-            for k in range(2):
-                tt(R("sm", 8 + k, 12, 2), R("sm", 8 + k, 12, 2), R("pen", 4, 6), OP.add)
-            tt(R(m), R(m), R("pen", 4, 6), OP.add)
+        act(R("sm", 2, 6, 2), R("sm", 0, 2), AF.Copy, bias=-4e29, scale=4e29)
+        act(R("sm", 3, 6, 2), R("sm", 0, 2), AF.Copy, scale=-4e29)
+        tt(R("sm", 8, 12), R("sc", 15, 64, 16), R("sm", 2, 6), OP.add)
 
     def statics(t, hi_own, hl):
         for h in range(2):
             a = 128 * t + 64 * h
-            act(R("mn", a, a + 64, 2), R("tk32"), AF.Square, bias=hi_own[h], scale=-1.0)
+            act(R("mn", a, a + 64, 2), R("j64", 0, 32), AF.Square, bias=hi_own[h], scale=-1.0)
             for k in range(2):
-                act(R("mn", a + 32 * k + 1, a + 32 * k + 32, 2), R("tk"), AF.Square, bias=R("hl", hl + 2 * h + k, hl + 2 * h + k + 1), scale=-1.0)
+                act(R("mn", a + 32 * k + 1, a + 32 * k + 32, 2), R("j64", 0, 16), AF.Square, bias=R("hl", hl + 2 * h + k, hl + 2 * h + k + 1), scale=-1.0)
             act(R("nat", 32 * t + 16 * h, 32 * t + 16 * h + 16), R("mn", a, a + 32, 2), AF.Relu, bias=0.0625, scale=-0.0625)
         for h in range(2):
             for k in range(2):
@@ -518,55 +438,60 @@ def program(g, core, T, topo):
                     bias=R("sm", 8 + 2 * h + k, 9 + 2 * h + k), scale=-8e29)
 
     def weights(t, lo_own, hl):
+        if t == 0:
+            act(R("sqb"), R("rowb"), AF.Square, bias=col(0), scale=-1.0)
         for h in range(2):
-            ts(R("ct", 1024 * t + h, 1024 * t + 1024, 4), R("rowb"), lo_own[h], OP.is_equal, BIG, OP.mult)
+            if t == 0:
+                act(R("ct", h, 1024, 4), R("sqb"), AF.Relu, bias=BIG, scale=-BIG)
+            else:
+                ts(R("ct", 1024 * t + h, 1024 * t + 1024, 4), R("rowb"), lo_own[h], OP.is_equal, BIG, OP.mult)
             for k in range(2):
                 a = 1024 * t + 512 * k
-                ts(R("ct", a + 2 + h, a + 512, 4), R("rowb", 0, 128), R("hl", hl + 4 + 2 * h + k, hl + 5 + 2 * h + k), OP.is_equal, BIG, OP.mult)
+                ts(R("ct", a + 2 + h, a + 512, 4), R("rowb", 0, 128), R("hl", hl + 2 * h + k, hl + 1 + 2 * h + k), OP.is_equal, BIG, OP.mult)
         qz(R("cqc", 256 * t, 256 * t + 256), R("cqs", 256 * t, 256 * t + 256), R("ct", 1024 * t, 1024 * t + 1024))
 
-    def flags_times(t, k, b, uq):
+    def flags_times(t, k, b, qc, qs, uq):
         ca = 256 * t + 128 * k
-        mm(bank(b, 128), R("cqc", ca, ca + 128), R("cqs", ca, ca + 128), R("uqc", uq, uq + 128), R("uqs", uq, uq + 128))
+        mm(bank(b, 128), R("cqc", ca, ca + 128), R("cqs", ca, ca + 128), R(qc, uq, uq + 128), R(qs, uq, uq + 128))
 
     def choose(t, bc, bs):
-        u, uq, z, xl = "u%d" % t, 128 * t, 96 * t, "xl%d" % t
-        arrive("a%d" % t, bc, 32, 256)
-        arrive("a%d" % t, bs, 32, 256)
+        u, uq, z, xl = "U%d" % t, 128 * t, 96 * t, "xl%d" % t
+        arrive("a%d" % t, bc, 0, 256)
+        arrive("a%d" % t, bs, 0, 256)
         for h in range(2):
             mm(bank(2 + h, 128), R(bc, 256 + 128 * h, 384 + 128 * h), R(bs, 256 + 128 * h, 384 + 128 * h),
                R(bc, 128 * h, 128 * h + 128), R(bs, 128 * h, 128 * h + 128))
         for h in range(2):
-            tt(R("xd", 128 * h, 128 * h + 128), bank(2 + h, 128), R("idn"), OP.mult)
-        act(R("jk", 0, 128), R("xd", 0, 128), AF.Identity, accum=R("sm", 16, 17))
-        red(R("sm", 17, 18), R("xd", 128, 256))
+            tt(R("xd", 129 * h, 129 * h + 128), bank(2 + h, 128), R("idn"), OP.mult)
+        act(R("jk", 0, 128 + t), R("xd", 0, 128 + t), AF.Identity, accum=R("sm", 16, 17))
+        red(R("sm", 17, 18), R("xd", 129, 257 + t))
         for h in range(2):
             ts(R(u, h, 128, 2), R("mq", 64 * h, 64 * h + 64), R("sm", 16 + h, 17 + h), OP.is_ge)
-        qz(R("uqc", uq, uq + 128), R("uqs", uq, uq + 128), R(u))
+        qz(R("uqc", uq, uq + 128), R("uqs", uq, uq + 128), R(u, 0, 512))
         for k in range(2):
-            flags_times(t, k, 2 + k, uq)
+            flags_times(t, k, 2 + k, "uqc", "uqs", uq)
         for k in range(2):
-            tt(R("z", z + k, z + 48, 3), R("bk%d" % (2 + k), 16 * k, 16 * k + 16), R(xl, 16 * k, 16 * k + 16), OP.add)
+            tt(R("z", z + k, z + 48, 3), bank(2 + k, 16, 16 * k), R(xl, 16 * k, 16 * k + 16), OP.add)
         scan(R("z", z + 48, z + 96), R("rs3"), R("z", z, z + 48), OP.mult, OP.max)
         cp(R("lp", 16 * t, 16 * t + 16), R("z", z + 50, z + 96, 3))
 
     def decide(t):
-        mx, v = "mx%d" % t, 512 * t
+        mx, u = "mx%d" % t, "U%d" % t
         arrive("e%d" % t, mx, 0, 8)
-        for a, b, i in ((0, 1, R("lmm")), (1, 4, R(mx, 1, 4)), (4, 8, R(mx, 4, 8))):
-            ts(R("ofx", a, b), i, R("sm", 16 + a // 4, 17 + a // 4), OP.is_lt, col2(4), OP.add)
         for h in range(2):
-            act(R("jk", 128 + 64 * h, 192 + 64 * h), ind(R("dw"), R("ofx", 4 * h, 4 * h + 4)), AF.Copy, accum=R("sm", 20 + h, 21 + h))
+            ts(R("ofx", 4 * h, 4 * h + 4), R(mx, 4 * h, 4 * h + 4), R("sm", 16 + h, 17 + h), OP.is_lt, col2(1), OP.add)
+        for h in range(2):
+            act(R("jq", 64 * h, 64 * h + 64), ind(R("dw"), R("ofx", 4 * h, 4 * h + 4)), AF.Copy, accum=R("sm", 20 + h, 21 + h))
         tt(R("sm", 22, 24), R("sm", 16, 18), R("m%d" % t), OP.is_gt)
         for h in range(2):
-            ts(R("ve", v + h, v + 64, 4), R("nat", 32 * t + 16 * h, 32 * t + 16 * h + 16), R("sm", 20 + h, 21 + h), OP.mult, R("sm", 22 + h, 23 + h), OP.mult)
+            ts(R(u, 576 + h, 640, 4), R("nat", 32 * t + 16 * h, 32 * t + 16 * h + 16), R("sm", 20 + h, 21 + h), OP.mult, R("sm", 22 + h, 23 + h), OP.mult)
         vq = 256 + 128 * t
-        qz(R("uqc", vq, vq + 128), R("uqs", vq, vq + 128), R("ve", v, v + 512))
-        flags_times(t, 0, 7, vq)
+        qz(R("uqc", vq, vq + 128), R("uqs", vq, vq + 128), R(u, 128, 640))
+        flags_times(t, 0, 7, "uqc", "uqs", vq)
         a = 48 * t
         ts(R("lnf", a, a + 16), R("z", 96 * t + 50, 96 * t + 96, 3), 256.0, OP.is_ge, 256.0, OP.mult)
         tt(R("lnf", a + 16, a + 32), R("lnf", a, a + 16), R("jl" if t else "jw"), OP.add)
-        tt(R("lnf", a + 32, a + 48), bank(7, 16), R("lnf", a + 16, a + 32), OP.add)
+        tt(R("lnf", a + 32, a + 48), bank(7, 16, 112), R("lnf", a + 16, a + 32), OP.add)
         cp(R("ln", 20 * t, 20 * t + 16), R("lnf", a + 32, a + 48))
 
     def own_parts(cc, cs, a):
@@ -585,113 +510,117 @@ def program(g, core, T, topo):
             for b in range(4):
                 oo = R("nt", 512 * h + b, 512 * h + 512, 4)
                 if b == 0:
-                    cp(oo, R("bk0", 128 * h, 128 * h + 128))
+                    ts(oo, R("bk0", 128 * h, 128 * h + 128), 0.5, OP.mult)
                 elif b == 2:
-                    cp(oo, bank(BK[h][b], 128))
+                    ts(oo, bank(BK[h][b], 128), 0.5, OP.mult)
                 else:
-                    act(oo, bank(BK[h][b], 128))
+                    act(oo, bank(BK[h][b], 128), AF.Copy, scale=0.5)
             qz(R(cc, base + 128 * h, base + 128 * h + 128), R(cs, base + 128 * h, base + 128 * h + 128), R("nt", 512 * h, 512 * h + 512))
+
+    def own_block(bc, bs, sc, ss, w, off):
+        pick(bc, bs, 32 * lb, 32 * lb + 32, sc, ss, 0, w, off, True)
 
     pick("b0c", "b0s", 256, 512, "q0c", "q0s", 0, 256, R("l18", 0, 16))
     send_w("b0c", "b0s", "a0")
-    pick("b0c", "b0s", 0, 32, "q0c", "q0s", 0, 256, R("l18", 16, 18))
+    own_block("b0c", "b0s", "q0c", "q0s", 256, R("l18", 16, 18))
     gram("b0c", "b0s", "q0c", "q0s", 0)
     for k in range(2):
         ts(R("o01", 16 * k, 16 * k + 16), nl[k], -256.0 * r, OP.add)
-        act(R("nr", 256 * k, 256 * k + 256), ind(R("iob"), R("o01", 16 * k, 16 * k + 16)))
-    ts(R("rs3"), R("k3"), 0.0, OP.not_equal)
-    tt(R("iv", 0, 16), R("nlst"), R("gm", 0, 16), OP.mult)
+    act(R("nr"), ind(R("iob"), R("o01")))
+    tt(R("iv", 0, 16), R("bk6", 0, 16), R("gm", 0, 16), OP.mult)
     scan(R("iv", 16, 32), R("rs8", 0, 16), R("iv", 0, 16), OP.mult, OP.add)
     inv = R("iv", 23, 32, 8)
     cp(R("of4", 0, 4, 2), inv)
     ts(R("of4", 1, 4, 2), inv, 256.0, OP.add)
-    diagonal(R("xi", 64, 128), R("nr"), R("of4"))
-    cp(R("xo"), R("xi", 79, 128, 16))
-    tt(R("p32a"), R("cmp", 0, 32, 1, 32), R("cmp", 0, 32, 1, 32), OP.mult)
-    ts(R("p32"), R("p32a"), 256.0, OP.is_equal)
-    fill(R("lmm"), 1e29)
+    diagonal(R("xi", 0, 64), R("xg"), R("nr"), R("of4"))
+    cp(R("xo"), R("xi", 15, 64, 16))
     for h in range(2):
-        fill(R("gs", 256 + 264 * h, 264 + 264 * h), -1e29)
+        sfill(R("gs", 256 + 264 * h, 264 + 264 * h), -1e29)
     ts(R("msk", 8, 16), R("d8"), col(2), OP.not_equal, 2e29, OP.mult)
     ts(R("msk", 0, 8), R("msk", 8, 16), -1e29, OP.add)
     local_scores(0)
+    diagonal(R("xi", 64, 128), R("xg2"), R("posn"), R("xo"))
+    cp(R("xi", 143, 160, 16), inv)
+    ts(R("xi", 160, 170), R("xi", 15, 160, 16), 4, OP.arith_shift_right)
+    ts(R("xi", 170, 180), R("xi", 15, 160, 16), 15, OP.bitwise_and)
+    cp(R("hl"), R("xi", 160, 180))
+    statics(0, [col(1), col2(0)], 4)
+    pickout(R("idn"), R("ones"), 0, 1)
+    ts(R("dw"), R("iob", 0, 32), col2(2), OP.is_equal)
+    weights(0, [col(0), col(0)], 14)
+    fill(R("P2", 0, 256), 0.0)
+    act(R("gms"), R("gm", 0, 8), AF.Copy, scale=1.0 / BIG)
     for k in range(2):
-        act(R("xr", 256 * k, 256 * k + 256), ind(R("posn"), R("o01", 16 * k, 16 * k + 16)))
-    diagonal(R("xi", 0, 64), R("xr"), R("of4"))
-    ts(R("xi", 128, 132), R("xi", 15, 64, 16), 4, OP.arith_shift_right)
-    ts(R("xi", 132, 136), R("xi", 15, 64, 16), 15, OP.bitwise_and)
-    cp(R("hl", 0, 8), R("xi", 128, 136))
-    statics(0, [col(1), col2(3)], 0)
-    ts(R("idn"), R("cmp"), 0.0, OP.is_equal)
-    ts(R("dw"), R("io32"), col2(5), OP.is_equal)
-    weights(0, [col(0), col(0)], 0)
-    act(R("ld", 0, 8), R("nlst", 0, 16, 2), AF.Copy, scale=col2(0))
-    act(R("ld", 8, 16), R("nlst", 1, 16, 2), AF.Copy, scale=col(3))
-    tt(R("ld", 16, 24), R("ld", 0, 8), R("ld", 8, 16), OP.add)
-    for k in range(2):
-        for w in range(2):
-            ts(R("ldu", 16 * k + w, 16 * k + 16, 2), R("ld", 16, 24), 256.0 * k, OP.add)
-    for k in range(2):
-        act(R("xlg", 256 * k, 256 * k + 256), ind(R("xr"), R("ldu", 16 * k, 16 * k + 16)))
+        for h in range(2):
+            a = 64 * k + 33 * h
+            ts(R("P2", a, 64 * k + 32 * h + 32, 4), R("gm", 0, 8), R("hl", 4 + 2 * h + k, 5 + 2 * h + k), OP.mult, 16.0 / BIG, OP.mult)
+            act(R("P2", a + 128, 64 * k + 32 * h + 160, 4), R("gms"), AF.Copy, scale=R("hl", 14 + 2 * h + k, 15 + 2 * h + k))
+    qz(R("pl2c", 0, 128), R("pl2s", 0, 128), R("P2", 0, 512))
+    flags_times(0, 0, 7, "pl2c", "pl2s", 0)
+    act(R("xlt", 0, 32), bank(7, 32, 32), AF.Copy, bias=256.0 - 2 * BIG)
+    tt(R("xl0"), bank(7, 32), R("xlt", 0, 32), OP.add)
+    pickout(R("et"), R("one"), 3, 4)
     for b in range(4):
-        one(R("et", 512 * b, 512 * b + 512), R("hf"), b)
-        qz(R("eqc", 128 * b, 128 * b + 128), R("eqs", 128 * b, 128 * b + 128), R("et", 512 * b, 512 * b + 512))
-    tr(R("xlt"), R("xlg"))
-    act(R("xl0"), R("xlt", 0, 512, 16), AF.Copy, bias=256.0 - 2 * BIG)
+        qz(R("eqc", 128 * b, 128 * b + 128), R("eqs", 128 * b, 128 * b + 128), R("et", 3 - b, 515 - b))
     own_parts("b0c", "b0s", 256)
+    fill(R("U0", 576, 640), 0.0)
     choose(0, "b0c", "b0s")
     merge(0, "b0c", "b0s", "b0c", "b0s", 256, 512)
     decide(0)
-    cp(R("ln", 16, 17), R("lnf", 33, 34))
-    cp(R("ln", 17, 18), R("lnf", 32, 33))
+    for k in range(2):
+        cp(R("ln", 16 + k, 17 + k), R("lnf", 33 + 2 * lb - k, 34 + 2 * lb - k))
     for h in range(2):
         pick("b1c", "b1s", 256 + 128 * h, 384 + 128 * h, "b0c", "b0s", 0, 640 + 128 * h, R("ln", 8 * h, 8 * h + 8))
 
     send_w("b1c", "b1s", "a1")
-    pick("b1c", "b1s", 0, 32, "b0c", "b0s", 0, 640, R("ln", 16, 18))
+    own_block("b1c", "b1s", "b0c", "b0s", 768, R("ln", 16, 18))
     gram("b1c", "b1s", "b1c", "b1s", 256)
     for k in range(2):
-        ts(R("fl", 16 * k, 16 * k + 16), R("z", k, 48, 3), 256.0, OP.is_ge)
-    ts(R("fl", 32, 48), bank(7, 16), 128.0, OP.is_ge)
+        act(R("fl", 16 * k, 16 * k + 16), R("z", k, 48, 3), AF.Sign, bias=-255.5)
+    ts(R("fl", 32, 48), bank(7, 16, 112), 128.0, OP.is_ge)
     tt(R("fl", 48, 96), R("fl", 0, 48), R("gm"), OP.mult)
     scan(R("fl", 96, 144), R("rs8"), R("fl", 48, 96), OP.mult, OP.add)
-    for k in range(3):
-        act(R("pen", k, 4, 2) if k < 2 else R("pen", 4, 6), R("fl", 103 + 16 * k, 112 + 16 * k, 8), AF.Copy, scale=256.0 if k < 2 else 1e29)
-    tt(R("pen", 8, 12), R("pen", 0, 4), R("xi", 15, 64, 16), OP.max)
-    cp(R("xoa"), R("pen", 8, 12))
-    local_scores(1)
-    act(R("xng", 512, 768), ind(R("posn"), R("dup", 0, 16)))
-    tr(R("xnt", 512, 768), R("xng", 512, 768))
-    cp(R("pou"), R("xnt", 512, 768, 16))
-    pick("fc", "fs", 0, 256, "b1c", "b1s", 256, 512, R("pou"))
-    own_parts("fc", "fs", 0)
-    ts(R("dup", 16, 32), R("tb"), col2(1), OP.add, 256.0, OP.add)
     for k in range(2):
-        act(R("xng", 256 * k, 256 * k + 256), ind(R("xr"), R("dup", 16 * k, 16 * k + 16)))
-    cp(R("xi", 136, 138), inv)
-    ts(R("xi", 144, 148), R("xi", 79, 128, 16), 4, OP.arith_shift_right)
-    ts(R("xi", 148, 152), R("xi", 79, 128, 16), 15, OP.bitwise_and)
-    ts(R("xi", 152, 154), R("xi", 136, 138), 4, OP.arith_shift_right)
-    ts(R("xi", 154, 156), R("xi", 136, 138), 15, OP.bitwise_and)
-    cp(R("hl", 8, 20), R("xi", 144, 156))
-    statics(1, [R("hl", 16, 17), R("hl", 17, 18)], 8)
-    tr(R("xnt", 0, 512), R("xng", 0, 512))
-    act(R("xl1"), R("xnt", 0, 512, 16), AF.Copy, bias=256.0 - 2 * BIG)
-    act(R("z", 98, 144, 3), R("xnt", 512, 768, 16))
-    weights(1, [R("hl", 18, 19), R("hl", 19, 20)], 8)
+        act(R("pen", k, 4, 2), R("fl", 103 + 16 * k, 112 + 16 * k, 8), AF.Copy, bias=128.0, scale=128.0)
+    tt(R("pen", 8, 12), R("pen", 0, 4), R("xi", 79, 128, 16), OP.max)
+    cp(R("xoa"), R("pen", 8, 12))
+    act(R("xd", 128, 258, 129), R("fl", 135, 144, 8), AF.Copy, scale=-1e29)
+    act(R("pen", 12, 16), R("fl", 103, 128, 8), AF.Copy, bias=16.0, scale=16.0)
+    act(R("pen", 16, 18), R("fl", 135, 144, 8), AF.Copy, scale=32.0)
+    local_scores(1)
+    pick("fc", "fs", 0, 256, "b1c", "b1s", 256, 512, R("pl"))
+    own_parts("fc", "fs", 0)
+    statics(1, [R("hl", 8, 9), R("hl", 9, 10)], 0)
+    weights(1, [R("hl", 18, 19), R("hl", 19, 20)], 10)
+    fill(R("P2", 640, 896), 0.0)
+    act(R("hls", 0, 4), R("hl", 4, 8), AF.Copy, scale=1.0 / 16)
+    act(R("hls", 4, 8), R("hl", 14, 18), AF.Copy, scale=1.0 / 256)
+    for e in range(2):
+        for k in range(2):
+            for h in range(2):
+                a = 640 + 128 * e + 64 * k
+                act(R("P2", a + h, a + 64, 4), R("nat", 32 + 16 * h, 48 + 16 * h), AF.Copy, scale=R("hls", 4 * e + 2 * h + k, 4 * e + 2 * h + k + 1))
+    qz(R("pl2c", 128, 256), R("pl2s", 128, 256), R("P2", 384, 896))
+    flags_times(1, 0, 7, "pl2c", "pl2s", 128)
+    act(R("xlt", 32, 64), bank(7, 32, 96), AF.Copy, bias=256.0 - 2 * BIG)
+    tt(R("xl1"), bank(7, 32, 64), R("xlt", 32, 64), OP.add)
+    fill(R("U1", 128, 320), 0.0)
+    sfill(R("U1", 576, 640), 0.0)
     for k in range(3):
         for h in range(2):
-            ts(R("u1", 192 + 64 * k + h, 256 + 64 * k, 4), R("nat", 32 + 16 * h, 48 + 16 * h), R("fl", 103 + 8 * (2 * k + h), 104 + 8 * (2 * k + h)), OP.mult, 32.0, OP.mult)
+            a = 128 + 64 * k
+            act(R("U1", a + h, a + 64, 4), R("nat", 32 + 16 * h, 48 + 16 * h), AF.Copy, scale=R("pen", 12 + 2 * k + h, 13 + 2 * k + h))
     qz(R("qwc"), R("qws"), R("wt"))
     choose(1, "b1c", "b1s")
     cp(R("zb", 0, 16), bank(2, 16))
-    cp(R("zb", 16, 96), R("bk3", 16, 96))
+    cp(R("zb", 16, 80), bank(3, 64, 16))
     for k in (0, 1, 3, 4, 5):
-        tt(R("zp", 16 * k, 16 * k + 16), R("zb", 16 * k, 16 * k + 16), nl[k % 3], OP.add)
+        a = 16 * k - (16 if k > 2 else 0)
+        tt(R("zp", 16 * k, 16 * k + 16), R("zb", a, a + 16), nl[k % 3], OP.add)
     merge(1, "b1c", "b1s", "fc", "fs", 0, 256)
     decide(1)
-    ts(R("zp", 160, 176), bank(7, 16), 32.0, OP.mult)
-    tt(R("zp", 32, 48), R("zp", 160, 176), n2, OP.add)
+    ts(R("zp", 160, 176), bank(7, 16, 112), 32.0, OP.mult)
+    tt(R("zp", 32, 48), R("zp", 160, 176), nl[2], OP.add)
     for t in range(2):
         a = 48 - 48 * t
         tt(R("zp", 128 + 16 * t, 144 + 16 * t), R("zp", a, a + 16), R("zp", a + 16, a + 32), OP.max)

import math
from concourse.bass import DstId, RemoteDMATransfer
from concourse.mybir import dt, AluOpType, AxisListType, ActivationFunctionType

OP = AluOpType
AF = ActivationFunctionType
BIG = 4096.0
RND = 1.5 * 2.0 ** 28
CY = 1.1e-3
FP8, U8, F32, BF, I32, U16 = "float8_e4m3fn_x4", "uint8", "float32", "bfloat16", "int32", "uint16"
ORDER = """
32 42 5 2 6 1 0 3 56 35 4 7 14 12 43 11 31 10 46 13 18 40 16 63 60 15 33 17 37 47 166 50 65 49 34 51 48 64 38 68 87 52 9 72 69 62 58 41 53 66
59 61 74 205 97 90 36 96 73 99 75 98 76 167 71 54 24 20 8 100 26 84 25 55 45 21 22 23 101 19 28 237 29 57 30 103 27 102 77 105 104 44 106 107
227 70 67 109 81 108 94 127 92 110 111 114 118 129 79 113 91 112 116 165 115 39 119 93 121 120 78 89 117 209 122 156 155 131 128 123 140 157
158 124 125 159 141 142 160 126 161 143 80 229 88 162 133 149 95 134 132 145 168 130 361 150 163 144 135 152 151 164 153 203 136 148 154 191
146 169 214 137 82 170 228 139 171 147 173 172 187 138 181 206 178 174 185 179 176 213 177 86 186 195 384 182 183 189 188 231 175 190 184 235
211 192 210 222 207 216 180 215 218 208 196 221 239 217 197 212 199 238 202 220 241 232 193 240 201 219 200 233 243 242 223 342 245 198 244
346 224 204 85 83 246 230 225 194 247 276 248 226 277 280 234 278 249 250 279 257 281 251 258 282 252 236 283 256 255 284 254 285 253 264 363
286 263 307 349 262 287 345 357 308 309 272 288 273 261 266 259 310 269 260 271 370 358 265 376 267 268 274 270 275 292 356 311 291 294 293
313 362 289 297 312 354 343 301 355 367 359 377 316 360 302 317 295 318 303 365 314 304 298 305 315 306 336 319 320 296 368 321 364 290 331
322 323 335 333 300 324 326 328 332 327 329 369 299 366 381 347 371 379 380 325 372 344 348 334 330 373 351 353 374 382 352 386 350 383 385
378 388 340 387 337 390 389 338 392 391 393 430 395 434 375 394 431 432 401 341 397 433 396 339 400 435 412 398 436 411 399 437 410 409 438
404 408 407 417 443 418 405 402 439 416 445 444 440 427 413 406 403 420 415 447 421 414 441 446 425 423 419 426 422 448 428 442 424 449 429
457 456 461 460 459 450 464 467 463 462 451 466 468 458 452 469 453 470 454 465 455 471
"""

SCRATCH = {"nst": ("dram", [16, 138], I32)}
for _t, _l in (
        (F32, "t48 48 k3 48 g24 48 j64 64 g48 48 d8 8 ones 128 idn 128 sqa 128 sqb 256 gms 8 col 8 col2 4 gl48 48 own48 48 "
              "jl 16 jw 16 dm 64 rs16 64 rs8 48 rs3 48 rs24 48 gm 48 gmt 48 mk48 48 msk 16 dw 32 iv 32 xg 64 xg2 64 hl 20 hls 8 "
              "xl0 32 xl1 32 xlt 64 mn 256 gs 528 gg 64 sc 64 pen 20 sm 32 m0 2 m1 2 ma0 8 ma1 8 mx0 8 mx1 8 mq 128 "
              "tkc 18 xd 260 jk 256 jq 128 z 192 zp 176 zb 80 fp 96 lnf 96 fl 144 ys 256 tab 2304"),
        (BF, "xt 1024 wt 512 iob 256 one 516 rowb 256 rowd 128 rowc 128 kr 256 krs 256 phb 2 et 516 pa 1024 P1 584 P2 896 U0 640 U1 640 "
             "posn 256 nr 512 nat 64 ct 2048 nt 1024"),
        (I32, "nbw 48 nn 138 hi 48 xi 180")):
    _w = _l.split()
    for _n, _k in zip(_w[0::2], _w[1::2]):
        SCRATCH[_n] = ("sbuf", [128, int(_k)], _t)
PIECE = {}
for _b, _t, _l in (
        ("uu", U16, "ku 16 l18 18 o01 32 of4 4 xo 4 xoa 4 ofx 8 lp 32 ln 36 pl 16"),
        ("cn", I32, "pp 2 ci 6"),
        ("fa", F32, "n2m 48 xa 48 kw 48 xm 48 kf 48 ks 48 km 48 kc 48 ss 2 lo 2 ph 4 nv 4 wr 2 tkw 16")):
    _w, _c = _l.split(), 0
    for _n, _k in zip(_w[0::2], _w[1::2]):
        PIECE[_n] = (_b, _c, int(_k))
        _c += int(_k)
    SCRATCH[_b] = ("sbuf", [128, _c], _t)
_w = "pa 256 pm 256 pl2 256 q0 256 qw 128 b0 768 b1 512 f 512 oq 256 eq 512 cq 512 uq 512 p0 256 p1 256".split()
for _n, _k in zip(_w[0::2], _w[1::2]):
    SCRATCH[_n + "c"] = ("sbuf", [128, int(_k)], FP8)
    SCRATCH[_n + "s"] = ("sbuf", [128, int(_k)], U8)
for _k in range(8):
    SCRATCH["bk%d" % _k] = ("psum", [128, 512], F32)

SEMAPHORES = ["qv", "qs", "qt", "qp", "lnb", "lx", "lx2", "lx3", "lw", "lst", "lnn", "st0", "lm0", "lm1", "loc", "a0", "a1", "e0", "e1"]


def program(g, core, T, topo):
    r = T.rank_of(core)
    blk = [(r + q) % 8 for q in range(8)]
    lb = blk[r]
    Q = {"v": g.vector, "s": g.scalar, "t": g.tensor, "y": g.sync, "p": g}
    cnt = {}
    known = {k: {} for k in Q}
    acc = {}
    ops = []
    group = {}

    def meet(a, b):
        return a[0] < b[1] and b[0] < a[1] and (a[0] - b[0]) % math.gcd(a[2], b[2]) == 0

    def issue(q, fn, reads, writes, sem, n, dur, lat=None):
        deps, me = set(), len(ops)
        for w, regs in ((False, reads), (True, writes)):
            for b, lo, hi, st in regs:
                for a in acc.get(b, []):
                    if (w or a[3]) and meet((lo, hi, st), a):
                        deps.update(group.get(ops[a[4]][3], [a[4]]))
        ops.append([q, fn, sorted(deps), sem, n, dur, dur if lat is None else lat])
        if n != 1:
            group.setdefault(sem, []).append(me)
        for w, regs in ((False, reads), (True, writes)):
            for b, lo, hi, st in regs:
                l = acc.setdefault(b, [])
                if w and st == 1:
                    l[:] = [a for a in l if not (lo <= a[0] and a[1] <= hi)]
                l.append((lo, hi, st, w, me))
        return me

    def emit():
        total = {m: sum(ops[i][4] for i in l) for m, l in group.items()}
        count, clock = [0] * len(ops), [None] * len(ops)
        for i in ([int(k) for k in ORDER.split()] or range(len(ops))):
            q, fn, deps, sem, n = ops[i][:5]
            if q == "a":
                count[i], clock[i] = n, {}
                continue
            kn = known[q]
            for d in sorted(deps, key=lambda d: -count[d]):
                if not ops[d][3] or (q == "t" and ops[d][0] == "t"):
                    continue
                m = ops[d][3]
                c = total.get(m, count[d])
                if kn.get(m, 0) < c:
                    Q[q].wait_ge(T.sem[m], c)
                    kn[m] = c
                for k, v in clock[d].items():
                    kn[k] = max(kn.get(k, 0), v)
            ins = fn()
            if sem:
                ins.then_inc(T.sem[sem], n)
                cnt[sem] = cnt.get(sem, 0) + n
                count[i] = cnt[sem]
            clock[i] = dict(kn)

    def R(n, a=0, b=None, s=1):
        n, base, w = PIECE.get(n, (n, 0, SCRATCH[n][1][1] if n in SCRATCH else 0))
        a, b = base + a, base + (w if b is None else b)
        ap = T[n][:, slice(a, b) if s == 1 else slice(a, b, s)]
        if SCRATCH[n][0] == "psum":
            return ap, [(n, 0, 512, 1)]
        return ap, [(n, a, b, s)]

    def W32(v):
        return v[0].bitcast(dt.uint32), v[1]

    def W8(v):
        return v[0].bitcast(dt.uint8), v[1]

    def ind(win, off):
        return win[0].indirect(off[0]), win[1] + off[1]

    def val(s):
        return (s[0], s[1]) if isinstance(s, tuple) else (s, [])

    def us(n, c=1.0):
        return max(64, n * c) * CY

    def width(v):
        r0 = v[1][0]
        return -(-(r0[2] - r0[1]) // r0[3])

    def half(*vs):
        return 0.5 if all(SCRATCH[v[1][0][0]][2] in (BF, U16) for v in vs) else 1.0

    def ts(o, i, s1, op0, s2=None, op1=None):
        a, b = val(s1), val(s2)
        rd = i[1] + a[1] + b[1]
        d = (0.05 + us(width(o), 1.5)) if len(i[1]) > 1 else us(width(o), half(o, i))
        if op1 is None:
            issue("v", lambda: g.vector.tensor_scalar(o[0], i[0], a[0], None, op0), rd, o[1], "qv", 1, d)
        else:
            issue("v", lambda: g.vector.tensor_scalar(o[0], i[0], a[0], b[0], op0, op1), rd, o[1], "qv", 1, d)

    def tt(o, a, b, op):
        issue("v", lambda: g.vector.tensor_tensor(o[0], a[0], b[0], op), a[1] + b[1], o[1], "qv", 1,
              (0.05 + us(width(o), 1.5)) if len(a[1]) > 1 else us(width(o), 1 if a[1][0][0][:2] == "bk" else 2))

    def cp(o, i, n=None):
        n = n or width(o)
        issue("v", lambda: g.vector.tensor_copy(o[0], i[0]), i[1], o[1], "qv", 1,
              (0.05 + us(n, 1.5)) if len(i[1]) > 1 else us(n, half(o, i)))

    def fill(o, c):
        issue("v", lambda: g.vector.memset(o[0], c), [], o[1], "qv", 1, us(width(o), half(o)))

    def red(o, i):
        issue("v", lambda: g.vector.tensor_reduce(o[0], i[0], AxisListType.X, OP.add), i[1], o[1], "qv", 1, us(width(i)))

    def scan(o, a, b, op0, op1, init=0.0):
        issue("v", lambda: g.vector.tensor_tensor_scan(o[0], a[0], b[0], init, op0, op1), a[1] + b[1], o[1], "qv", 1, us(width(o), half(o, a)))

    def qz(c, s, i):
        issue("v", lambda: g.vector.quantize_mx(c[0], s[0], i[0]), i[1], c[1] + s[1], "qv", 1, 0.02 + width(i) * 0.26e-3)

    def act(o, i, f=AF.Copy, bias=None, scale=None, accum=None, lock=(), n=None):
        kw, rd, wr = {}, list(i[1]), list(o[1]) + list(lock)
        if bias is not None:
            kw["bias"] = val(bias)[0]
            rd += val(bias)[1]
        if scale is not None:
            kw["scale"] = val(scale)[0]
            rd += val(scale)[1]
        if accum is not None:
            kw["accum_out"] = accum[0]
            wr += accum[1]
        n = n or width(o)
        issue("s", lambda: g.scalar.activation(o[0], i[0], f, **kw), rd, wr, "qs", 1,
              (0.08 + us(n, 1.5)) if len(i[1]) > 1 else 0.03 + us(n))

    def mm(o, lc, ls, rc, rs, start=True, stop=True):
        issue("t", lambda: g.tensor.matmul_mx(o[0], lc[0], ls[0], rc[0], rs[0], start, stop),
              lc[1] + ls[1] + rc[1] + rs[1], o[1], "qt", 1, us(width(rc) + 16, 1.25))

    def iota(o, pat, base, cm):
        issue("p", lambda: g.iota(o[0], pat, base, cm, allow_small_or_imprecise_dtypes=True), [], o[1], "qp", 1, 0.13 + us(width(o), 2))

    def resets(o, a, b):
        issue("p", lambda: g.affine_select(o[0], T.ones[:, 0:a * b], [[0, a], [1, b]], OP.not_equal, 0.0, 0, 0), R("ones", 0, a * b)[1], o[1], "qp", 1,
              0.17 + us(a * b, 2))

    def pickout(o, i, base, cm):
        issue("p", lambda: g.affine_select(o[0], i[0], [[-1, width(o)]], OP.is_equal, 0.0, base, cm), i[1], o[1], "qp", 1, 0.17 + us(width(o), 2))

    def sfill(o, c):
        act(o, R("one", 0, width(o)), AF.Copy, scale=c)

    def dma(q, sem, out, i):
        issue(q, lambda: Q[q].dma_start(out[0], i[0]), i[1], out[1], sem, 16, 0.07, 2.5)

    for gr in range(8):
        dma("ys"[gr % 2], "lnb", (T.nbw[16 * gr:16 * gr + 16, :], [("nbw", 0, 48, 1)] if gr == 0 else []), (T.nb[:, :], []))
    dma("s", "lx", R("xt"), (T.x[:, :], []))
    dma("s", "lx2", R("P1", 72, 520), (T.x[:, 0:448], []))
    first = True
    for k in range(3):
        i = 0
        while i < 16:
            a, o = (3 * i + k) % 16, (3 * i + k) // 16
            n = min((15 - a) // 3 + 1, 16 - i)
            dma("y", "lst", (T.nst[i:i + n, 46 * k:46 * k + 46], [("nst", 0, 138, 1)] if first else []),
                (T.nb[a:a + 3 * (n - 1) + 1:3, o:o + 46], []))
            i, first = i + n, False
    for gr in range(8):
        dma("y", "lnn", (T.nn[16 * gr:16 * gr + 16, :], [("nn", 0, 138, 1)] if gr == 0 else []), (T.nst[:, :], [("nst", 0, 138, 1)]))
    for b, lo, hi in (("P2", 256, 640), ("U0", 128, 576), ("U1", 320, 576)):
        dma("y", "lx3", R(b, lo, hi), (T.x[:, 0:hi - lo], []))
    dma("y", "lw", R("wt"), (T.w[:, :], []))
    nl = [R("nn", 46 * k, 46 * k + 46, 3) for k in range(3)]

    iota(R("pp", 0, 1), [[0, 1]], 0, 1)
    iota(R("pp", 1, 2), [[0, 1]], 10, 11)
    iota(R("k3"), [[0, 16], [1, 3]], 0, 0)
    iota(R("t48"), [[16, 16], [0, 3]], 256 * r, 0)
    iota(R("g24"), [[0, 2], [1, 8], [0, 3]], 0, 0)
    iota(R("rowd"), [[0, 8], [2, 16]], 0, 0)
    iota(R("g48"), [[0, 6], [1, 8]], 0, 0)
    iota(R("rowb"), [[0, 16], [1, 16]], 0, 0)
    iota(R("j64"), [[0, 4], [1, 16]], 0, 0)
    iota(R("d8"), [[0, 2], [1, 4]], 0, 0)
    iota(R("tab", 1792, 2304), [[1, 512]], 1792, 0)
    fill(R("one", 0, 256), 1.0)
    scan(R("iob"), R("one", 0, 256), R("one", 0, 256), OP.add, OP.mult, -1.0)
    fill(R("one", 256, 516), 1.0)
    act(R("ones"), R("one", 0, 128))

    def c(k):
        return R("ci", k, k + 1)

    def col(k):
        return R("col", k, k + 1)

    def col2(k):
        return R("col2", k, k + 1)
    ts(c(3), R("pp", 1, 2), 15, OP.bitwise_and)
    ts(c(4), c(3), 3, OP.mult, 2, OP.add)
    ts(c(5), c(4), 4, OP.arith_shift_right)
    ts(c(0), R("pp", 0, 1), 15, OP.bitwise_and)
    ts(c(1), R("pp", 0, 1), 4, OP.arith_shift_right)
    ts(c(2), R("pp", 0, 1), 5, OP.arith_shift_right)
    cp(R("col", 0, 6), R("ci"))
    ts(R("mk48"), R("k3"), col(5), OP.is_equal)
    ts(R("gmt"), R("g24"), col(1), OP.is_equal)
    ts(R("rs3"), R("k3"), 0.0, OP.not_equal)
    fill(R("rs24"), 1.0)
    fill(R("rs24", 0, 48, 24), 0.0)
    act(R("gl48"), R("t48"), AF.Identity, bias=col(3))
    act(R("own48"), R("gl48"), AF.Copy, bias=256.0 * (1 - r))
    for b in range(7):
        if b % 2:
            act(R("tab", 256 * b, 256 * b + 256), R("iob"), AF.Copy, bias=256.0 * b)
        else:
            ts(R("tab", 256 * b, 256 * b + 256), R("iob"), 256.0 * b, OP.add)
    act(R("rowc"), R("rowd"), AF.Copy, bias=-255.0)
    act(R("tkc", 0, 16), R("iob", 0, 16), AF.Copy, bias=RND - 64.0 * r, scale=32.0)
    ts(R("tkw"), R("iob", 0, 16), 2.0 * r, OP.is_lt, 512.0, OP.mult)
    tt(R("tkc", 0, 16), R("tkc", 0, 16), R("tkw"), OP.add)
    for k in range(2):
        act(R("tkc", 16 + k, 17 + k), R("iob", 2 * r + 1 - k, 2 * r + 2 - k), AF.Copy, bias=RND, scale=32.0)
    for h in range(2):
        act(R("nv", 2 * h, 2 * h + 1), col(1), AF.Copy, bias=128.0 * h, scale=16.0)
        act(R("nv", 2 * h + 1, 2 * h + 2), col(3), AF.Copy)
    ts(R("gm"), R("g48"), col(1), OP.is_equal)
    resets(R("rs8"), 6, 8)
    resets(R("rs16"), 4, 16)
    ts(R("dm"), R("j64"), col(0), OP.is_equal)
    act(R("jl"), R("iob", 0, 16), AF.Identity, bias=col(0), scale=16.0)
    act(R("jw"), R("jl"), AF.Copy, bias=256.0)
    act(R("z", 2, 48, 3), R("jl"))
    act(col2(0), col(1), AF.Copy, bias=8.0)
    act(col2(1), col(0), AF.Copy, scale=2.0)
    act(col2(2), col(0), AF.Copy, bias=1.0, scale=2.0)
    sfill(R("P1", 520, 584), 0.0)
    for h in range(2):
        act(R("P1", 522 + 30 * h, 552 + 32 * h, 4), R("gm", 0, 8), AF.Copy, scale=64.0 * r)
    act(R("sqa"), R("rowb", 0, 128), AF.Square, bias=col(3), scale=-1.0)
    for e in range(4):
        act(R("pa", 512 + e, 1024, 4), R("sqa"), AF.Relu, bias=1.0, scale=-1.0)
    qz(R("pac", 128, 256), R("pas", 128, 256), R("pa", 512, 1024))

    tt(R("n2m"), R("nbw"), R("mk48"), OP.mult)
    ts(R("hi"), R("nbw"), 1792, OP.bitwise_and)
    tt(R("kw"), R("n2m"), R("gl48"), OP.is_gt)
    tt(R("xa"), R("hi"), R("own48"), OP.add)
    tt(R("xm"), R("kw"), R("xa"), OP.mult)
    tt(R("kf"), R("n2m"), R("xm"), OP.max)
    tt(R("km"), R("kf"), R("gmt"), OP.mult)
    scan(R("ks"), R("rs3"), R("kf"), OP.mult, OP.add)
    scan(R("kc"), R("rs24"), R("km"), OP.mult, OP.add)
    cp(R("ku"), R("ks", 2, 48, 3))
    act(R("jk"), ind(R("tab"), R("ku")), AF.Sign, bias=R("kc", 23, 24), scale=-1.0, accum=R("ss", 0, 1))
    ts(R("kr"), ind(R("tab"), R("ku")), R("kc", 47, 48), OP.is_lt, 2.0, OP.mult)
    scan(R("krs"), R("kr"), R("kr"), OP.add, OP.max)
    p2 = [R("ss", 0, 1), R("krs", 255, 256)]
    rw = [R("rowc"), R("rowd")]
    hi2 = [R("ph", 2, 3), R("phb", 0, 1)]
    for h in range(2):
        ts(R("ph", h, h + 1), p2[h], -15.0 if h else 240.0, OP.add, RND, OP.add)
        ts(hi2[h], R("ph", h, h + 1), -RND, OP.add)
    for e in range(4):
        ts(R("P1", e, 72, 4), R("tkc"), R("ph", e // 2, e // 2 + 1), OP.is_equal, R("nv", e, e + 1), OP.mult)
    qz(R("pmc", 0, 128), R("pms", 0, 128), R("P1", 0, 512))
    for e in range(4):
        ts(R("pa", e, 512, 4), rw[e // 2], hi2[e // 2], OP.add, p2[e // 2], OP.is_equal)
    qz(R("pac", 0, 128), R("pas", 0, 128), R("pa", 0, 512))
    mm(R("bk6", 0, 128), R("pac", 0, 128), R("pas", 0, 128), R("pmc", 0, 128), R("pms", 0, 128))
    cp(R("l18"), R("bk6", 0, 18))
    ts(R("lo", 0, 1), p2[0], 255.0, OP.add, hi2[0], OP.subtract)
    ts(R("lo", 1, 2), p2[1], hi2[1], OP.subtract)
    for h in range(2):
        ts(R("wr", h, h + 1), p2[h], 257.0 + 255 * h - 64 * r, OP.is_ge, -512.0, OP.mult)
    for h in range(2):
        a = 520 + 34 * h
        if h == 0:
            act(R("P1", a, 552, 4), R("gm", 0, 8), AF.Copy, scale=hi2[0])
        else:
            ts(R("P1", a, 584, 4), R("gm", 0, 8), hi2[1], OP.mult)
        act(R("P1", a + 1, 552 + 32 * h, 4), R("gm", 0, 8), AF.Copy, scale=R("lo", h, h + 1))
        act(R("P1", 523 + 30 * h, 552 + 32 * h, 4), R("gm", 0, 8), AF.Copy, scale=R("wr", h, h + 1))
    qz(R("pmc", 128, 256), R("pms", 128, 256), R("P1", 72, 584))
    mm(R("bk5", 0, 128), R("pac", 128, 256), R("pas", 128, 256), R("pmc", 128, 256), R("pms", 128, 256))
    ts(R("pl"), R("bk5", 112, 128), 0.5, OP.mult)
    act(R("z", 98, 144, 3), R("bk5", 112, 128), AF.Copy, scale=0.5, lock=R("bk5")[1])
    act(R("posn"), ind(R("iob"), R("pl")))
    qz(R("q0c"), R("q0s"), R("xt"))

    def pick(dc, ds, a, b, sc, ss, w0, w1, off, own=False):
        oc, os = R(dc, a, b), R(ds, a, b)
        if own:
            oc, os = (oc[0], [(dc, 0, 256, 1)]), (os[0], [(ds, 0, 256, 1)])
        cp(W32(oc), ind(W32(R(sc, w0, w1)), off), b - a)
        act(os, ind(R(ss, w0, w1), off), n=b - a)

    others = [d for d in range(1, 8)]
    far = [d for d in others if topo.die(T.cores[r ^ d]) != topo.die(core)]
    near = [d for d in others if d not in far]
    lanes = {}
    for k, l in enumerate((far, near)):
        for n, d in enumerate(l):
            e = topo.engines(core, T.cores[r ^ d])
            lanes[d] = [e[4 * n + k], e[4 * n + 2 + k]]

    def send(srcs, dsts, sem, regs):
        def call():
            tf = []
            for d in others:
                ad = topo.addr(T.cores[r ^ d])
                tf.append(RemoteDMATransfer(dst_ids=[DstId(rid=ad[0], pnc=ad[1])], dma_engine_mask=sum(1 << e for e in lanes[d]),
                                            remote_sem=T.sem[sem], src=srcs(blk[r ^ d]), dst=dsts(blk[r ^ d])))
            g.remote_dma_fused(tf, local_sem=T.sem.loc)
            cnt["loc"] = cnt.get("loc", 0) + 14
        me = issue("p", call, [(b, lo, hi, 1) for b, lo, hi in regs], [], None, 1, 0.7, 0.7)
        group.setdefault(sem, []).append(len(ops))
        ops.append(["a", None, [me], sem, 14, 0.0, 2.5])

    def arrive(sem, b, lo, hi):
        acc.setdefault(b, []).append((lo, hi, 1, True, group[sem][0]))

    def send_w(bc, bs, sem):
        send(lambda q: T[bc][:, 256 + 32 * q:288 + 32 * q].bitcast(dt.uint8), lambda q: T[bc][:, 32 * q:32 * q + 32].bitcast(dt.uint8),
             sem, [(bc, 256, 512)])
        send(lambda q: T[bs][:, 256 + 32 * q:288 + 32 * q], lambda q: T[bs][:, 32 * q:32 * q + 32], sem, [(bs, 256, 512)])

    def bank(k, n, a=0):
        return R("bk%d" % k, a, a + n)

    def gram(bc, bs, mc, ms, m0):
        mm(bank(0, 256), R(bc, 256, 384), R(bs, 256, 384), R(mc, m0, m0 + 256), R(ms, m0, m0 + 256))
        for k, j in enumerate((1, 3)):
            a = m0 + 128 * k
            mm(bank(j, 128), R(bc, 384, 512), R(bs, 384, 512), R(mc, a, a + 128), R(ms, a, a + 128))
        act(R("gs", 0, 256), bank(0, 256))
        cp(R("gs", 264, 392), bank(1, 128))
        cp(R("gs", 392, 520), bank(3, 128))

    BK = [[0, 4, 5, 6], [0, 1, 2, 3]]

    def dec(h, b, cc, cs, a, start):
        w = 256 if b == 0 else 128
        mm(bank(BK[h][b], w), R("eqc", 128 * b, 128 * b + 128), R("eqs", 128 * b, 128 * b + 128),
           R(cc, a + 128 * h, a + 128 * h + w), R(cs, a + 128 * h, a + 128 * h + w), start, not start)

    def diagonal(o, x, i, off):
        tt(x, ind(i, off), R("dm"), OP.mult)
        scan(o, R("rs16"), x, OP.mult, OP.add)

    def local_scores(t):
        for h in range(2):
            tt(R("gg", 32 * h, 32 * h + 32), ind(R("gs", 264 * h, 264 * h + 264), R("xoa" if t else "xo", 2 * h, 2 * h + 2)), R("dm", 0, 32), OP.mult)
        scan(R("sc"), R("rs16"), R("gg"), OP.mult, OP.add)
        s0, s1 = R("sc", 15, 64, 32), R("sc", 31, 64, 32)
        m, ma, mx = "m%d" % t, "ma%d" % t, "mx%d" % t
        for h in range(2):
            ts(R(ma, 4 * h, 4 * h + 4), R("msk", 4 * h, 4 * h + 4), R("sc", 15 + 32 * h, 16 + 32 * h), OP.max, R("sc", 31 + 32 * h, 32 + 32 * h), OP.max)
        send(lambda q: T[ma][:, q:q + 1], lambda q: T[mx][:, q:q + 1], "e%d" % t, [(ma, 0, 8)])
        b = 32 * (lb % 4)
        rest = [(0, b), (b + 32, 128)] if 0 < b < 96 else [(32 - b // 3, 64), (64, 128 - b // 3)]
        for i, (lo, hi, to) in enumerate([(b, b + 16, b + 16), (b + 16, b + 32, b)] + [(lo, hi, lo) for lo, hi in rest]):
            dma("y", "lm%d" % t, (T[mx][to:to + hi - lo, lb:lb + 1], [(mx, 0, 8, 1)] if i == 0 else []), (T[ma][lo:hi, lb:lb + 1], [(ma, 0, 8, 1)]))
        tt(R(m), s0, s1, OP.max)
        tt(R("sm", 0, 2), s0, s1, OP.is_ge)
        act(R("sm", 2, 6, 2), R("sm", 0, 2), AF.Copy, bias=-4e29, scale=4e29)
        act(R("sm", 3, 6, 2), R("sm", 0, 2), AF.Copy, scale=-4e29)
        tt(R("sm", 8, 12), R("sc", 15, 64, 16), R("sm", 2, 6), OP.add)

    def statics(t, hi_own, hl):
        for h in range(2):
            a = 128 * t + 64 * h
            act(R("mn", a, a + 64, 2), R("j64", 0, 32), AF.Square, bias=hi_own[h], scale=-1.0)
            for k in range(2):
                act(R("mn", a + 32 * k + 1, a + 32 * k + 32, 2), R("j64", 0, 16), AF.Square, bias=R("hl", hl + 2 * h + k, hl + 2 * h + k + 1), scale=-1.0)
            act(R("nat", 32 * t + 16 * h, 32 * t + 16 * h + 16), R("mn", a, a + 32, 2), AF.Relu, bias=0.0625, scale=-0.0625)
        for h in range(2):
            for k in range(2):
                a = 64 * h + 32 * k
                act(R("mq", a, a + 32), R("mn", 128 * t + a, 128 * t + a + 32), AF.Identity,
                    bias=R("sm", 8 + 2 * h + k, 9 + 2 * h + k), scale=-8e29)

    def weights(t, lo_own, hl):
        if t == 0:
            act(R("sqb"), R("rowb"), AF.Square, bias=col(0), scale=-1.0)
        for h in range(2):
            if t == 0:
                act(R("ct", h, 1024, 4), R("sqb"), AF.Relu, bias=BIG, scale=-BIG)
            else:
                ts(R("ct", 1024 * t + h, 1024 * t + 1024, 4), R("rowb"), lo_own[h], OP.is_equal, BIG, OP.mult)
            for k in range(2):
                a = 1024 * t + 512 * k
                ts(R("ct", a + 2 + h, a + 512, 4), R("rowb", 0, 128), R("hl", hl + 2 * h + k, hl + 1 + 2 * h + k), OP.is_equal, BIG, OP.mult)
        qz(R("cqc", 256 * t, 256 * t + 256), R("cqs", 256 * t, 256 * t + 256), R("ct", 1024 * t, 1024 * t + 1024))

    def flags_times(t, k, b, qc, qs, uq):
        ca = 256 * t + 128 * k
        mm(bank(b, 128), R("cqc", ca, ca + 128), R("cqs", ca, ca + 128), R(qc, uq, uq + 128), R(qs, uq, uq + 128))

    def choose(t, bc, bs):
        u, uq, z, xl = "U%d" % t, 128 * t, 96 * t, "xl%d" % t
        arrive("a%d" % t, bc, 0, 256)
        arrive("a%d" % t, bs, 0, 256)
        for h in range(2):
            mm(bank(2 + h, 128), R(bc, 256 + 128 * h, 384 + 128 * h), R(bs, 256 + 128 * h, 384 + 128 * h),
               R(bc, 128 * h, 128 * h + 128), R(bs, 128 * h, 128 * h + 128))
        for h in range(2):
            tt(R("xd", 129 * h, 129 * h + 128), bank(2 + h, 128), R("idn"), OP.mult)
        act(R("jk", 0, 128 + t), R("xd", 0, 128 + t), AF.Identity, accum=R("sm", 16, 17))
        red(R("sm", 17, 18), R("xd", 129, 257 + t))
        for h in range(2):
            ts(R(u, h, 128, 2), R("mq", 64 * h, 64 * h + 64), R("sm", 16 + h, 17 + h), OP.is_ge)
        qz(R("uqc", uq, uq + 128), R("uqs", uq, uq + 128), R(u, 0, 512))
        for k in range(2):
            flags_times(t, k, 2 + k, "uqc", "uqs", uq)
        for k in range(2):
            tt(R("z", z + k, z + 48, 3), bank(2 + k, 16, 16 * k), R(xl, 16 * k, 16 * k + 16), OP.add)
        scan(R("z", z + 48, z + 96), R("rs3"), R("z", z, z + 48), OP.mult, OP.max)
        cp(R("lp", 16 * t, 16 * t + 16), R("z", z + 50, z + 96, 3))

    def decide(t):
        mx, u = "mx%d" % t, "U%d" % t
        arrive("e%d" % t, mx, 0, 8)
        for h in range(2):
            ts(R("ofx", 4 * h, 4 * h + 4), R(mx, 4 * h, 4 * h + 4), R("sm", 16 + h, 17 + h), OP.is_lt, col2(1), OP.add)
        for h in range(2):
            act(R("jq", 64 * h, 64 * h + 64), ind(R("dw"), R("ofx", 4 * h, 4 * h + 4)), AF.Copy, accum=R("sm", 20 + h, 21 + h))
        tt(R("sm", 22, 24), R("sm", 16, 18), R("m%d" % t), OP.is_gt)
        for h in range(2):
            ts(R(u, 576 + h, 640, 4), R("nat", 32 * t + 16 * h, 32 * t + 16 * h + 16), R("sm", 20 + h, 21 + h), OP.mult, R("sm", 22 + h, 23 + h), OP.mult)
        vq = 256 + 128 * t
        qz(R("uqc", vq, vq + 128), R("uqs", vq, vq + 128), R(u, 128, 640))
        flags_times(t, 0, 7, "uqc", "uqs", vq)
        a = 48 * t
        ts(R("lnf", a, a + 16), R("z", 96 * t + 50, 96 * t + 96, 3), 256.0, OP.is_ge, 256.0, OP.mult)
        tt(R("lnf", a + 16, a + 32), R("lnf", a, a + 16), R("jl" if t else "jw"), OP.add)
        tt(R("lnf", a + 32, a + 48), bank(7, 16, 112), R("lnf", a + 16, a + 32), OP.add)
        cp(R("ln", 20 * t, 20 * t + 16), R("lnf", a + 32, a + 48))

    def own_parts(cc, cs, a):
        for h, b in ((0, 0), (0, 1), (0, 2), (0, 3), (1, 1)):
            dec(h, b, cc, cs, a, True)

    def merge(t, bc, bs, cc, cs, own, base):
        pc, psn, off = "p%dc" % t, "p%ds" % t, 16 * t
        for h in range(2):
            pick(pc, psn, 128 * h, 128 * h + 128, bc, bs, 0, 512, R("lp", off + 8 * h, off + 8 * h + 8))
        for b in range(2, 4):
            dec(1, b, cc, cs, own, True)
        for h, b in ((0, 1), (0, 2), (0, 3), (0, 0), (1, 1), (1, 2), (1, 3)):
            dec(h, b, pc, psn, 0, False)
        for h in range(2):
            for b in range(4):
                oo = R("nt", 512 * h + b, 512 * h + 512, 4)
                if b == 0:
                    ts(oo, R("bk0", 128 * h, 128 * h + 128), 0.5, OP.mult)
                elif b == 2:
                    ts(oo, bank(BK[h][b], 128), 0.5, OP.mult)
                else:
                    act(oo, bank(BK[h][b], 128), AF.Copy, scale=0.5)
            qz(R(cc, base + 128 * h, base + 128 * h + 128), R(cs, base + 128 * h, base + 128 * h + 128), R("nt", 512 * h, 512 * h + 512))

    def own_block(bc, bs, sc, ss, w, off):
        pick(bc, bs, 32 * lb, 32 * lb + 32, sc, ss, 0, w, off, True)

    pick("b0c", "b0s", 256, 512, "q0c", "q0s", 0, 256, R("l18", 0, 16))
    send_w("b0c", "b0s", "a0")
    own_block("b0c", "b0s", "q0c", "q0s", 256, R("l18", 16, 18))
    gram("b0c", "b0s", "q0c", "q0s", 0)
    for k in range(2):
        ts(R("o01", 16 * k, 16 * k + 16), nl[k], -256.0 * r, OP.add)
    act(R("nr"), ind(R("iob"), R("o01")))
    tt(R("iv", 0, 16), R("bk6", 0, 16), R("gm", 0, 16), OP.mult)
    scan(R("iv", 16, 32), R("rs8", 0, 16), R("iv", 0, 16), OP.mult, OP.add)
    inv = R("iv", 23, 32, 8)
    cp(R("of4", 0, 4, 2), inv)
    ts(R("of4", 1, 4, 2), inv, 256.0, OP.add)
    diagonal(R("xi", 0, 64), R("xg"), R("nr"), R("of4"))
    cp(R("xo"), R("xi", 15, 64, 16))
    for h in range(2):
        sfill(R("gs", 256 + 264 * h, 264 + 264 * h), -1e29)
    ts(R("msk", 8, 16), R("d8"), col(2), OP.not_equal, 2e29, OP.mult)
    ts(R("msk", 0, 8), R("msk", 8, 16), -1e29, OP.add)
    local_scores(0)
    diagonal(R("xi", 64, 128), R("xg2"), R("posn"), R("xo"))
    cp(R("xi", 143, 160, 16), inv)
    ts(R("xi", 160, 170), R("xi", 15, 160, 16), 4, OP.arith_shift_right)
    ts(R("xi", 170, 180), R("xi", 15, 160, 16), 15, OP.bitwise_and)
    cp(R("hl"), R("xi", 160, 180))
    statics(0, [col(1), col2(0)], 4)
    pickout(R("idn"), R("ones"), 0, 1)
    ts(R("dw"), R("iob", 0, 32), col2(2), OP.is_equal)
    weights(0, [col(0), col(0)], 14)
    fill(R("P2", 0, 256), 0.0)
    act(R("gms"), R("gm", 0, 8), AF.Copy, scale=1.0 / BIG)
    for k in range(2):
        for h in range(2):
            a = 64 * k + 33 * h
            ts(R("P2", a, 64 * k + 32 * h + 32, 4), R("gm", 0, 8), R("hl", 4 + 2 * h + k, 5 + 2 * h + k), OP.mult, 16.0 / BIG, OP.mult)
            act(R("P2", a + 128, 64 * k + 32 * h + 160, 4), R("gms"), AF.Copy, scale=R("hl", 14 + 2 * h + k, 15 + 2 * h + k))
    qz(R("pl2c", 0, 128), R("pl2s", 0, 128), R("P2", 0, 512))
    flags_times(0, 0, 7, "pl2c", "pl2s", 0)
    act(R("xlt", 0, 32), bank(7, 32, 32), AF.Copy, bias=256.0 - 2 * BIG)
    tt(R("xl0"), bank(7, 32), R("xlt", 0, 32), OP.add)
    pickout(R("et"), R("one"), 3, 4)
    for b in range(4):
        qz(R("eqc", 128 * b, 128 * b + 128), R("eqs", 128 * b, 128 * b + 128), R("et", 3 - b, 515 - b))
    own_parts("b0c", "b0s", 256)
    fill(R("U0", 576, 640), 0.0)
    choose(0, "b0c", "b0s")
    merge(0, "b0c", "b0s", "b0c", "b0s", 256, 512)
    decide(0)
    for k in range(2):
        cp(R("ln", 16 + k, 17 + k), R("lnf", 33 + 2 * lb - k, 34 + 2 * lb - k))
    for h in range(2):
        pick("b1c", "b1s", 256 + 128 * h, 384 + 128 * h, "b0c", "b0s", 0, 640 + 128 * h, R("ln", 8 * h, 8 * h + 8))

    send_w("b1c", "b1s", "a1")
    own_block("b1c", "b1s", "b0c", "b0s", 768, R("ln", 16, 18))
    gram("b1c", "b1s", "b1c", "b1s", 256)
    for k in range(2):
        act(R("fl", 16 * k, 16 * k + 16), R("z", k, 48, 3), AF.Sign, bias=-255.5)
    ts(R("fl", 32, 48), bank(7, 16, 112), 128.0, OP.is_ge)
    tt(R("fl", 48, 96), R("fl", 0, 48), R("gm"), OP.mult)
    scan(R("fl", 96, 144), R("rs8"), R("fl", 48, 96), OP.mult, OP.add)
    for k in range(2):
        act(R("pen", k, 4, 2), R("fl", 103 + 16 * k, 112 + 16 * k, 8), AF.Copy, bias=128.0, scale=128.0)
    tt(R("pen", 8, 12), R("pen", 0, 4), R("xi", 79, 128, 16), OP.max)
    cp(R("xoa"), R("pen", 8, 12))
    act(R("xd", 128, 258, 129), R("fl", 135, 144, 8), AF.Copy, scale=-1e29)
    act(R("pen", 12, 16), R("fl", 103, 128, 8), AF.Copy, bias=16.0, scale=16.0)
    act(R("pen", 16, 18), R("fl", 135, 144, 8), AF.Copy, scale=32.0)
    local_scores(1)
    pick("fc", "fs", 0, 256, "b1c", "b1s", 256, 512, R("pl"))
    own_parts("fc", "fs", 0)
    statics(1, [R("hl", 8, 9), R("hl", 9, 10)], 0)
    weights(1, [R("hl", 18, 19), R("hl", 19, 20)], 10)
    fill(R("P2", 640, 896), 0.0)
    act(R("hls", 0, 4), R("hl", 4, 8), AF.Copy, scale=1.0 / 16)
    act(R("hls", 4, 8), R("hl", 14, 18), AF.Copy, scale=1.0 / 256)
    for e in range(2):
        for k in range(2):
            for h in range(2):
                a = 640 + 128 * e + 64 * k
                act(R("P2", a + h, a + 64, 4), R("nat", 32 + 16 * h, 48 + 16 * h), AF.Copy, scale=R("hls", 4 * e + 2 * h + k, 4 * e + 2 * h + k + 1))
    qz(R("pl2c", 128, 256), R("pl2s", 128, 256), R("P2", 384, 896))
    flags_times(1, 0, 7, "pl2c", "pl2s", 128)
    act(R("xlt", 32, 64), bank(7, 32, 96), AF.Copy, bias=256.0 - 2 * BIG)
    tt(R("xl1"), bank(7, 32, 64), R("xlt", 32, 64), OP.add)
    fill(R("U1", 128, 320), 0.0)
    sfill(R("U1", 576, 640), 0.0)
    for k in range(3):
        for h in range(2):
            a = 128 + 64 * k
            act(R("U1", a + h, a + 64, 4), R("nat", 32 + 16 * h, 48 + 16 * h), AF.Copy, scale=R("pen", 12 + 2 * k + h, 13 + 2 * k + h))
    qz(R("qwc"), R("qws"), R("wt"))
    choose(1, "b1c", "b1s")
    cp(R("zb", 0, 16), bank(2, 16))
    cp(R("zb", 16, 80), bank(3, 64, 16))
    for k in (0, 1, 3, 4, 5):
        a = 16 * k - (16 if k > 2 else 0)
        tt(R("zp", 16 * k, 16 * k + 16), R("zb", a, a + 16), nl[k % 3], OP.add)
    merge(1, "b1c", "b1s", "fc", "fs", 0, 256)
    decide(1)
    ts(R("zp", 160, 176), bank(7, 16, 112), 32.0, OP.mult)
    tt(R("zp", 32, 48), R("zp", 160, 176), nl[2], OP.add)
    for t in range(2):
        a = 48 - 48 * t
        tt(R("zp", 128 + 16 * t, 144 + 16 * t), R("zp", a, a + 16), R("zp", a + 16, a + 32), OP.max)
        tt(R("zp", 96 + 16 * t, 112 + 16 * t), R("zp", 128 + 16 * t, 144 + 16 * t), R("zp", a + 32, a + 48), OP.max)
    ts(R("fp", 0, 32), R("zp", 96, 128), -2 * BIG, OP.add, -1.0, OP.max)
    tt(R("fp", 32, 64), R("fp", 0, 32), R("gm", 0, 32), OP.mult)
    scan(R("fp", 64, 96), R("rs8", 0, 32), R("fp", 32, 64), OP.mult, OP.add)
    for t in range(2):
        for h in range(2):
            a = 64 + 8 * (2 * t + h) + 7
            dma("y", "st0", (T.pr[t:t + 1, 128 * h:128 * h + 128], []), R("fp", a, a + 1))
    for h in range(2):
        a, b = 128 * h, 128 * h + 128
        pick("oqc", "oqs", a, b, "fc", "fs", 0, 384 + 128 * h, R("ln", 20 + 8 * h, 28 + 8 * h))
        dma("y", "st0", (T.oc[:, 4 * a:4 * b], []), W8(R("oqc", a, b)))
        mm(bank(4 + h, 128), R("qwc"), R("qws"), R("oqc", a, b), R("oqs", a, b))
    for k in range(4):
        dma("s" if k % 2 else "y", "st0", (T.osc[4 * k:4 * k + 4, :], []), (T.oqs[32 * k:32 * k + 4, :], [("oqs", 0, 256, 1)]))
    cp(R("ys", 0, 128), bank(4, 128))
    act(R("ys", 128, 256), bank(5, 128))
    for h in range(2):
        dma("y" if h == 0 else "s", "st0", (T.y[:, 128 * h:128 * h + 128], []), R("ys", 128 * h, 128 * h + 128))

    emit()
    cnt.update({"a0": 28, "a1": 28, "e0": 14, "e1": 14})
    for sem in sorted(cnt):
        g.wait_ge(T.sem[sem], cnt[sem])


def rank_program(g, core, T, topo):
    if T.rank_of(core) is not None:
        program(g, core, T, topo)
